import numpy as np
import ml_dtypes


def mxq(x, axis, fmt="e4m3"):
    dtype, down = {"e4m3": (ml_dtypes.float8_e4m3fn, 7), "e5m2": (ml_dtypes.float8_e5m2, 14)}[fmt]
    v = np.moveaxis(np.asarray(x, np.float32).astype(ml_dtypes.bfloat16).astype(np.float64), axis, -1)
    blocks = v.reshape(v.shape[:-1] + (-1, 32))
    amax = np.abs(blocks).max(-1, keepdims=True)
    byte = np.maximum(np.where(amax > 0, np.frexp(amax)[1] - 1 + 127, 0) - down, 1)
    scale = np.exp2(byte - 127.0)
    codes = (blocks / scale).astype(np.float32).astype(dtype).astype(np.float64)
    return np.moveaxis((codes * scale).reshape(v.shape), -1, axis)


WIDE = False


def mx_kscale(k):
    if not WIDE:
        return np.ones(k)
    levels = np.array([10, -10, 5, -5, 0])
    if k % 512:
        return np.exp2(np.random.permutation(np.resize(levels, k // 32))).repeat(32)
    a = np.empty((k // 512, 16))
    for p in range(k // 512):
        a[p, :8] = np.random.permutation(np.resize(levels, 8))
        for g in range(8):
            far = levels[np.abs(levels - a[p, g]) >= 10]
            a[p, g + 8] = far[np.random.randint(len(far))]
    return np.exp2(a.ravel()).repeat(32)


def f64(x):
    return np.asarray(x).astype(np.float64)


def striped(idx):
    return np.tile(idx.reshape(-1, 16).T, (8, 1)).astype(np.uint16)


def unstriped(offs):
    return offs[:16].T.reshape(-1).astype(np.int64)


E2M1 = np.array([0.0, 0.5, 1.0, 1.5, 2.0, 3.0, 4.0, 6.0, -0.0, -0.5, -1.0, -1.5, -2.0, -3.0, -4.0, -6.0])


def pack_weight(w, fmt):
    k, n = w.shape
    w = f64(np.asarray(w, np.float32).astype(ml_dtypes.bfloat16)).reshape(k // 32, 32, n)
    amax = np.abs(w).max(1)
    if fmt == "e4m3":
        byte = np.frexp(amax)[1] - 1 + 127 - 7
    else:
        mant, ex = np.frexp(amax / 6.0)
        byte = np.where(mant > 0.5, ex, ex - 1) + 127
    byte = np.clip(np.where(amax > 0, byte, 1), 1, 254)
    scaled = (w * np.exp2(127.0 - byte)[:, None, :]).reshape(k, n).astype(np.float32)
    by_word = np.ascontiguousarray(scaled.reshape(k // 512, 128, 4, n).transpose(0, 1, 3, 2))
    if fmt == "e4m3":
        words = by_word.astype(ml_dtypes.float8_e4m3fn).view(np.uint8)
    else:
        c = by_word.astype(ml_dtypes.float4_e2m1fn).view(np.uint8) & 0xF
        words = (c[..., 0::2] | (c[..., 1::2] << 4)).reshape(k // 512, 128, 2 * n)
    return np.ascontiguousarray(words), np.ascontiguousarray(byte.astype(np.uint8).reshape(k // 512, 16, n))


def unpack_weight(words, scales, fmt):
    g, _, n = scales.shape
    words = np.ascontiguousarray(words).reshape(g, 128, n, -1)
    if fmt == "e4m3":
        vals = words.view(ml_dtypes.float8_e4m3fn).astype(np.float64)
    else:
        nib = np.empty((g, 128, n, 4), np.uint8)
        nib[..., 0::2] = words & 0xF
        nib[..., 1::2] = words >> 4
        vals = E2M1[nib]
    vals = vals * np.repeat(np.exp2(scales.astype(np.float64) - 127.0), 8, axis=1)[..., None]
    return vals.transpose(0, 1, 3, 2).reshape(g * 512, n)


def gelu(v):
    return 0.5 * v * (1.0 + np.tanh(np.sqrt(2.0 / np.pi) * (v + 0.044715 * v**3)))


def bf(x):
    return np.asarray(x, np.float32).astype(ml_dtypes.bfloat16)

def planes(Y):
    n, m = Y.shape
    b = f64(bf(Y)).reshape(n // 32, 32, m)
    amax = np.abs(b).max(1)
    byte = np.clip(np.where(amax > 0, np.frexp(amax)[1] - 1 + 127 - 7, 1), 1, 254)
    codes = (b * np.exp2(127.0 - byte)[:, None, :]).reshape(n, m).astype(np.float32).astype(ml_dtypes.float8_e4m3fn).view(np.uint8)
    words = codes.reshape(n // 512, 128, 4, m).transpose(0, 1, 3, 2)
    return np.ascontiguousarray(words), np.ascontiguousarray(byte.astype(np.uint8).reshape(n // 512, 16, m))


K, T, S, T2, S2, N = 512, 2048, 1024, 4096, 1024, 512

def setup_inputs():
    n = np.random.standard_normal
    s = mx_kscale(K)[:, None]
    u = mx_kscale(S)[:, None]
    r = np.exp(0.8 * n(N))
    tab_words, tab_scales = pack_weight(0.36 * n((K, T)) / np.sqrt(K) / s, "e4m3")
    tab2_words, tab2_scales = pack_weight(n((K, T2)) * s, "e4m3")
    w4_words, w4_scales = pack_weight(0.7 * n((K, N)) / np.sqrt(K) / s * r, "e2m1")
    return {
        "tab_words": tab_words, "tab_scales": tab_scales,
        "tab2_words": tab2_words, "tab2_scales": tab2_scales,
        "offs": striped(np.random.permutation(T)[:S]),
        "offs2": striped(np.random.permutation(T2)[:S2]),
        "phase": np.random.uniform(-0.8, 0.8, S).astype(np.float32),
        "amp": (np.exp(0.3 * n(S)) * u[:, 0]).astype(np.float32),
        "wm": (1.5 * n((S, N)) / np.sqrt(S) / u * r).astype(np.float32),
        "w4_words": w4_words, "w4_scales": w4_scales,
        "bias": (0.4 * n(N) * r).astype(np.float32),
    }

def reference(tab_words, tab_scales, tab2_words, tab2_scales, offs, offs2, phase, amp, wm, w4_words, w4_scales, bias):
    v = unpack_weight(tab_words, tab_scales, "e4m3")[:, unstriped(offs)]
    v2 = unpack_weight(tab2_words, tab2_scales, "e4m3")[:, unstriped(offs2)]
    w4 = unpack_weight(w4_words, w4_scales, "e2m1")
    a = v.T @ v2
    h = f64(amp)[:, None] * np.sin(a + f64(phase)[:, None])
    mix = mxq(f64(wm), 0, "e4m3").T @ mxq(h, 0, "e4m3") + w4.T @ v2
    y = mix + f64(bias)[:, None]
    words, scales = planes(y)
    return y, words, scales

@@ -1,0 +1,239 @@
+from contextlib import ExitStack
+
+import concourse.mybir as mybir
+
+K, T, S, T2, S2, N = 512, 2048, 1024, 4096, 1024, 512
+FLOPS = 2 * (K * S * S2 + S * N * S2 + K * N * S2)
+
+F32 = mybir.dt.float32
+BF16 = mybir.dt.bfloat16
+I32 = mybir.dt.int32
+U32 = mybir.dt.uint32
+U16 = mybir.dt.uint16
+U8 = mybir.dt.uint8
+FP8X4 = mybir.dt.float8_e4m3fn_x4
+FP4X4 = mybir.dt.float4_e2m1fn_x4
+ACT = mybir.ActivationFunctionType
+ALU = mybir.AluOpType
+
+P = 128
+BANK = 512
+CHUNKS0 = (256, 256, 512)
+CHUNKS1 = (512, 256, 256)
+
+
+def ranges(widths):
+    out = []
+    j0 = 0
+    for w in widths:
+        out.append((j0, w))
+        j0 = j0 + w
+    return out
+
+
+def tile_list_band_sine_field_kernel(
+    tc, tab_words, tab_scales, tab2_words, tab2_scales, offs, offs2, phase, amp, wm, w4_words, w4_scales, bias,
+    out_0, out_1, out_2,
+):
+    nc = tc.nc
+    with ExitStack() as ctx:
+        lists = ctx.enter_context(tc.tile_pool(name="lists", bufs=1))
+        keep = ctx.enter_context(tc.tile_pool(name="keep", bufs=1))
+        ring = ctx.enter_context(tc.tile_pool(name="ring", bufs=3))
+        psum = ctx.enter_context(tc.psum_pool(name="psum", bufs=4))
+
+        idx2 = lists.tile([P, S2 // 16], U16, name="idx2")
+        idx = lists.tile([P, S // 16], U16, name="idx")
+        nc.sync.dma_start(idx2[:], offs2)
+        nc.sync.dma_start(idx[:], offs)
+
+        v_win = keep.tile([P, T], I32, name="v_win", align_bytes=64)
+        v2_win = keep.tile([P, T2], I32, name="v2_win", align_bytes=64)
+        nc.sync.dma_start(v_win[:], tab_words[0].rearrange("p t i -> p (t i)").bitcast(I32))
+        nc.sync.dma_start(v2_win[:], tab2_words[0].rearrange("p t i -> p (t i)").bitcast(I32))
+
+        s2_win = keep.tile([P, T2], U8, name="s2_win", align_bytes=64)
+        s_win = keep.tile([P, T], U8, name="s_win", align_bytes=64)
+        s4_raw = keep.tile([P, N], U8, name="s4_raw", align_bytes=64)
+        planes = keep.tile([P, S2 + S + N], U8, name="planes", align_bytes=64)
+        warm = keep.tile([P, 8], F32, name="warm")
+        warm2 = keep.tile([P, 8], F32, name="warm2")
+        nc.vector.memset(s2_win[:].bitcast(I32), 0)
+        nc.vector.memset(s_win[:].bitcast(I32), 0)
+        nc.vector.memset(warm[:], 0.0)
+        nc.vector.memset(planes[:].bitcast(I32), 0)
+        nc.scalar.dma_start(s2_win[0:P:8, :].bitcast(I32), tab2_scales[0].bitcast(I32))
+        nc.scalar.dma_start(s_win[0:P:8, :].bitcast(I32), tab_scales[0].bitcast(I32))
+        nc.scalar.activation(out=warm2[:, 0:1], in_=warm[:, 0:1], func=ACT.Sin)
+
+        w4_raw = keep.tile([P, N // 2], I32, name="w4_raw", align_bytes=64)
+        ph = keep.tile([P, 2, 4], F32, name="ph")
+        am = keep.tile([P, 2, 4], F32, name="am")
+        bi = keep.tile([P, 4], F32, name="bi")
+        nc.gpsimd.memset(s4_raw[:].bitcast(I32), 0)
+        nc.gpsimd.dma_start(s4_raw[0:P:8, :].bitcast(I32), w4_scales[0].bitcast(I32))
+        nc.gpsimd.dma_start(ph[:], phase.rearrange("(b p t) -> p b t", b=2, t=4))
+        nc.gpsimd.dma_start(am[:], amp.rearrange("(b p t) -> p b t", b=2, t=4))
+        nc.gpsimd.dma_start(w4_raw[:], w4_words[0].bitcast(I32))
+        nc.gpsimd.dma_start(bi[:], bias.rearrange("(p t) -> p t", t=4))
+
+        wm_raw0 = keep.tile([P, 4, N], F32, name="wm_raw0", align_bytes=64)
+        nc.sync.dma_start(wm_raw0[:], wm[0:512, :].rearrange("(p j) n -> p j n", j=4))
+
+        g2 = keep.tile([P, S2], U8, name="g2", align_bytes=64)
+        g1 = keep.tile([P, S], U8, name="g1", align_bytes=64)
+        stage = keep.tile([P, S2 + S + N], U8, name="stage", tag="late", align_bytes=64)
+        nc.vector.tensor_copy(g2[:], s2_win[:].indirect(idx2[:]))
+        nc.vector.tensor_copy(g1[:], s_win[:].indirect(idx[:]))
+        nc.vector.tensor_copy(stage[:, 0:S2].bitcast(I32), g2[:].bitcast(I32))
+        nc.vector.tensor_copy(
+            stage[:, S2 + S :].rearrange("p (t m) -> p t m", t=4), s4_raw[:].rearrange("p (m t) -> p t m", t=4)
+        )
+        nc.vector.tensor_copy(
+            stage[:, S2 : S2 + S].rearrange("p (b t q) -> p b t q", b=2, t=4),
+            g1[:].rearrange("p (b q t) -> p b t q", b=2, t=4),
+        )
+        for q in range(4):
+            nc.scalar.dma_start(
+                planes[32 * q : 32 * q + 4, :].bitcast(I32), stage[32 * q : 32 * q + 32 : 8, :].bitcast(I32)
+            )
+        v2_sc = planes[:, 0:S2]
+        v_sc = planes[:, S2 : S2 + S]
+        w4_sc = planes[:, S2 + S :]
+
+        wm_raw1 = keep.tile([P, 4, N], F32, name="wm_raw1", tag="late", align_bytes=64)
+        nc.sync.dma_start(wm_raw1[:], wm[512:1024, :].rearrange("(p j) n -> p j n", j=4))
+
+        w4_q = keep.tile([P, 2 * N], U8, name="w4_q", align_bytes=64)
+
+        v2_q = keep.tile([P, S2], U32, name="v2_q", align_bytes=64)
+
+        def gather_v(b):
+            v_q = keep.tile([P, 512], U32, name="v_q", tag="v_q", align_bytes=64)
+            nc.vector.tensor_copy(
+                v_q[:].rearrange("p (t q) -> p q t", t=4),
+                v_win[:].bitcast(U32).indirect(idx[:, 32 * b : 32 * b + 32]),
+            )
+            return v_q
+
+        def gather_v2(h):
+            nc.vector.tensor_copy(
+                v2_q[:, 512 * h : 512 * h + 512], v2_win[:].bitcast(U32).indirect(idx2[:, 32 * h : 32 * h + 32])
+            )
+
+        h_q = [keep.tile([P, S2], U32, name="h_q%d" % b, align_bytes=64) for b in range(2)]
+        h_sc = [keep.tile([P, S2], U8, name="h_sc%d" % b, align_bytes=64) for b in range(2)]
+        wm_q = [keep.tile([P, N], U32, name="wm_q%d" % b, align_bytes=64) for b in range(2)]
+        wm_sc = [keep.tile([P, N], U8, name="wm_sc%d" % b, align_bytes=64) for b in range(2)]
+        y_q = keep.tile([P, S2], U32, name="y_q", align_bytes=64)
+        y_sc = keep.tile([P, S2], U8, name="y_sc", align_bytes=64)
+
+        def slots(tag, w):
+            per = BANK // w
+            banks = [psum.tile([P, BANK], F32, name=tag, tag=tag) for u in range(4 // per)]
+            return [banks[t // per][:, (t % per) * w : (t % per + 1) * w] for t in range(4)]
+
+        def sines(b, v_q, j0, w):
+            acc = slots("a", w)
+            for t in range(4):
+                nc.tensor.matmul_mx(
+                    out=acc[t],
+                    lhsT=v_q[:, P * t : P * (t + 1)].bitcast(FP8X4),
+                    lhsT_scale=v_sc[:, 512 * b + P * t : 512 * b + P * (t + 1)],
+                    rhs=v2_q[:, j0 : j0 + w].bitcast(FP8X4),
+                    rhs_scale=v2_sc[:, j0 : j0 + w],
+                    start=True,
+                    stop=True,
+                )
+            sn = ring.tile([P, 4, w], F32, name="sn", tag="sn", align_bytes=64)
+            for t in range(4):
+                nc.scalar.activation(out=sn[:, t, :], in_=acc[t], func=ACT.Sin, bias=ph[:, b, t : t + 1])
+            return sn
+
+        def amplify(b, sn, w):
+            hb = ring.tile([P, 4 * w], BF16, name="hb", tag="hb", align_bytes=64)
+            nc.vector.tensor_tensor(
+                hb[:].rearrange("p (c i t) -> p c t i", i=2, t=4),
+                sn[:].rearrange("p t (c i) -> p c t i", i=2),
+                am[:, b, :].rearrange("p (c t i) -> p c t i", c=1, i=1).to_broadcast([P, w // 2, 4, 2]),
+                ALU.mult,
+            )
+            return hb
+
+        def quantise_h(b, hb, j0, w):
+            nc.vector.quantize_mx(
+                out=h_q[b][:, j0 : j0 + w].bitcast(FP8X4), scales=h_sc[b][:, j0 : j0 + w], in_=hb[:]
+            )
+
+        def round_wm(b, raw):
+            wb = keep.tile([P, 4 * N], BF16, name="wb%d" % b, align_bytes=64)
+            dst = wb[:].rearrange("p (t m j) -> p m j t", t=4, j=4)
+            src = raw[:].rearrange("p j (m t) -> p m j t", t=4)
+            for u in range(2):
+                nc.scalar.copy(dst[:, 64 * u : 64 * u + 64], src[:, 64 * u : 64 * u + 64])
+            nc.vector.quantize_mx(out=wm_q[b][:].bitcast(FP8X4), scales=wm_sc[b][:], in_=wb[:])
+
+        def mix(j0, w):
+            acc = slots("y", w)
+            per = BANK // w
+            w4n = w if w == BANK else P
+            for t in range(4):
+                for c in range(0, w, w4n):
+                    nc.tensor.matmul_mx(
+                        out=acc[t][:, c : c + w4n],
+                        lhsT=w4_q[:, 2 * P * t : 2 * P * (t + 1)].bitcast(FP4X4),
+                        lhsT_scale=w4_sc[:, P * t : P * (t + 1)],
+                        rhs=v2_q[:, j0 + c : j0 + c + w4n].bitcast(FP8X4),
+                        rhs_scale=v2_sc[:, j0 + c : j0 + c + w4n],
+                        start=(t % per == 0 and c == 0),
+                        stop=False,
+                    )
+            for b in range(2):
+                for t in range(4):
+                    nc.tensor.matmul_mx(
+                        out=acc[t],
+                        lhsT=wm_q[b][:, P * t : P * (t + 1)].bitcast(FP8X4),
+                        lhsT_scale=wm_sc[b][:, P * t : P * (t + 1)],
+                        rhs=h_q[b][:, j0 : j0 + w].bitcast(FP8X4),
+                        rhs_scale=h_sc[b][:, j0 : j0 + w],
+                        start=False,
+                        stop=(b == 1 and t % per == per - 1),
+                    )
+            y = ring.tile([P, 4, w], F32, name="y", tag="y", align_bytes=64)
+            for t in range(4):
+                nc.scalar.activation(out=y[:, t, :], in_=acc[t], func=ACT.Identity, bias=bi[:, t : t + 1])
+            nc.sync.dma_start(out_0.rearrange("(p t) j -> p t j", t=4)[:, :, j0 : j0 + w], y[:])
+            return y
+
+        def planes_of(y, j0, w):
+            yb = ring.tile([P, 4 * w], BF16, name="yb", tag="yb", align_bytes=64)
+            nc.vector.tensor_copy(
+                yb[:].rearrange("p (c i t) -> p c t i", i=2, t=4), y[:].rearrange("p t (c i) -> p c t i", i=2)
+            )
+            nc.vector.quantize_mx(out=y_q[:, j0 : j0 + w].bitcast(FP8X4), scales=y_sc[:, j0 : j0 + w], in_=yb[:])
+            nc.sync.dma_start(
+                out_1[0].rearrange("p m t -> p (m t)").bitcast(I32)[:, j0 : j0 + w], y_q[:, j0 : j0 + w].bitcast(I32)
+            )
+
+        v_q = gather_v(0)
+        gather_v2(0)
+        gather_v2(1)
+        nc.vector.tensor_copy(
+            w4_q[:].bitcast(U16).rearrange("p (t m) -> p t m", t=4),
+            w4_raw[:].bitcast(U16).rearrange("p (m t) -> p t m", t=4),
+        )
+        for j0, w in ranges(CHUNKS0):
+            quantise_h(0, amplify(0, sines(0, v_q, j0, w), w), j0, w)
+        v_q = gather_v(1)
+        round_wm(0, wm_raw0)
+        first = True
+        for j0, w in ranges(CHUNKS1):
+            sn = sines(1, v_q, j0, w)
+            if first:
+                round_wm(1, wm_raw1)
+                first = False
+            quantise_h(1, amplify(1, sn, w), j0, w)
+            planes_of(mix(j0, w), j0, w)
+        for q in range(4):
+            eng = nc.scalar if q % 2 else nc.sync
+            eng.dma_start(out_2[0, 4 * q : 4 * q + 4, :].bitcast(I32), y_sc[32 * q : 32 * q + 4, :].bitcast(I32))

@@ -18,8 +18,9 @@ ALU = mybir.AluOpType
 
 P = 128
 BANK = 512
-CHUNKS0 = (256, 256, 512)
-CHUNKS1 = (512, 256, 256)
+CHUNKS = (512, 256, 256)
+PIECE = 256
+SCALAR_PIECES = 0
 
 
 def ranges(widths):
@@ -39,77 +40,70 @@ def tile_list_band_sine_field_kernel(
     with ExitStack() as ctx:
         lists = ctx.enter_context(tc.tile_pool(name="lists", bufs=1))
         keep = ctx.enter_context(tc.tile_pool(name="keep", bufs=1))
-        ring = ctx.enter_context(tc.tile_pool(name="ring", bufs=3))
+        ring = ctx.enter_context(tc.tile_pool(name="ring", bufs=4))
         psum = ctx.enter_context(tc.psum_pool(name="psum", bufs=4))
 
-        idx2 = lists.tile([P, S2 // 16], U16, name="idx2")
         idx = lists.tile([P, S // 16], U16, name="idx")
-        nc.sync.dma_start(idx2[:], offs2)
+        idx2 = lists.tile([P, S2 // 16], U16, name="idx2")
         nc.sync.dma_start(idx[:], offs)
-
-        v_win = keep.tile([P, T], I32, name="v_win", align_bytes=64)
-        v2_win = keep.tile([P, T2], I32, name="v2_win", align_bytes=64)
-        nc.sync.dma_start(v_win[:], tab_words[0].rearrange("p t i -> p (t i)").bitcast(I32))
-        nc.sync.dma_start(v2_win[:], tab2_words[0].rearrange("p t i -> p (t i)").bitcast(I32))
-
+        nc.sync.dma_start(idx2[:], offs2)
         s2_win = keep.tile([P, T2], U8, name="s2_win", align_bytes=64)
         s_win = keep.tile([P, T], U8, name="s_win", align_bytes=64)
-        s4_raw = keep.tile([P, N], U8, name="s4_raw", align_bytes=64)
-        planes = keep.tile([P, S2 + S + N], U8, name="planes", align_bytes=64)
+        s4_raw = keep.tile([P, N], U8, name="s4_raw", tag="s4", align_bytes=64)
         warm = keep.tile([P, 8], F32, name="warm")
         warm2 = keep.tile([P, 8], F32, name="warm2")
-        nc.vector.memset(s2_win[:].bitcast(I32), 0)
-        nc.vector.memset(s_win[:].bitcast(I32), 0)
         nc.vector.memset(warm[:], 0.0)
-        nc.vector.memset(planes[:].bitcast(I32), 0)
-        nc.scalar.dma_start(s2_win[0:P:8, :].bitcast(I32), tab2_scales[0].bitcast(I32))
-        nc.scalar.dma_start(s_win[0:P:8, :].bitcast(I32), tab_scales[0].bitcast(I32))
+        for win, rows in ((s_win, tab_scales), (s2_win, tab2_scales)):
+            nc.vector.memset(win[32:64, :].bitcast(I32), 0)
+            nc.vector.memset(win[64:P, :].bitcast(I32), 0)
+            nc.sync.dma_start(win[0:16, :].bitcast(I32), rows[0].bitcast(I32))
+            nc.sync.dma_start(win[16:32, :].bitcast(I32), rows[0].bitcast(I32))
         nc.scalar.activation(out=warm2[:, 0:1], in_=warm[:, 0:1], func=ACT.Sin)
 
-        w4_raw = keep.tile([P, N // 2], I32, name="w4_raw", align_bytes=64)
+        v_win = keep.tile([P, T], I32, name="v_win", tag="win", align_bytes=64)
+        v2_win = keep.tile([P, T2], I32, name="v2_win", tag="win2", align_bytes=64)
+        nc.sync.dma_start(v2_win[:], tab2_words[0].rearrange("p t i -> p (t i)").bitcast(I32))
+        wm_raw0 = keep.tile([P, 4, N], F32, name="wm_raw0", align_bytes=64)
+        nc.sync.dma_start(wm_raw0[:], wm[0:512, :].rearrange("(p j) n -> p j n", j=4))
         ph = keep.tile([P, 2, 4], F32, name="ph")
         am = keep.tile([P, 2, 4], F32, name="am")
         bi = keep.tile([P, 4], F32, name="bi")
+        nc.sync.dma_start(ph[:], phase.rearrange("(b p t) -> p b t", b=2, t=4))
+        nc.sync.dma_start(am[:], amp.rearrange("(b p t) -> p b t", b=2, t=4))
+        nc.sync.dma_start(bi[:], bias.rearrange("(p t) -> p t", t=4))
+        nc.sync.dma_start(v_win[:], tab_words[0].rearrange("p t i -> p (t i)").bitcast(I32))
+
+        w4_raw = keep.tile([P, N // 2], I32, name="w4_raw", tag="w4", align_bytes=64)
         nc.gpsimd.memset(s4_raw[:].bitcast(I32), 0)
-        nc.gpsimd.dma_start(s4_raw[0:P:8, :].bitcast(I32), w4_scales[0].bitcast(I32))
-        nc.gpsimd.dma_start(ph[:], phase.rearrange("(b p t) -> p b t", b=2, t=4))
-        nc.gpsimd.dma_start(am[:], amp.rearrange("(b p t) -> p b t", b=2, t=4))
         nc.gpsimd.dma_start(w4_raw[:], w4_words[0].bitcast(I32))
-        nc.gpsimd.dma_start(bi[:], bias.rearrange("(p t) -> p t", t=4))
+        for q in range(4):
+            nc.gpsimd.dma_start(
+                s4_raw[32 * q : 32 * q + 4, :].bitcast(I32), w4_scales[0, 4 * q : 4 * q + 4, :].bitcast(I32)
+            )
 
-        wm_raw0 = keep.tile([P, 4, N], F32, name="wm_raw0", align_bytes=64)
-        nc.sync.dma_start(wm_raw0[:], wm[0:512, :].rearrange("(p j) n -> p j n", j=4))
-
-        g2 = keep.tile([P, S2], U8, name="g2", align_bytes=64)
+        g2 = keep.tile([P, S2], U8, name="g2", tag="g2", align_bytes=64)
         g1 = keep.tile([P, S], U8, name="g1", align_bytes=64)
-        stage = keep.tile([P, S2 + S + N], U8, name="stage", tag="late", align_bytes=64)
-        nc.vector.tensor_copy(g2[:], s2_win[:].indirect(idx2[:]))
+        planes = keep.tile([P, S2 + S], U8, name="planes", align_bytes=64)
         nc.vector.tensor_copy(g1[:], s_win[:].indirect(idx[:]))
-        nc.vector.tensor_copy(stage[:, 0:S2].bitcast(I32), g2[:].bitcast(I32))
+        nc.vector.tensor_copy(g2[:], s2_win[:].indirect(idx2[:]))
         nc.vector.tensor_copy(
-            stage[:, S2 + S :].rearrange("p (t m) -> p t m", t=4), s4_raw[:].rearrange("p (m t) -> p t m", t=4)
-        )
-        nc.vector.tensor_copy(
-            stage[:, S2 : S2 + S].rearrange("p (b t q) -> p b t q", b=2, t=4),
+            planes[:, S2 : S2 + S].rearrange("p (b t q) -> p b t q", b=2, t=4),
             g1[:].rearrange("p (b q t) -> p b t q", b=2, t=4),
         )
-        for q in range(4):
-            nc.scalar.dma_start(
-                planes[32 * q : 32 * q + 4, :].bitcast(I32), stage[32 * q : 32 * q + 32 : 8, :].bitcast(I32)
-            )
+        nc.vector.tensor_copy(planes[:, 0:S2].bitcast(I32), g2[:].bitcast(I32))
+        for q in range(1, 4):
+            src = 4 * q + 16 * (q // 2)
+            nc.sync.dma_start(planes[32 * q : 32 * q + 4, :].bitcast(I32), planes[src : src + 4, :].bitcast(I32))
+        wm_raw1 = keep.tile([P, 4, N], F32, name="wm_raw1", tag="g2", align_bytes=64)
+        nc.sync.dma_start(wm_raw1[:], wm[512:1024, :].rearrange("(p j) n -> p j n", j=4))
         v2_sc = planes[:, 0:S2]
         v_sc = planes[:, S2 : S2 + S]
-        w4_sc = planes[:, S2 + S :]
 
-        wm_raw1 = keep.tile([P, 4, N], F32, name="wm_raw1", tag="late", align_bytes=64)
-        nc.sync.dma_start(wm_raw1[:], wm[512:1024, :].rearrange("(p j) n -> p j n", j=4))
-
-        w4_q = keep.tile([P, 2 * N], U8, name="w4_q", align_bytes=64)
 
         v2_q = keep.tile([P, S2], U32, name="v2_q", align_bytes=64)
 
-        def gather_v(b):
-            v_q = keep.tile([P, 512], U32, name="v_q", tag="v_q", align_bytes=64)
+        def gather_v(b, tag):
+            v_q = keep.tile([P, 512], U32, name="v_q%d" % b, tag=tag, align_bytes=64)
             nc.vector.tensor_copy(
                 v_q[:].rearrange("p (t q) -> p q t", t=4),
                 v_win[:].bitcast(U32).indirect(idx[:, 32 * b : 32 * b + 32]),
@@ -123,7 +117,7 @@ def tile_list_band_sine_field_kernel(
 
         h_q = [keep.tile([P, S2], U32, name="h_q%d" % b, align_bytes=64) for b in range(2)]
         h_sc = [keep.tile([P, S2], U8, name="h_sc%d" % b, align_bytes=64) for b in range(2)]
-        wm_q = [keep.tile([P, N], U32, name="wm_q%d" % b, align_bytes=64) for b in range(2)]
+        wm_q = []
         wm_sc = [keep.tile([P, N], U8, name="wm_sc%d" % b, align_bytes=64) for b in range(2)]
         y_q = keep.tile([P, S2], U32, name="y_q", align_bytes=64)
         y_sc = keep.tile([P, S2], U8, name="y_sc", align_bytes=64)
@@ -165,13 +159,17 @@ def tile_list_band_sine_field_kernel(
                 out=h_q[b][:, j0 : j0 + w].bitcast(FP8X4), scales=h_sc[b][:, j0 : j0 + w], in_=hb[:]
             )
 
-        def round_wm(b, raw):
-            wb = keep.tile([P, 4 * N], BF16, name="wb%d" % b, align_bytes=64)
-            dst = wb[:].rearrange("p (t m j) -> p m j t", t=4, j=4)
+        wb = [keep.tile([P, 4 * N], BF16, name="wb%d" % b, align_bytes=64) for b in range(2)]
+
+        def round_wm(b, raw, u, parts):
+            dst = wb[b][:].rearrange("p (t m j) -> p m j t", t=4, j=4)
             src = raw[:].rearrange("p j (m t) -> p m j t", t=4)
-            for u in range(2):
-                nc.scalar.copy(dst[:, 64 * u : 64 * u + 64], src[:, 64 * u : 64 * u + 64])
-            nc.vector.quantize_mx(out=wm_q[b][:].bitcast(FP8X4), scales=wm_sc[b][:], in_=wb[:])
+            m = P // parts
+            nc.scalar.copy(dst[:, m * u : m * u + m], src[:, m * u : m * u + m])
+
+        def quantise_wm(b, tag):
+            wm_q.append(keep.tile([P, N], U32, name="wm_q%d" % b, tag=tag, align_bytes=64))
+            nc.vector.quantize_mx(out=wm_q[b][:].bitcast(FP8X4), scales=wm_sc[b][:], in_=wb[b][:])
 
         def mix(j0, w):
             acc = slots("y", w)
@@ -206,34 +204,47 @@ def tile_list_band_sine_field_kernel(
             return y
 
         def planes_of(y, j0, w):
-            yb = ring.tile([P, 4 * w], BF16, name="yb", tag="yb", align_bytes=64)
-            nc.vector.tensor_copy(
-                yb[:].rearrange("p (c i t) -> p c t i", i=2, t=4), y[:].rearrange("p t (c i) -> p c t i", i=2)
-            )
-            nc.vector.quantize_mx(out=y_q[:, j0 : j0 + w].bitcast(FP8X4), scales=y_sc[:, j0 : j0 + w], in_=yb[:])
+            for c in range(0, w, PIECE):
+                j = j0 + c
+                copy = nc.scalar.copy if j < SCALAR_PIECES * PIECE else nc.vector.tensor_copy
+                yb = ring.tile([P, 4 * PIECE], BF16, name="yb", tag="yb", align_bytes=64)
+                copy(
+                    yb[:].rearrange("p (c i t) -> p c t i", i=2, t=4),
+                    y[:, :, c : c + PIECE].rearrange("p t (c i) -> p c t i", i=2),
+                )
+                nc.vector.quantize_mx(
+                    out=y_q[:, j : j + PIECE].bitcast(FP8X4), scales=y_sc[:, j : j + PIECE], in_=yb[:]
+                )
             nc.sync.dma_start(
                 out_1[0].rearrange("p m t -> p (m t)").bitcast(I32)[:, j0 : j0 + w], y_q[:, j0 : j0 + w].bitcast(I32)
             )
 
-        v_q = gather_v(0)
+        def features(j0, w):
+            sn = [sines(b, v_q[b], j0, w) for b in range(2)]
+            hb = [amplify(b, sn[b], w) for b in range(2)]
+            for b in range(2):
+                quantise_h(b, hb[b], j0, w)
+
+        round_wm(0, wm_raw0, 0, 1)
         gather_v2(0)
         gather_v2(1)
+        v_q = [gather_v(b, "v_q%d" % b) for b in range(2)]
+        chunks = ranges(CHUNKS)
+        features(*chunks[0])
+        w4_q = keep.tile([P, 2 * N], U8, name="w4_q", tag="win", align_bytes=64)
         nc.vector.tensor_copy(
             w4_q[:].bitcast(U16).rearrange("p (t m) -> p t m", t=4),
             w4_raw[:].bitcast(U16).rearrange("p (m t) -> p t m", t=4),
         )
-        for j0, w in ranges(CHUNKS0):
-            quantise_h(0, amplify(0, sines(0, v_q, j0, w), w), j0, w)
-        v_q = gather_v(1)
-        round_wm(0, wm_raw0)
-        first = True
-        for j0, w in ranges(CHUNKS1):
-            sn = sines(1, v_q, j0, w)
-            if first:
-                round_wm(1, wm_raw1)
-                first = False
-            quantise_h(1, amplify(1, sn, w), j0, w)
-            planes_of(mix(j0, w), j0, w)
+        w4_sc = keep.tile([P, N], U8, name="w4_sc", tag="w4", align_bytes=64)
+        nc.vector.tensor_copy(w4_sc[:].rearrange("p (t m) -> p t m", t=4), s4_raw[:].rearrange("p (m t) -> p t m", t=4))
+        quantise_wm(0, "s4")
+        round_wm(1, wm_raw1, 0, 1)
+        quantise_wm(1, "wm_q1")
+        features(*chunks[1])
+        features(*chunks[2])
+        for chunk in chunks:
+            planes_of(mix(*chunk), *chunk)
         for q in range(4):
             eng = nc.scalar if q % 2 else nc.sync
             eng.dma_start(out_2[0, 4 * q : 4 * q + 4, :].bitcast(I32), y_sc[32 * q : 32 * q + 4, :].bitcast(I32))

@@ -17,19 +17,12 @@ ACT = mybir.ActivationFunctionType
 ALU = mybir.AluOpType
 
 P = 128
+PACK = 4
+PASS = P * PACK
 BANK = 512
-CHUNKS = (512, 256, 256)
-PIECE = 256
-SCALAR_PIECES = 0
-
-
-def ranges(widths):
-    out = []
-    j0 = 0
-    for w in widths:
-        out.append((j0, w))
-        j0 = j0 + w
-    return out
+QUAD = 32
+ROWS = 16
+CHUNKS = ((0, 512), (512, 256), (768, 256))
 
 
 def tile_list_band_sine_field_kernel(
@@ -45,149 +38,147 @@ def tile_list_band_sine_field_kernel(
 
         idx = lists.tile([P, S // 16], U16, name="idx")
         idx2 = lists.tile([P, S2 // 16], U16, name="idx2")
-        nc.sync.dma_start(idx[:], offs)
-        nc.sync.dma_start(idx2[:], offs2)
         s2_win = keep.tile([P, T2], U8, name="s2_win", align_bytes=64)
         s_win = keep.tile([P, T], U8, name="s_win", align_bytes=64)
-        s4_raw = keep.tile([P, N], U8, name="s4_raw", tag="s4", align_bytes=64)
-        warm = keep.tile([P, 8], F32, name="warm")
-        warm2 = keep.tile([P, 8], F32, name="warm2")
-        nc.vector.memset(warm[:], 0.0)
-        for win, rows in ((s_win, tab_scales), (s2_win, tab2_scales)):
-            nc.vector.memset(win[32:64, :].bitcast(I32), 0)
-            nc.vector.memset(win[64:P, :].bitcast(I32), 0)
-            nc.sync.dma_start(win[0:16, :].bitcast(I32), rows[0].bitcast(I32))
-            nc.sync.dma_start(win[16:32, :].bitcast(I32), rows[0].bitcast(I32))
-        nc.scalar.activation(out=warm2[:, 0:1], in_=warm[:, 0:1], func=ACT.Sin)
+        for win, rows, offsets, given in ((s_win, tab_scales, idx, offs), (s2_win, tab2_scales, idx2, offs2)):
+            nc.sync.dma_start(offsets[:], given)
+            nc.vector.memset(win[QUAD : 2 * QUAD, :].bitcast(I32), 0)
+            nc.vector.memset(win[2 * QUAD : P, :].bitcast(I32), 0)
+            nc.sync.dma_start(win[0:ROWS, :].bitcast(I32), rows[0].bitcast(I32))
+            nc.sync.dma_start(win[ROWS : 2 * ROWS, :].bitcast(I32), rows[0].bitcast(I32))
 
-        v_win = keep.tile([P, T], I32, name="v_win", tag="win", align_bytes=64)
-        v2_win = keep.tile([P, T2], I32, name="v2_win", tag="win2", align_bytes=64)
-        nc.sync.dma_start(v2_win[:], tab2_words[0].rearrange("p t i -> p (t i)").bitcast(I32))
-        wm_raw0 = keep.tile([P, 4, N], F32, name="wm_raw0", align_bytes=64)
-        nc.sync.dma_start(wm_raw0[:], wm[0:512, :].rearrange("(p j) n -> p j n", j=4))
-        ph = keep.tile([P, 2, 4], F32, name="ph")
-        am = keep.tile([P, 2, 4], F32, name="am")
-        bi = keep.tile([P, 4], F32, name="bi")
-        nc.sync.dma_start(ph[:], phase.rearrange("(b p t) -> p b t", b=2, t=4))
-        nc.sync.dma_start(am[:], amp.rearrange("(b p t) -> p b t", b=2, t=4))
-        nc.sync.dma_start(bi[:], bias.rearrange("(p t) -> p t", t=4))
-        nc.sync.dma_start(v_win[:], tab_words[0].rearrange("p t i -> p (t i)").bitcast(I32))
+        v_win = keep.tile([P, T], I32, name="v_win", tag="v_win", align_bytes=64)
+        v2_win = keep.tile([P, T2], I32, name="v2_win", align_bytes=64)
+        wm_raw0 = keep.tile([P, PACK, N], F32, name="wm_raw0", align_bytes=64)
+        wm_rows = wm.rearrange("(b p u) n -> b p u n", b=2, u=PACK)
+        ph = keep.tile([P, 2, PACK], F32, name="ph")
+        am = keep.tile([P, 2, PACK], F32, name="am")
+        bi = keep.tile([P, PACK], F32, name="bi")
+        w4_raw = keep.tile([P, N // 2], I32, name="w4_raw", tag="w4_raw", align_bytes=64)
+        nc.sync.dma_start(v2_win[:], tab2_words[0].rearrange("p c t -> p (c t)").bitcast(I32))
+        nc.sync.dma_start(wm_raw0[:], wm_rows[0])
+        nc.sync.dma_start(ph[:], phase.rearrange("(b p t) -> p b t", b=2, t=PACK))
+        nc.sync.dma_start(am[:], amp.rearrange("(b p t) -> p b t", b=2, t=PACK))
+        nc.sync.dma_start(bi[:], bias.rearrange("(p t) -> p t", t=PACK))
+        nc.sync.dma_start(v_win[:], tab_words[0].rearrange("p c t -> p (c t)").bitcast(I32))
+        nc.sync.dma_start(w4_raw[:], w4_words[0].bitcast(I32))
 
-        w4_raw = keep.tile([P, N // 2], I32, name="w4_raw", tag="w4", align_bytes=64)
-        nc.gpsimd.memset(s4_raw[:].bitcast(I32), 0)
-        nc.gpsimd.dma_start(w4_raw[:], w4_words[0].bitcast(I32))
-        for q in range(4):
-            nc.gpsimd.dma_start(
-                s4_raw[32 * q : 32 * q + 4, :].bitcast(I32), w4_scales[0, 4 * q : 4 * q + 4, :].bitcast(I32)
-            )
-
-        g2 = keep.tile([P, S2], U8, name="g2", tag="g2", align_bytes=64)
-        g1 = keep.tile([P, S], U8, name="g1", align_bytes=64)
+        s2_picked = keep.tile([P, S2], U8, name="s2_picked", tag="s2_picked", align_bytes=64)
+        s_picked = keep.tile([P, S], U8, name="s_picked", tag="s_picked", align_bytes=64)
         planes = keep.tile([P, S2 + S], U8, name="planes", align_bytes=64)
-        nc.vector.tensor_copy(g1[:], s_win[:].indirect(idx[:]))
-        nc.vector.tensor_copy(g2[:], s2_win[:].indirect(idx2[:]))
-        nc.vector.tensor_copy(
-            planes[:, S2 : S2 + S].rearrange("p (b t q) -> p b t q", b=2, t=4),
-            g1[:].rearrange("p (b q t) -> p b t q", b=2, t=4),
-        )
-        nc.vector.tensor_copy(planes[:, 0:S2].bitcast(I32), g2[:].bitcast(I32))
-        for q in range(1, 4):
-            src = 4 * q + 16 * (q // 2)
-            nc.sync.dma_start(planes[32 * q : 32 * q + 4, :].bitcast(I32), planes[src : src + 4, :].bitcast(I32))
-        wm_raw1 = keep.tile([P, 4, N], F32, name="wm_raw1", tag="g2", align_bytes=64)
-        nc.sync.dma_start(wm_raw1[:], wm[512:1024, :].rearrange("(p j) n -> p j n", j=4))
         v2_sc = planes[:, 0:S2]
         v_sc = planes[:, S2 : S2 + S]
+        nc.vector.tensor_copy(s_picked[:], s_win[:].indirect(idx[:]))
+        nc.vector.tensor_copy(s2_picked[:], s2_win[:].indirect(idx2[:]))
+        nc.vector.tensor_copy(
+            v_sc.rearrange("p (b t m) -> p b t m", b=2, t=PACK),
+            s_picked[:].rearrange("p (b m t) -> p b t m", b=2, t=PACK),
+        )
+        nc.vector.tensor_copy(v2_sc.bitcast(I32), s2_picked[:].bitcast(I32))
+        for quad in range(1, 4):
+            first = 4 * quad + ROWS * (quad // 2)
+            nc.sync.dma_start(
+                planes[QUAD * quad : QUAD * quad + 4, :].bitcast(I32), planes[first : first + 4, :].bitcast(I32)
+            )
 
+        wm_raw1 = keep.tile([P, PACK, N], F32, name="wm_raw1", tag="s2_picked", align_bytes=64)
+        s4_raw = keep.tile([P, N], U8, name="s4_raw", tag="s_picked", align_bytes=64)
+        nc.vector.memset(s4_raw[:].bitcast(I32), 0)
+        nc.sync.dma_start(wm_raw1[:], wm_rows[1])
+        for quad in range(4):
+            nc.sync.dma_start(
+                s4_raw[QUAD * quad : QUAD * quad + 4, :].bitcast(I32),
+                w4_scales[0, 4 * quad : 4 * quad + 4, :].bitcast(I32),
+            )
 
         v2_q = keep.tile([P, S2], U32, name="v2_q", align_bytes=64)
-
-        def gather_v(b, tag):
-            v_q = keep.tile([P, 512], U32, name="v_q%d" % b, tag=tag, align_bytes=64)
-            nc.vector.tensor_copy(
-                v_q[:].rearrange("p (t q) -> p q t", t=4),
-                v_win[:].bitcast(U32).indirect(idx[:, 32 * b : 32 * b + 32]),
-            )
-            return v_q
-
-        def gather_v2(h):
-            nc.vector.tensor_copy(
-                v2_q[:, 512 * h : 512 * h + 512], v2_win[:].bitcast(U32).indirect(idx2[:, 32 * h : 32 * h + 32])
-            )
-
         h_q = [keep.tile([P, S2], U32, name="h_q%d" % b, align_bytes=64) for b in range(2)]
         h_sc = [keep.tile([P, S2], U8, name="h_sc%d" % b, align_bytes=64) for b in range(2)]
-        wm_q = []
         wm_sc = [keep.tile([P, N], U8, name="wm_sc%d" % b, align_bytes=64) for b in range(2)]
         y_q = keep.tile([P, S2], U32, name="y_q", align_bytes=64)
         y_sc = keep.tile([P, S2], U8, name="y_sc", align_bytes=64)
 
-        def slots(tag, w):
-            per = BANK // w
-            banks = [psum.tile([P, BANK], F32, name=tag, tag=tag) for u in range(4 // per)]
-            return [banks[t // per][:, (t % per) * w : (t % per + 1) * w] for t in range(4)]
+        def gather_v(b):
+            dealt = keep.tile([P, PASS], U32, name="v_q%d" % b, align_bytes=64)
+            cols = PASS // 16
+            nc.vector.tensor_copy(
+                dealt[:].rearrange("p (t m) -> p m t", t=PACK),
+                v_win[:].bitcast(U32).indirect(idx[:, cols * b : cols * (b + 1)]),
+            )
+            return dealt
 
-        def sines(b, v_q, j0, w):
-            acc = slots("a", w)
-            for t in range(4):
+        def round_wm(b, raw):
+            rounded = keep.tile([P, PACK * N], BF16, name="wm_bf%d" % b, align_bytes=64)
+            nc.scalar.copy(
+                rounded[:].rearrange("p (t m u) -> p m u t", t=PACK, u=PACK),
+                raw[:].rearrange("p u (m t) -> p m u t", t=PACK),
+            )
+            return rounded
+
+        def quantise_wm(b, rounded, tag):
+            codes = keep.tile([P, N], U32, name="wm_q%d" % b, tag=tag, align_bytes=64)
+            nc.vector.quantize_mx(out=codes[:].bitcast(FP8X4), scales=wm_sc[b][:], in_=rounded[:])
+            return codes
+
+        def psum_slices(tag, w):
+            per = BANK // w
+            banks = [psum.tile([P, BANK], F32, name=tag, tag=tag) for bank in range(PACK // per)]
+            return [banks[t // per][:, (t % per) * w : (t % per + 1) * w] for t in range(PACK)]
+
+        def woven(tile):
+            return tile[:].rearrange("p (c e t) -> p c t e", e=2, t=PACK)
+
+        def by_pairs(tile):
+            return tile[:].rearrange("p t (c e) -> p c t e", e=2)
+
+        def sines(b, j0, w):
+            acc = psum_slices("a", w)
+            for t in range(PACK):
                 nc.tensor.matmul_mx(
                     out=acc[t],
-                    lhsT=v_q[:, P * t : P * (t + 1)].bitcast(FP8X4),
-                    lhsT_scale=v_sc[:, 512 * b + P * t : 512 * b + P * (t + 1)],
+                    lhsT=v_q[b][:, P * t : P * (t + 1)].bitcast(FP8X4),
+                    lhsT_scale=v_sc[:, PASS * b + P * t : PASS * b + P * (t + 1)],
                     rhs=v2_q[:, j0 : j0 + w].bitcast(FP8X4),
                     rhs_scale=v2_sc[:, j0 : j0 + w],
                     start=True,
                     stop=True,
                 )
-            sn = ring.tile([P, 4, w], F32, name="sn", tag="sn", align_bytes=64)
-            for t in range(4):
+            sn = ring.tile([P, PACK, w], F32, name="sn", tag="sn", align_bytes=64)
+            for t in range(PACK):
                 nc.scalar.activation(out=sn[:, t, :], in_=acc[t], func=ACT.Sin, bias=ph[:, b, t : t + 1])
             return sn
 
         def amplify(b, sn, w):
-            hb = ring.tile([P, 4 * w], BF16, name="hb", tag="hb", align_bytes=64)
-            nc.vector.tensor_tensor(
-                hb[:].rearrange("p (c i t) -> p c t i", i=2, t=4),
-                sn[:].rearrange("p t (c i) -> p c t i", i=2),
-                am[:, b, :].rearrange("p (c t i) -> p c t i", c=1, i=1).to_broadcast([P, w // 2, 4, 2]),
-                ALU.mult,
-            )
-            return hb
+            h_bf = ring.tile([P, PACK * w], BF16, name="h_bf", tag="h_bf", align_bytes=64)
+            spread = am[:, b, :].rearrange("p (c t e) -> p c t e", c=1, e=1).to_broadcast([P, w // 2, PACK, 2])
+            nc.vector.tensor_tensor(woven(h_bf), by_pairs(sn), spread, ALU.mult)
+            return h_bf
 
-        def quantise_h(b, hb, j0, w):
-            nc.vector.quantize_mx(
-                out=h_q[b][:, j0 : j0 + w].bitcast(FP8X4), scales=h_sc[b][:, j0 : j0 + w], in_=hb[:]
-            )
-
-        wb = [keep.tile([P, 4 * N], BF16, name="wb%d" % b, align_bytes=64) for b in range(2)]
-
-        def round_wm(b, raw, u, parts):
-            dst = wb[b][:].rearrange("p (t m j) -> p m j t", t=4, j=4)
-            src = raw[:].rearrange("p j (m t) -> p m j t", t=4)
-            m = P // parts
-            nc.scalar.copy(dst[:, m * u : m * u + m], src[:, m * u : m * u + m])
-
-        def quantise_wm(b, tag):
-            wm_q.append(keep.tile([P, N], U32, name="wm_q%d" % b, tag=tag, align_bytes=64))
-            nc.vector.quantize_mx(out=wm_q[b][:].bitcast(FP8X4), scales=wm_sc[b][:], in_=wb[b][:])
+        def features(j0, w):
+            sn = [sines(b, j0, w) for b in range(2)]
+            h_bf = [amplify(b, sn[b], w) for b in range(2)]
+            for b in range(2):
+                nc.vector.quantize_mx(
+                    out=h_q[b][:, j0 : j0 + w].bitcast(FP8X4), scales=h_sc[b][:, j0 : j0 + w], in_=h_bf[b][:]
+                )
 
         def mix(j0, w):
-            acc = slots("y", w)
+            acc = psum_slices("y", w)
             per = BANK // w
-            w4n = w if w == BANK else P
-            for t in range(4):
-                for c in range(0, w, w4n):
+            step = w if w == BANK else P
+            for t in range(PACK):
+                for c in range(0, w, step):
                     nc.tensor.matmul_mx(
-                        out=acc[t][:, c : c + w4n],
+                        out=acc[t][:, c : c + step],
                         lhsT=w4_q[:, 2 * P * t : 2 * P * (t + 1)].bitcast(FP4X4),
                         lhsT_scale=w4_sc[:, P * t : P * (t + 1)],
-                        rhs=v2_q[:, j0 + c : j0 + c + w4n].bitcast(FP8X4),
-                        rhs_scale=v2_sc[:, j0 + c : j0 + c + w4n],
+                        rhs=v2_q[:, j0 + c : j0 + c + step].bitcast(FP8X4),
+                        rhs_scale=v2_sc[:, j0 + c : j0 + c + step],
                         start=(t % per == 0 and c == 0),
                         stop=False,
                     )
             for b in range(2):
-                for t in range(4):
+                for t in range(PACK):
                     nc.tensor.matmul_mx(
                         out=acc[t],
                         lhsT=wm_q[b][:, P * t : P * (t + 1)].bitcast(FP8X4),
@@ -197,54 +188,46 @@ def tile_list_band_sine_field_kernel(
                         start=False,
                         stop=(b == 1 and t % per == per - 1),
                     )
-            y = ring.tile([P, 4, w], F32, name="y", tag="y", align_bytes=64)
-            for t in range(4):
+            y = ring.tile([P, PACK, w], F32, name="y", tag="y", align_bytes=64)
+            out_rows = out_0.rearrange("(p t) j -> p t j", t=PACK)
+            for t in range(PACK):
                 nc.scalar.activation(out=y[:, t, :], in_=acc[t], func=ACT.Identity, bias=bi[:, t : t + 1])
-            nc.sync.dma_start(out_0.rearrange("(p t) j -> p t j", t=4)[:, :, j0 : j0 + w], y[:])
+                if t % 2 == 1:
+                    nc.sync.dma_start(out_rows[:, t - 1 : t + 1, j0 : j0 + w], y[:, t - 1 : t + 1, :])
             return y
 
-        def planes_of(y, j0, w):
-            for c in range(0, w, PIECE):
-                j = j0 + c
-                copy = nc.scalar.copy if j < SCALAR_PIECES * PIECE else nc.vector.tensor_copy
-                yb = ring.tile([P, 4 * PIECE], BF16, name="yb", tag="yb", align_bytes=64)
-                copy(
-                    yb[:].rearrange("p (c i t) -> p c t i", i=2, t=4),
-                    y[:, :, c : c + PIECE].rearrange("p t (c i) -> p c t i", i=2),
-                )
-                nc.vector.quantize_mx(
-                    out=y_q[:, j : j + PIECE].bitcast(FP8X4), scales=y_sc[:, j : j + PIECE], in_=yb[:]
-                )
+        def store_codes(y, j0, w):
+            y_bf = ring.tile([P, PACK * w], BF16, name="y_bf", tag="y_bf", align_bytes=64)
+            nc.vector.tensor_copy(woven(y_bf), by_pairs(y))
+            nc.vector.quantize_mx(out=y_q[:, j0 : j0 + w].bitcast(FP8X4), scales=y_sc[:, j0 : j0 + w], in_=y_bf[:])
             nc.sync.dma_start(
-                out_1[0].rearrange("p m t -> p (m t)").bitcast(I32)[:, j0 : j0 + w], y_q[:, j0 : j0 + w].bitcast(I32)
+                out_1[0].rearrange("p j t -> p (j t)").bitcast(I32)[:, j0 : j0 + w], y_q[:, j0 : j0 + w].bitcast(I32)
             )
 
-        def features(j0, w):
-            sn = [sines(b, v_q[b], j0, w) for b in range(2)]
-            hb = [amplify(b, sn[b], w) for b in range(2)]
-            for b in range(2):
-                quantise_h(b, hb[b], j0, w)
+        wm_bf0 = round_wm(0, wm_raw0)
+        nc.vector.tensor_copy(v2_q[:], v2_win[:].bitcast(U32).indirect(idx2[:]))
+        v_q = [gather_v(b) for b in range(2)]
+        features(*CHUNKS[0])
 
-        round_wm(0, wm_raw0, 0, 1)
-        gather_v2(0)
-        gather_v2(1)
-        v_q = [gather_v(b, "v_q%d" % b) for b in range(2)]
-        chunks = ranges(CHUNKS)
-        features(*chunks[0])
-        w4_q = keep.tile([P, 2 * N], U8, name="w4_q", tag="win", align_bytes=64)
+        w4_q = keep.tile([P, 2 * N], U8, name="w4_q", tag="v_win", align_bytes=64)
         nc.vector.tensor_copy(
-            w4_q[:].bitcast(U16).rearrange("p (t m) -> p t m", t=4),
-            w4_raw[:].bitcast(U16).rearrange("p (m t) -> p t m", t=4),
+            w4_q[:].bitcast(U16).rearrange("p (t m) -> p t m", t=PACK),
+            w4_raw[:].bitcast(U16).rearrange("p (m t) -> p t m", t=PACK),
         )
-        w4_sc = keep.tile([P, N], U8, name="w4_sc", tag="w4", align_bytes=64)
-        nc.vector.tensor_copy(w4_sc[:].rearrange("p (t m) -> p t m", t=4), s4_raw[:].rearrange("p (m t) -> p t m", t=4))
-        quantise_wm(0, "s4")
-        round_wm(1, wm_raw1, 0, 1)
-        quantise_wm(1, "wm_q1")
-        features(*chunks[1])
-        features(*chunks[2])
-        for chunk in chunks:
-            planes_of(mix(*chunk), *chunk)
-        for q in range(4):
-            eng = nc.scalar if q % 2 else nc.sync
-            eng.dma_start(out_2[0, 4 * q : 4 * q + 4, :].bitcast(I32), y_sc[32 * q : 32 * q + 4, :].bitcast(I32))
+        wm_q = [quantise_wm(0, wm_bf0, "w4_raw")]
+        w4_sc = keep.tile([P, N], U8, name="w4_sc", align_bytes=64)
+        nc.vector.tensor_copy(
+            w4_sc[:].rearrange("p (t m) -> p t m", t=PACK), s4_raw[:].rearrange("p (m t) -> p t m", t=PACK)
+        )
+        wm_q.append(quantise_wm(1, round_wm(1, wm_raw1), "wm_q1"))
+
+        for chunk in CHUNKS[1:]:
+            features(*chunk)
+        for chunk in CHUNKS:
+            store_codes(mix(*chunk), *chunk)
+
+        for quad in range(4):
+            queue = nc.scalar if quad % 2 else nc.sync
+            queue.dma_start(
+                out_2[0, 4 * quad : 4 * quad + 4, :].bitcast(I32), y_sc[QUAD * quad : QUAD * quad + 4, :].bitcast(I32)
+            )

@@ -22,7 +22,7 @@ PASS = P * PACK
 BANK = 512
 QUAD = 32
 ROWS = 16
-CHUNKS = ((0, 512), (512, 256), (768, 256))
+LOW = P - ROWS
 
 
 def tile_list_band_sine_field_kernel(
@@ -33,91 +33,98 @@ def tile_list_band_sine_field_kernel(
     with ExitStack() as ctx:
         lists = ctx.enter_context(tc.tile_pool(name="lists", bufs=1))
         keep = ctx.enter_context(tc.tile_pool(name="keep", bufs=1))
-        ring = ctx.enter_context(tc.tile_pool(name="ring", bufs=4))
         psum = ctx.enter_context(tc.psum_pool(name="psum", bufs=4))
 
         idx = lists.tile([P, S // 16], U16, name="idx")
         idx2 = lists.tile([P, S2 // 16], U16, name="idx2")
-        s2_win = keep.tile([P, T2], U8, name="s2_win", align_bytes=64)
         s_win = keep.tile([P, T], U8, name="s_win", align_bytes=64)
-        for win, rows, offsets, given in ((s_win, tab_scales, idx, offs), (s2_win, tab2_scales, idx2, offs2)):
-            nc.sync.dma_start(offsets[:], given)
-            nc.vector.memset(win[QUAD : 2 * QUAD, :].bitcast(I32), 0)
-            nc.vector.memset(win[2 * QUAD : P, :].bitcast(I32), 0)
-            nc.sync.dma_start(win[0:ROWS, :].bitcast(I32), rows[0].bitcast(I32))
-            nc.sync.dma_start(win[ROWS : 2 * ROWS, :].bitcast(I32), rows[0].bitcast(I32))
+        s2_win = keep.tile([P, T2], U8, name="s2_win", align_bytes=64)
+        s4_raw = keep.tile([P, N], U8, name="s4_raw", align_bytes=64)
+        planes = keep.tile([P, S2 + S + N], U8, name="planes", align_bytes=64)
+        nc.vector.memset(s_win[0:LOW, :].bitcast(I32), 0)
+        for win in (s2_win, s4_raw):
+            nc.gpsimd.memset(win[0:LOW, :].bitcast(I32), 0)
+        nc.gpsimd.memset(planes[:].bitcast(I32), 0)
 
         v_win = keep.tile([P, T], I32, name="v_win", tag="v_win", align_bytes=64)
-        v2_win = keep.tile([P, T2], I32, name="v2_win", align_bytes=64)
-        wm_raw0 = keep.tile([P, PACK, N], F32, name="wm_raw0", align_bytes=64)
+        v2_win = keep.tile([P, T2], I32, name="v2_win", tag="v2_win", align_bytes=64)
         wm_rows = wm.rearrange("(b p u) n -> b p u n", b=2, u=PACK)
         ph = keep.tile([P, 2, PACK], F32, name="ph")
         am = keep.tile([P, 2, PACK], F32, name="am")
         bi = keep.tile([P, PACK], F32, name="bi")
         w4_raw = keep.tile([P, N // 2], I32, name="w4_raw", tag="w4_raw", align_bytes=64)
-        nc.sync.dma_start(v2_win[:], tab2_words[0].rearrange("p c t -> p (c t)").bitcast(I32))
-        nc.sync.dma_start(wm_raw0[:], wm_rows[0])
+        nc.sync.dma_start(idx[:], offs)
+        nc.sync.dma_start(s_win[LOW:P, :].bitcast(I32), tab_scales[0].bitcast(I32))
+        nc.sync.dma_start(idx2[:], offs2)
+        nc.sync.dma_start(s2_win[LOW:P, :].bitcast(I32), tab2_scales[0].bitcast(I32))
+        nc.sync.dma_start(s4_raw[LOW:P, :].bitcast(I32), w4_scales[0].bitcast(I32))
+        nc.sync.dma_start(v_win[:], tab_words[0].rearrange("p c t -> p (c t)").bitcast(I32))
         nc.sync.dma_start(ph[:], phase.rearrange("(b p t) -> p b t", b=2, t=PACK))
+        nc.sync.dma_start(v2_win[:], tab2_words[0].rearrange("p c t -> p (c t)").bitcast(I32))
+        nc.sync.dma_start(w4_raw[:], w4_words[0].bitcast(I32))
         nc.sync.dma_start(am[:], amp.rearrange("(b p t) -> p b t", b=2, t=PACK))
         nc.sync.dma_start(bi[:], bias.rearrange("(p t) -> p t", t=PACK))
-        nc.sync.dma_start(v_win[:], tab_words[0].rearrange("p c t -> p (c t)").bitcast(I32))
-        nc.sync.dma_start(w4_raw[:], w4_words[0].bitcast(I32))
 
+        s_picked = keep.tile([P, S], U8, name="s_picked", align_bytes=64)
         s2_picked = keep.tile([P, S2], U8, name="s2_picked", tag="s2_picked", align_bytes=64)
-        s_picked = keep.tile([P, S], U8, name="s_picked", tag="s_picked", align_bytes=64)
-        planes = keep.tile([P, S2 + S], U8, name="planes", align_bytes=64)
-        v2_sc = planes[:, 0:S2]
-        v_sc = planes[:, S2 : S2 + S]
+        staged = keep.tile([P, S2 + S + N], U8, name="staged", tag="staged", align_bytes=64)
         nc.vector.tensor_copy(s_picked[:], s_win[:].indirect(idx[:]))
         nc.vector.tensor_copy(s2_picked[:], s2_win[:].indirect(idx2[:]))
         nc.vector.tensor_copy(
-            v_sc.rearrange("p (b t m) -> p b t m", b=2, t=PACK),
+            staged[:, S2 : S2 + S].rearrange("p (b t m) -> p b t m", b=2, t=PACK),
             s_picked[:].rearrange("p (b m t) -> p b t m", b=2, t=PACK),
         )
-        nc.vector.tensor_copy(v2_sc.bitcast(I32), s2_picked[:].bitcast(I32))
-        for quad in range(1, 4):
-            first = 4 * quad + ROWS * (quad // 2)
-            nc.sync.dma_start(
-                planes[QUAD * quad : QUAD * quad + 4, :].bitcast(I32), planes[first : first + 4, :].bitcast(I32)
-            )
-
-        wm_raw1 = keep.tile([P, PACK, N], F32, name="wm_raw1", tag="s2_picked", align_bytes=64)
-        s4_raw = keep.tile([P, N], U8, name="s4_raw", tag="s_picked", align_bytes=64)
-        nc.vector.memset(s4_raw[:].bitcast(I32), 0)
-        nc.sync.dma_start(wm_raw1[:], wm_rows[1])
+        nc.vector.tensor_copy(
+            staged[:, S2 + S :].rearrange("p (t m) -> p t m", t=PACK), s4_raw[:].rearrange("p (m t) -> p t m", t=PACK)
+        )
+        nc.vector.tensor_copy(staged[:, 0:S2].bitcast(I32), s2_picked[:].bitcast(I32))
         for quad in range(4):
             nc.sync.dma_start(
-                s4_raw[QUAD * quad : QUAD * quad + 4, :].bitcast(I32),
-                w4_scales[0, 4 * quad : 4 * quad + 4, :].bitcast(I32),
+                planes[QUAD * quad : QUAD * quad + 4, :].bitcast(I32),
+                staged[LOW + 4 * quad : LOW + 4 * quad + 4, :].bitcast(I32),
             )
+        v2_sc = planes[:, 0:S2]
+        v_sc = planes[:, S2 : S2 + S]
+        w4_sc = planes[:, S2 + S :]
 
-        v2_q = keep.tile([P, S2], U32, name="v2_q", align_bytes=64)
-        h_q = [keep.tile([P, S2], U32, name="h_q%d" % b, align_bytes=64) for b in range(2)]
-        h_sc = [keep.tile([P, S2], U8, name="h_sc%d" % b, align_bytes=64) for b in range(2)]
+        wm_raw0 = keep.tile([P, PACK, N], F32, name="wm_raw0", tag="s2_picked", align_bytes=64)
+        nc.sync.dma_start(wm_raw0[:], wm_rows[0])
+        wm_raw1 = keep.tile([P, PACK, N], F32, name="wm_raw1", tag="staged", align_bytes=64)
+        nc.sync.dma_start(wm_raw1[:], wm_rows[1])
+
+        v2_q = [keep.tile([P, BANK], U32, name="v2_q%d" % c, align_bytes=64) for c in range(2)]
+        h_q = [[keep.tile([P, BANK], U32, name="h_q%d%d" % (b, c), align_bytes=64) for c in range(2)] for b in range(2)]
+        h_sc = [[keep.tile([P, BANK], U8, name="h_sc%d%d" % (b, c), align_bytes=64) for c in range(2)] for b in range(2)]
         wm_sc = [keep.tile([P, N], U8, name="wm_sc%d" % b, align_bytes=64) for b in range(2)]
+        wm_bf = []
         y_q = keep.tile([P, S2], U32, name="y_q", align_bytes=64)
         y_sc = keep.tile([P, S2], U8, name="y_sc", align_bytes=64)
 
-        def gather_v(b):
-            dealt = keep.tile([P, PASS], U32, name="v_q%d" % b, align_bytes=64)
-            cols = PASS // 16
+        def cols(pair, j0, w):
+            return pair[j0 // BANK][:, j0 % BANK : j0 % BANK + w]
+
+        def gather_v(b, tag):
+            dealt = keep.tile([P, PASS], U32, name="v_q%d" % b, tag=tag, align_bytes=64)
+            span = PASS // 16
             nc.vector.tensor_copy(
                 dealt[:].rearrange("p (t m) -> p m t", t=PACK),
-                v_win[:].bitcast(U32).indirect(idx[:, cols * b : cols * (b + 1)]),
+                v_win[:].bitcast(U32).indirect(idx[:, span * b : span * (b + 1)]),
             )
             return dealt
 
-        def round_wm(b, raw):
-            rounded = keep.tile([P, PACK * N], BF16, name="wm_bf%d" % b, align_bytes=64)
-            nc.scalar.copy(
-                rounded[:].rearrange("p (t m u) -> p m u t", t=PACK, u=PACK),
-                raw[:].rearrange("p u (m t) -> p m u t", t=PACK),
-            )
-            return rounded
+        def gather_v2(c):
+            span = BANK // 16
+            nc.vector.tensor_copy(v2_q[c][:], v2_win[:].bitcast(U32).indirect(idx2[:, span * c : span * (c + 1)]))
 
-        def quantise_wm(b, rounded, tag):
+        def round_wm(b, raw, m0, m1, copy):
+            copy(
+                wm_bf[b][:].rearrange("p (t m u) -> p m u t", t=PACK, u=PACK)[:, m0:m1],
+                raw[:].rearrange("p u (m t) -> p m u t", t=PACK)[:, m0:m1],
+            )
+
+        def quantise_wm(b, tag):
             codes = keep.tile([P, N], U32, name="wm_q%d" % b, tag=tag, align_bytes=64)
-            nc.vector.quantize_mx(out=codes[:].bitcast(FP8X4), scales=wm_sc[b][:], in_=rounded[:])
+            nc.vector.quantize_mx(out=codes[:].bitcast(FP8X4), scales=wm_sc[b][:], in_=wm_bf[b][:])
             return codes
 
         def psum_slices(tag, w):
@@ -126,10 +133,10 @@ def tile_list_band_sine_field_kernel(
             return [banks[t // per][:, (t % per) * w : (t % per + 1) * w] for t in range(PACK)]
 
         def woven(tile):
-            return tile[:].rearrange("p (c e t) -> p c t e", e=2, t=PACK)
+            return tile.rearrange("p (c e t) -> p c t e", e=2, t=PACK)
 
         def by_pairs(tile):
-            return tile[:].rearrange("p t (c e) -> p c t e", e=2)
+            return tile.rearrange("p t (c e) -> p c t e", e=2)
 
         def sines(b, j0, w):
             acc = psum_slices("a", w)
@@ -138,29 +145,24 @@ def tile_list_band_sine_field_kernel(
                     out=acc[t],
                     lhsT=v_q[b][:, P * t : P * (t + 1)].bitcast(FP8X4),
                     lhsT_scale=v_sc[:, PASS * b + P * t : PASS * b + P * (t + 1)],
-                    rhs=v2_q[:, j0 : j0 + w].bitcast(FP8X4),
+                    rhs=cols(v2_q, j0, w).bitcast(FP8X4),
                     rhs_scale=v2_sc[:, j0 : j0 + w],
                     start=True,
                     stop=True,
                 )
-            sn = ring.tile([P, PACK, w], F32, name="sn", tag="sn", align_bytes=64)
+            sn = keep.tile([P, PACK, w], F32, name="sn%d_%d" % (b, j0), align_bytes=64)
             for t in range(PACK):
                 nc.scalar.activation(out=sn[:, t, :], in_=acc[t], func=ACT.Sin, bias=ph[:, b, t : t + 1])
             return sn
 
-        def amplify(b, sn, w):
-            h_bf = ring.tile([P, PACK * w], BF16, name="h_bf", tag="h_bf", align_bytes=64)
+        def amplify(b, j0, w, sn):
+            h_bf = keep.tile([P, PACK * w], BF16, name="h_bf", tag="h_bf%d_%d" % (b, j0), align_bytes=64)
             spread = am[:, b, :].rearrange("p (c t e) -> p c t e", c=1, e=1).to_broadcast([P, w // 2, PACK, 2])
-            nc.vector.tensor_tensor(woven(h_bf), by_pairs(sn), spread, ALU.mult)
+            nc.vector.tensor_tensor(woven(h_bf[:]), by_pairs(sn[:]), spread, ALU.mult)
             return h_bf
 
-        def features(j0, w):
-            sn = [sines(b, j0, w) for b in range(2)]
-            h_bf = [amplify(b, sn[b], w) for b in range(2)]
-            for b in range(2):
-                nc.vector.quantize_mx(
-                    out=h_q[b][:, j0 : j0 + w].bitcast(FP8X4), scales=h_sc[b][:, j0 : j0 + w], in_=h_bf[b][:]
-                )
+        def quantise_h(b, j0, w, h_bf):
+            nc.vector.quantize_mx(out=cols(h_q[b], j0, w).bitcast(FP8X4), scales=cols(h_sc[b], j0, w), in_=h_bf[:])
 
         def mix(j0, w):
             acc = psum_slices("y", w)
@@ -172,7 +174,7 @@ def tile_list_band_sine_field_kernel(
                         out=acc[t][:, c : c + step],
                         lhsT=w4_q[:, 2 * P * t : 2 * P * (t + 1)].bitcast(FP4X4),
                         lhsT_scale=w4_sc[:, P * t : P * (t + 1)],
-                        rhs=v2_q[:, j0 + c : j0 + c + step].bitcast(FP8X4),
+                        rhs=cols(v2_q, j0 + c, step).bitcast(FP8X4),
                         rhs_scale=v2_sc[:, j0 + c : j0 + c + step],
                         start=(t % per == 0 and c == 0),
                         stop=False,
@@ -183,12 +185,12 @@ def tile_list_band_sine_field_kernel(
                         out=acc[t],
                         lhsT=wm_q[b][:, P * t : P * (t + 1)].bitcast(FP8X4),
                         lhsT_scale=wm_sc[b][:, P * t : P * (t + 1)],
-                        rhs=h_q[b][:, j0 : j0 + w].bitcast(FP8X4),
-                        rhs_scale=h_sc[b][:, j0 : j0 + w],
+                        rhs=cols(h_q[b], j0, w).bitcast(FP8X4),
+                        rhs_scale=cols(h_sc[b], j0, w),
                         start=False,
                         stop=(b == 1 and t % per == per - 1),
                     )
-            y = ring.tile([P, PACK, w], F32, name="y", tag="y", align_bytes=64)
+            y = keep.tile([P, PACK, w], F32, name="y%d" % j0, align_bytes=64)
             out_rows = out_0.rearrange("(p t) j -> p t j", t=PACK)
             for t in range(PACK):
                 nc.scalar.activation(out=y[:, t, :], in_=acc[t], func=ACT.Identity, bias=bi[:, t : t + 1])
@@ -196,36 +198,45 @@ def tile_list_band_sine_field_kernel(
                     nc.sync.dma_start(out_rows[:, t - 1 : t + 1, j0 : j0 + w], y[:, t - 1 : t + 1, :])
             return y
 
-        def store_codes(y, j0, w):
-            y_bf = ring.tile([P, PACK * w], BF16, name="y_bf", tag="y_bf", align_bytes=64)
-            nc.vector.tensor_copy(woven(y_bf), by_pairs(y))
+        def round_y(j0, w, y, copy):
+            y_bf = keep.tile([P, PACK * w], BF16, name="y_bf%d" % j0, align_bytes=64)
+            copy(woven(y_bf[:]), by_pairs(y[:]))
+            return y_bf
+
+        def store_codes(j0, w, y_bf):
             nc.vector.quantize_mx(out=y_q[:, j0 : j0 + w].bitcast(FP8X4), scales=y_sc[:, j0 : j0 + w], in_=y_bf[:])
             nc.sync.dma_start(
                 out_1[0].rearrange("p j t -> p (j t)").bitcast(I32)[:, j0 : j0 + w], y_q[:, j0 : j0 + w].bitcast(I32)
             )
 
-        wm_bf0 = round_wm(0, wm_raw0)
-        nc.vector.tensor_copy(v2_q[:], v2_win[:].bitcast(U32).indirect(idx2[:]))
-        v_q = [gather_v(b) for b in range(2)]
-        features(*CHUNKS[0])
+        v_q = [gather_v(0, "v_q0")]
+        gather_v2(0)
+        gather_v2(1)
+        v_q.append(gather_v(1, "v2_win"))
 
-        w4_q = keep.tile([P, 2 * N], U8, name="w4_q", tag="v_win", align_bytes=64)
+        def features(pieces):
+            sn = [sines(*piece) for piece in pieces]
+            h_bf = [amplify(*piece, s) for piece, s in zip(pieces, sn)]
+            for piece, h in zip(pieces, h_bf):
+                quantise_h(*piece, h)
+
+        features(((0, 0, 256), (0, 256, 256), (1, 0, 512)))
+        w4_q = keep.tile([P, 2 * N], U8, name="w4_q", tag="h_bf0_0", align_bytes=64)
         nc.vector.tensor_copy(
             w4_q[:].bitcast(U16).rearrange("p (t m) -> p t m", t=PACK),
             w4_raw[:].bitcast(U16).rearrange("p (m t) -> p t m", t=PACK),
         )
-        wm_q = [quantise_wm(0, wm_bf0, "w4_raw")]
-        w4_sc = keep.tile([P, N], U8, name="w4_sc", align_bytes=64)
-        nc.vector.tensor_copy(
-            w4_sc[:].rearrange("p (t m) -> p t m", t=PACK), s4_raw[:].rearrange("p (m t) -> p t m", t=PACK)
-        )
-        wm_q.append(quantise_wm(1, round_wm(1, wm_raw1), "wm_q1"))
-
-        for chunk in CHUNKS[1:]:
-            features(*chunk)
-        for chunk in CHUNKS:
-            store_codes(mix(*chunk), *chunk)
-
+        wm_bf.append(keep.tile([P, PACK * N], BF16, name="wm_bf0", tag="h_bf0_256", align_bytes=64))
+        wm_bf.append(keep.tile([P, PACK * N], BF16, name="wm_bf1", tag="h_bf1_0", align_bytes=64))
+        round_wm(0, wm_raw0, 0, P, nc.scalar.copy)
+        round_wm(1, wm_raw1, 0, P, nc.vector.tensor_copy)
+        wm_q = [quantise_wm(0, "wm_q0"), quantise_wm(1, "wm_q1")]
+        features(((0, 512, 512),))
+        features(((1, 512, 256), (1, 768, 256)))
+        y0 = mix(0, 512)
+        store_codes(0, 512, round_y(0, 512, y0, nc.vector.tensor_copy))
+        for chunk in ((512, 256), (768, 256)):
+            store_codes(*chunk, round_y(*chunk, mix(*chunk), nc.vector.tensor_copy))
         for quad in range(4):
             queue = nc.scalar if quad % 2 else nc.sync
             queue.dma_start(

@@ -1,6 +1,7 @@
 from contextlib import ExitStack
 
 import concourse.mybir as mybir
+from concourse.masks import make_identity
 
 K, T, S, T2, S2, N = 512, 2048, 1024, 4096, 1024, 512
 FLOPS = 2 * (K * S * S2 + S * N * S2 + K * N * S2)
@@ -23,6 +24,7 @@ BANK = 512
 QUAD = 32
 ROWS = 16
 LOW = P - ROWS
+RUN = 4
 
 
 def tile_list_band_sine_field_kernel(
@@ -41,6 +43,9 @@ def tile_list_band_sine_field_kernel(
         s2_win = keep.tile([P, T2], U8, name="s2_win", align_bytes=64)
         s4_raw = keep.tile([P, N], U8, name="s4_raw", align_bytes=64)
         planes = keep.tile([P, S2 + S + N], U8, name="planes", align_bytes=64)
+        warm = keep.tile([P, 2], F32, name="warm")
+        nc.vector.memset(warm[:, 0:1], 0.0)
+        nc.scalar.activation(out=warm[:, 1:2], in_=warm[:, 0:1], func=ACT.Sin)
         nc.vector.memset(s_win[0:LOW, :].bitcast(I32), 0)
         for win in (s2_win, s4_raw):
             nc.gpsimd.memset(win[0:LOW, :].bitcast(I32), 0)
@@ -48,9 +53,11 @@ def tile_list_band_sine_field_kernel(
 
         v_win = keep.tile([P, T], I32, name="v_win", tag="v_win", align_bytes=64)
         v2_win = keep.tile([P, T2], I32, name="v2_win", tag="v2_win", align_bytes=64)
-        wm_rows = wm.rearrange("(b p u) n -> b p u n", b=2, u=PACK)
-        ph = keep.tile([P, 2, PACK], F32, name="ph")
-        am = keep.tile([P, 2, PACK], F32, name="am")
+        wm_rows = wm.rearrange("(b a u r) n -> b u a r n", b=2, u=PACK, r=RUN)
+        rows = keep.tile([P, PASS], F32, name="rows")
+        nc.gpsimd.memset(rows[0 : P - 4, :], 0.0)
+        ident = keep.tile([P, P], F32, name="ident")
+        make_identity(nc, ident[:])
         bi = keep.tile([P, PACK], F32, name="bi")
         w4_raw = keep.tile([P, N // 2], I32, name="w4_raw", tag="w4_raw", align_bytes=64)
         nc.sync.dma_start(idx[:], offs)
@@ -59,10 +66,10 @@ def tile_list_band_sine_field_kernel(
         nc.sync.dma_start(s2_win[LOW:P, :].bitcast(I32), tab2_scales[0].bitcast(I32))
         nc.sync.dma_start(s4_raw[LOW:P, :].bitcast(I32), w4_scales[0].bitcast(I32))
         nc.sync.dma_start(v_win[:], tab_words[0].rearrange("p c t -> p (c t)").bitcast(I32))
-        nc.sync.dma_start(ph[:], phase.rearrange("(b p t) -> p b t", b=2, t=PACK))
+        nc.sync.dma_start(rows[P - 4 : P - 2, :], phase.rearrange("(b e) -> b e", b=2))
+        nc.sync.dma_start(rows[P - 2 : P, :], amp.rearrange("(b e) -> b e", b=2))
         nc.sync.dma_start(v2_win[:], tab2_words[0].rearrange("p c t -> p (c t)").bitcast(I32))
         nc.sync.dma_start(w4_raw[:], w4_words[0].bitcast(I32))
-        nc.sync.dma_start(am[:], amp.rearrange("(b p t) -> p b t", b=2, t=PACK))
         nc.sync.dma_start(bi[:], bias.rearrange("(p t) -> p t", t=PACK))
 
         s_picked = keep.tile([P, S], U8, name="s_picked", align_bytes=64)
@@ -71,8 +78,8 @@ def tile_list_band_sine_field_kernel(
         nc.vector.tensor_copy(s_picked[:], s_win[:].indirect(idx[:]))
         nc.vector.tensor_copy(s2_picked[:], s2_win[:].indirect(idx2[:]))
         nc.vector.tensor_copy(
-            staged[:, S2 : S2 + S].rearrange("p (b t m) -> p b t m", b=2, t=PACK),
-            s_picked[:].rearrange("p (b m t) -> p b t m", b=2, t=PACK),
+            staged[:, S2 : S2 + S].bitcast(I32).rearrange("p (b t a) -> p b t a", b=2, t=PACK),
+            s_picked[:].bitcast(I32).rearrange("p (b a t) -> p b t a", b=2, t=PACK),
         )
         nc.vector.tensor_copy(
             staged[:, S2 + S :].rearrange("p (t m) -> p t m", t=PACK), s4_raw[:].rearrange("p (m t) -> p t m", t=PACK)
@@ -83,14 +90,28 @@ def tile_list_band_sine_field_kernel(
                 planes[QUAD * quad : QUAD * quad + 4, :].bitcast(I32),
                 staged[LOW + 4 * quad : LOW + 4 * quad + 4, :].bitcast(I32),
             )
+        sorted_rows = keep.tile([P, PASS], F32, name="sorted_rows")
+        nc.scalar.copy(
+            sorted_rows[:].rearrange("p (t a r) -> p t a r", t=PACK, r=RUN),
+            rows[:].rearrange("p (a t r) -> p t a r", t=PACK, r=RUN),
+        )
+        turned = psum.tile([P, BANK], F32, name="turned", tag="a")
+        for t in range(PACK):
+            nc.tensor.transpose(turned[:, P * t : P * (t + 1)], sorted_rows[:, P * t : P * (t + 1)], ident[:])
+        coef = keep.tile([P, 4, PACK], F32, name="coef")
+        nc.scalar.copy(coef[:], turned[:].rearrange("p (t n) -> p n t", t=PACK)[:, P - 4 : P, :])
+        ph = coef[:, 0:2, :]
+        am = coef[:, 2:4, :]
         v2_sc = planes[:, 0:S2]
         v_sc = planes[:, S2 : S2 + S]
         w4_sc = planes[:, S2 + S :]
 
         wm_raw0 = keep.tile([P, PACK, N], F32, name="wm_raw0", tag="s2_picked", align_bytes=64)
-        nc.sync.dma_start(wm_raw0[:], wm_rows[0])
+        for u in range(PACK):
+            nc.sync.dma_start(wm_raw0[:, u, :], wm_rows[0, u])
         wm_raw1 = keep.tile([P, PACK, N], F32, name="wm_raw1", tag="staged", align_bytes=64)
-        nc.sync.dma_start(wm_raw1[:], wm_rows[1])
+        for u in range(PACK):
+            nc.sync.dma_start(wm_raw1[:, u, :], wm_rows[1, u])
 
         v2_q = [keep.tile([P, BANK], U32, name="v2_q%d" % c, align_bytes=64) for c in range(2)]
         h_q = [[keep.tile([P, BANK], U32, name="h_q%d%d" % (b, c), align_bytes=64) for c in range(2)] for b in range(2)]
@@ -107,7 +128,7 @@ def tile_list_band_sine_field_kernel(
             dealt = keep.tile([P, PASS], U32, name="v_q%d" % b, tag=tag, align_bytes=64)
             span = PASS // 16
             nc.vector.tensor_copy(
-                dealt[:].rearrange("p (t m) -> p m t", t=PACK),
+                dealt[:].rearrange("p (t a r) -> p a t r", t=PACK, r=RUN),
                 v_win[:].bitcast(U32).indirect(idx[:, span * b : span * (b + 1)]),
             )
             return dealt
@@ -138,7 +159,7 @@ def tile_list_band_sine_field_kernel(
         def by_pairs(tile):
             return tile.rearrange("p t (c e) -> p c t e", e=2)
 
-        def sines(b, j0, w):
+        def sines(b, j0, w, tag=None):
             acc = psum_slices("a", w)
             for t in range(PACK):
                 nc.tensor.matmul_mx(
@@ -150,7 +171,7 @@ def tile_list_band_sine_field_kernel(
                     start=True,
                     stop=True,
                 )
-            sn = keep.tile([P, PACK, w], F32, name="sn%d_%d" % (b, j0), align_bytes=64)
+            sn = keep.tile([P, PACK, w], F32, name="sn", tag=tag or "sn%d_%d" % (b, j0), align_bytes=64)
             for t in range(PACK):
                 nc.scalar.activation(out=sn[:, t, :], in_=acc[t], func=ACT.Sin, bias=ph[:, b, t : t + 1])
             return sn
@@ -214,29 +235,39 @@ def tile_list_band_sine_field_kernel(
         gather_v2(1)
         v_q.append(gather_v(1, "v2_win"))
 
-        def features(pieces):
-            sn = [sines(*piece) for piece in pieces]
-            h_bf = [amplify(*piece, s) for piece, s in zip(pieces, sn)]
-            for piece, h in zip(pieces, h_bf):
-                quantise_h(*piece, h)
-
-        features(((0, 0, 256), (0, 256, 256), (1, 0, 512)))
+        first = ((0, 0, 256), (0, 256, 256), (1, 0, 512))
+        sn = [sines(*piece) for piece in first]
+        h0 = amplify(*first[0], sn[0])
+        h1 = amplify(*first[1], sn[1])
+        quantise_h(*first[0], h0)
+        quantise_h(*first[1], h1)
         w4_q = keep.tile([P, 2 * N], U8, name="w4_q", tag="h_bf0_0", align_bytes=64)
         nc.vector.tensor_copy(
             w4_q[:].bitcast(U16).rearrange("p (t m) -> p t m", t=PACK),
             w4_raw[:].bitcast(U16).rearrange("p (m t) -> p t m", t=PACK),
         )
+        h2 = amplify(*first[2], sn[2])
         wm_bf.append(keep.tile([P, PACK * N], BF16, name="wm_bf0", tag="h_bf0_256", align_bytes=64))
-        wm_bf.append(keep.tile([P, PACK * N], BF16, name="wm_bf1", tag="h_bf1_0", align_bytes=64))
+        wm_bf.append(keep.tile([P, PACK * N], BF16, name="wm_bf1", tag="sn1_0", align_bytes=64))
         round_wm(0, wm_raw0, 0, P, nc.scalar.copy)
-        round_wm(1, wm_raw1, 0, P, nc.vector.tensor_copy)
-        wm_q = [quantise_wm(0, "wm_q0"), quantise_wm(1, "wm_q1")]
-        features(((0, 512, 512),))
-        features(((1, 512, 256), (1, 768, 256)))
-        y0 = mix(0, 512)
-        store_codes(0, 512, round_y(0, 512, y0, nc.vector.tensor_copy))
-        for chunk in ((512, 256), (768, 256)):
-            store_codes(*chunk, round_y(*chunk, mix(*chunk), nc.vector.tensor_copy))
+        round_wm(1, wm_raw1, 0, P // 2, nc.vector.tensor_copy)
+        quantise_h(*first[2], h2)
+        wm_q = [quantise_wm(0, "wm_q0")]
+        rest = ((0, 512, 512), (1, 512, 256), (1, 768, 256))
+        sn = [sines(*rest[0])]
+        round_wm(1, wm_raw1, P // 2, P, nc.scalar.copy)
+        sn.extend(sines(*piece) for piece in rest[1:])
+        h3 = amplify(*rest[0], sn[0])
+        wm_q.append(quantise_wm(1, "wm_q1"))
+        quantise_h(*rest[0], h3)
+        h4 = amplify(*rest[1], sn[1])
+        h5 = amplify(*rest[2], sn[2])
+        quantise_h(*rest[1], h4)
+        quantise_h(*rest[2], h5)
+        chunks = ((0, 512), (512, 256), (768, 256))
+        y_bf = [round_y(*chunk, mix(*chunk), nc.vector.tensor_copy) for chunk in chunks]
+        for chunk, rounded in zip(chunks, y_bf):
+            store_codes(*chunk, rounded)
         for quad in range(4):
             queue = nc.scalar if quad % 2 else nc.sync
             queue.dma_start(

@@ -42,20 +42,18 @@ def tile_list_band_sine_field_kernel(
         s_win = keep.tile([P, T], U8, name="s_win", align_bytes=64)
         s2_win = keep.tile([P, T2], U8, name="s2_win", align_bytes=64)
         s4_raw = keep.tile([P, N], U8, name="s4_raw", align_bytes=64)
-        planes = keep.tile([P, S2 + S + N], U8, name="planes", align_bytes=64)
         warm = keep.tile([P, 2], F32, name="warm")
         nc.vector.memset(warm[:, 0:1], 0.0)
         nc.scalar.activation(out=warm[:, 1:2], in_=warm[:, 0:1], func=ACT.Sin)
         nc.vector.memset(s_win[0:LOW, :].bitcast(I32), 0)
         for win in (s2_win, s4_raw):
-            nc.gpsimd.memset(win[0:LOW, :].bitcast(I32), 0)
-        nc.gpsimd.memset(planes[:].bitcast(I32), 0)
+            nc.vector.memset(win[0:LOW, :].bitcast(I32), 0)
 
         v_win = keep.tile([P, T], I32, name="v_win", tag="v_win", align_bytes=64)
         v2_win = keep.tile([P, T2], I32, name="v2_win", tag="v2_win", align_bytes=64)
         wm_rows = wm.rearrange("(b a u r) n -> b u a r n", b=2, u=PACK, r=RUN)
         rows = keep.tile([P, PASS], F32, name="rows")
-        nc.gpsimd.memset(rows[0 : P - 4, :], 0.0)
+        nc.vector.memset(rows[0 : P - 4, :], 0.0)
         ident = keep.tile([P, P], F32, name="ident")
         make_identity(nc, ident[:])
         bi = keep.tile([P, PACK], F32, name="bi")
@@ -74,21 +72,21 @@ def tile_list_band_sine_field_kernel(
 
         s_picked = keep.tile([P, S], U8, name="s_picked", align_bytes=64)
         s2_picked = keep.tile([P, S2], U8, name="s2_picked", tag="s2_picked", align_bytes=64)
-        staged = keep.tile([P, S2 + S + N], U8, name="staged", tag="staged", align_bytes=64)
+        planes = keep.tile([P, S2 + S + N], U8, name="planes", align_bytes=64)
         nc.vector.tensor_copy(s_picked[:], s_win[:].indirect(idx[:]))
         nc.vector.tensor_copy(s2_picked[:], s2_win[:].indirect(idx2[:]))
         nc.vector.tensor_copy(
-            staged[:, S2 : S2 + S].bitcast(I32).rearrange("p (b t a) -> p b t a", b=2, t=PACK),
+            planes[:, S2 : S2 + S].bitcast(I32).rearrange("p (b t a) -> p b t a", b=2, t=PACK),
             s_picked[:].bitcast(I32).rearrange("p (b a t) -> p b t a", b=2, t=PACK),
         )
         nc.vector.tensor_copy(
-            staged[:, S2 + S :].rearrange("p (t m) -> p t m", t=PACK), s4_raw[:].rearrange("p (m t) -> p t m", t=PACK)
+            planes[:, S2 + S :].rearrange("p (t m) -> p t m", t=PACK), s4_raw[:].rearrange("p (m t) -> p t m", t=PACK)
         )
-        nc.vector.tensor_copy(staged[:, 0:S2].bitcast(I32), s2_picked[:].bitcast(I32))
+        nc.vector.tensor_copy(planes[:, 0:S2].bitcast(I32), s2_picked[:].bitcast(I32))
         for quad in range(4):
             nc.sync.dma_start(
                 planes[QUAD * quad : QUAD * quad + 4, :].bitcast(I32),
-                staged[LOW + 4 * quad : LOW + 4 * quad + 4, :].bitcast(I32),
+                planes[LOW + 4 * quad : LOW + 4 * quad + 4, :].bitcast(I32),
             )
         sorted_rows = keep.tile([P, PASS], F32, name="sorted_rows")
         nc.scalar.copy(
@@ -98,20 +96,20 @@ def tile_list_band_sine_field_kernel(
         turned = psum.tile([P, BANK], F32, name="turned", tag="a")
         for t in range(PACK):
             nc.tensor.transpose(turned[:, P * t : P * (t + 1)], sorted_rows[:, P * t : P * (t + 1)], ident[:])
-        coef = keep.tile([P, 4, PACK], F32, name="coef")
-        nc.scalar.copy(coef[:], turned[:].rearrange("p (t n) -> p n t", t=PACK)[:, P - 4 : P, :])
-        ph = coef[:, 0:2, :]
-        am = coef[:, 2:4, :]
+        by_row = turned[:].rearrange("p (t n) -> p n t", t=PACK)
+        ph = keep.tile([P, 2, PACK], F32, name="ph")
+        nc.scalar.copy(ph[:], by_row[:, P - 4 : P - 2, :])
+        am = keep.tile([P, 2, PACK, 2], F32, name="am")
+        nc.scalar.copy(am[:], by_row[:, P - 2 : P, :].unsqueeze(3).to_broadcast([P, 2, PACK, 2]))
         v2_sc = planes[:, 0:S2]
         v_sc = planes[:, S2 : S2 + S]
         w4_sc = planes[:, S2 + S :]
 
-        wm_raw0 = keep.tile([P, PACK, N], F32, name="wm_raw0", tag="s2_picked", align_bytes=64)
-        for u in range(PACK):
-            nc.sync.dma_start(wm_raw0[:, u, :], wm_rows[0, u])
-        wm_raw1 = keep.tile([P, PACK, N], F32, name="wm_raw1", tag="staged", align_bytes=64)
-        for u in range(PACK):
-            nc.sync.dma_start(wm_raw1[:, u, :], wm_rows[1, u])
+        wm_raw = keep.tile([P, 2, PACK, N], F32, name="wm_raw", tag="s2_picked", align_bytes=64)
+        for b in range(2):
+            for u in range(PACK):
+                nc.sync.dma_start(wm_raw[:, b, u, :], wm_rows[b, u])
+        wm_raw0, wm_raw1 = wm_raw[:, 0], wm_raw[:, 1]
 
         v2_q = [keep.tile([P, BANK], U32, name="v2_q%d" % c, align_bytes=64) for c in range(2)]
         h_q = [[keep.tile([P, BANK], U32, name="h_q%d%d" % (b, c), align_bytes=64) for c in range(2)] for b in range(2)]
@@ -140,7 +138,7 @@ def tile_list_band_sine_field_kernel(
         def round_wm(b, raw, m0, m1, copy):
             copy(
                 wm_bf[b][:].rearrange("p (t m u) -> p m u t", t=PACK, u=PACK)[:, m0:m1],
-                raw[:].rearrange("p u (m t) -> p m u t", t=PACK)[:, m0:m1],
+                raw.rearrange("p u (m t) -> p m u t", t=PACK)[:, m0:m1],
             )
 
         def quantise_wm(b, tag):
@@ -178,7 +176,7 @@ def tile_list_band_sine_field_kernel(
 
         def amplify(b, j0, w, sn):
             h_bf = keep.tile([P, PACK * w], BF16, name="h_bf", tag="h_bf%d_%d" % (b, j0), align_bytes=64)
-            spread = am[:, b, :].rearrange("p (c t e) -> p c t e", c=1, e=1).to_broadcast([P, w // 2, PACK, 2])
+            spread = am[:, b : b + 1].to_broadcast([P, w // 2, PACK, 2])
             nc.vector.tensor_tensor(woven(h_bf[:]), by_pairs(sn[:]), spread, ALU.mult)
             return h_bf
 

@@ -25,6 +25,9 @@ QUAD = 32
 ROWS = 16
 LOW = P - ROWS
 RUN = 4
+SCALE_ROWS = ROWS * QUAD // P
+WM_SPLIT = P // 2
+COEF = P - 4
 
 
 def tile_list_band_sine_field_kernel(
@@ -42,30 +45,25 @@ def tile_list_band_sine_field_kernel(
         s_win = keep.tile([P, T], U8, name="s_win", align_bytes=64)
         s2_win = keep.tile([P, T2], U8, name="s2_win", align_bytes=64)
         s4_raw = keep.tile([P, N], U8, name="s4_raw", align_bytes=64)
-        warm = keep.tile([P, 2], F32, name="warm")
-        nc.vector.memset(warm[:, 0:1], 0.0)
-        nc.scalar.activation(out=warm[:, 1:2], in_=warm[:, 0:1], func=ACT.Sin)
-        nc.vector.memset(s_win[0:LOW, :].bitcast(I32), 0)
-        for win in (s2_win, s4_raw):
+        for win in (s_win, s2_win, s4_raw):
             nc.vector.memset(win[0:LOW, :].bitcast(I32), 0)
 
-        v_win = keep.tile([P, T], I32, name="v_win", tag="v_win", align_bytes=64)
+        v_win = keep.tile([P, T], I32, name="v_win", align_bytes=64)
         v2_win = keep.tile([P, T2], I32, name="v2_win", tag="v2_win", align_bytes=64)
-        wm_rows = wm.rearrange("(b a u r) n -> b u a r n", b=2, u=PACK, r=RUN)
-        rows = keep.tile([P, PASS], F32, name="rows")
-        nc.vector.memset(rows[0 : P - 4, :], 0.0)
+        coef_rows = keep.tile([P, PASS], F32, name="coef_rows")
+        nc.vector.memset(coef_rows[0:COEF, :], 0.0)
         ident = keep.tile([P, P], F32, name="ident")
         make_identity(nc, ident[:])
         bi = keep.tile([P, PACK], F32, name="bi")
-        w4_raw = keep.tile([P, N // 2], I32, name="w4_raw", tag="w4_raw", align_bytes=64)
+        w4_raw = keep.tile([P, N // 2], I32, name="w4_raw", align_bytes=64)
         nc.sync.dma_start(idx[:], offs)
         nc.sync.dma_start(s_win[LOW:P, :].bitcast(I32), tab_scales[0].bitcast(I32))
         nc.sync.dma_start(idx2[:], offs2)
         nc.sync.dma_start(s2_win[LOW:P, :].bitcast(I32), tab2_scales[0].bitcast(I32))
         nc.sync.dma_start(s4_raw[LOW:P, :].bitcast(I32), w4_scales[0].bitcast(I32))
         nc.sync.dma_start(v_win[:], tab_words[0].rearrange("p c t -> p (c t)").bitcast(I32))
-        nc.sync.dma_start(rows[P - 4 : P - 2, :], phase.rearrange("(b e) -> b e", b=2))
-        nc.sync.dma_start(rows[P - 2 : P, :], amp.rearrange("(b e) -> b e", b=2))
+        nc.sync.dma_start(coef_rows[COEF : COEF + 2, :], phase.rearrange("(b e) -> b e", b=2))
+        nc.sync.dma_start(coef_rows[COEF + 2 : P, :], amp.rearrange("(b e) -> b e", b=2))
         nc.sync.dma_start(v2_win[:], tab2_words[0].rearrange("p c t -> p (c t)").bitcast(I32))
         nc.sync.dma_start(w4_raw[:], w4_words[0].bitcast(I32))
         nc.sync.dma_start(bi[:], bias.rearrange("(p t) -> p t", t=PACK))
@@ -83,33 +81,34 @@ def tile_list_band_sine_field_kernel(
             planes[:, S2 + S :].rearrange("p (t m) -> p t m", t=PACK), s4_raw[:].rearrange("p (m t) -> p t m", t=PACK)
         )
         nc.vector.tensor_copy(planes[:, 0:S2].bitcast(I32), s2_picked[:].bitcast(I32))
-        for quad in range(4):
+        for quad in range(P // QUAD):
             nc.sync.dma_start(
-                planes[QUAD * quad : QUAD * quad + 4, :].bitcast(I32),
-                planes[LOW + 4 * quad : LOW + 4 * quad + 4, :].bitcast(I32),
+                planes[QUAD * quad : QUAD * quad + SCALE_ROWS, :].bitcast(I32),
+                planes[LOW + SCALE_ROWS * quad : LOW + SCALE_ROWS * (quad + 1), :].bitcast(I32),
             )
+        v2_sc = planes[:, 0:S2]
+        v_sc = planes[:, S2 : S2 + S]
+        w4_sc = planes[:, S2 + S :]
+
         sorted_rows = keep.tile([P, PASS], F32, name="sorted_rows")
         nc.scalar.copy(
             sorted_rows[:].rearrange("p (t a r) -> p t a r", t=PACK, r=RUN),
-            rows[:].rearrange("p (a t r) -> p t a r", t=PACK, r=RUN),
+            coef_rows[:].rearrange("p (a t r) -> p t a r", t=PACK, r=RUN),
         )
         turned = psum.tile([P, BANK], F32, name="turned", tag="a")
         for t in range(PACK):
             nc.tensor.transpose(turned[:, P * t : P * (t + 1)], sorted_rows[:, P * t : P * (t + 1)], ident[:])
         by_row = turned[:].rearrange("p (t n) -> p n t", t=PACK)
         ph = keep.tile([P, 2, PACK], F32, name="ph")
-        nc.scalar.copy(ph[:], by_row[:, P - 4 : P - 2, :])
+        nc.vector.tensor_copy(ph[:], by_row[:, COEF : COEF + 2, :])
         am = keep.tile([P, 2, PACK, 2], F32, name="am")
-        nc.scalar.copy(am[:], by_row[:, P - 2 : P, :].unsqueeze(3).to_broadcast([P, 2, PACK, 2]))
-        v2_sc = planes[:, 0:S2]
-        v_sc = planes[:, S2 : S2 + S]
-        w4_sc = planes[:, S2 + S :]
+        nc.scalar.copy(am[:], by_row[:, COEF + 2 : P, :].unsqueeze(3).to_broadcast([P, 2, PACK, 2]))
 
+        wm_rows = wm.rearrange("(b a u r) n -> b u a r n", b=2, u=PACK, r=RUN)
         wm_raw = keep.tile([P, 2, PACK, N], F32, name="wm_raw", tag="s2_picked", align_bytes=64)
         for b in range(2):
             for u in range(PACK):
                 nc.sync.dma_start(wm_raw[:, b, u, :], wm_rows[b, u])
-        wm_raw0, wm_raw1 = wm_raw[:, 0], wm_raw[:, 1]
 
         v2_q = [keep.tile([P, BANK], U32, name="v2_q%d" % c, align_bytes=64) for c in range(2)]
         h_q = [[keep.tile([P, BANK], U32, name="h_q%d%d" % (b, c), align_bytes=64) for c in range(2)] for b in range(2)]
@@ -135,14 +134,14 @@ def tile_list_band_sine_field_kernel(
             span = BANK // 16
             nc.vector.tensor_copy(v2_q[c][:], v2_win[:].bitcast(U32).indirect(idx2[:, span * c : span * (c + 1)]))
 
-        def round_wm(b, raw, m0, m1, copy):
+        def round_wm(b, m0, m1, copy):
             copy(
                 wm_bf[b][:].rearrange("p (t m u) -> p m u t", t=PACK, u=PACK)[:, m0:m1],
-                raw.rearrange("p u (m t) -> p m u t", t=PACK)[:, m0:m1],
+                wm_raw[:, b].rearrange("p u (m t) -> p m u t", t=PACK)[:, m0:m1],
             )
 
-        def quantise_wm(b, tag):
-            codes = keep.tile([P, N], U32, name="wm_q%d" % b, tag=tag, align_bytes=64)
+        def quantise_wm(b):
+            codes = keep.tile([P, N], U32, name="wm_q%d" % b, align_bytes=64)
             nc.vector.quantize_mx(out=codes[:].bitcast(FP8X4), scales=wm_sc[b][:], in_=wm_bf[b][:])
             return codes
 
@@ -157,7 +156,7 @@ def tile_list_band_sine_field_kernel(
         def by_pairs(tile):
             return tile.rearrange("p t (c e) -> p c t e", e=2)
 
-        def sines(b, j0, w, tag=None):
+        def sines(b, j0, w):
             acc = psum_slices("a", w)
             for t in range(PACK):
                 nc.tensor.matmul_mx(
@@ -169,7 +168,7 @@ def tile_list_band_sine_field_kernel(
                     start=True,
                     stop=True,
                 )
-            sn = keep.tile([P, PACK, w], F32, name="sn", tag=tag or "sn%d_%d" % (b, j0), align_bytes=64)
+            sn = keep.tile([P, PACK, w], F32, name="sn", tag="sn%d_%d" % (b, j0), align_bytes=64)
             for t in range(PACK):
                 nc.scalar.activation(out=sn[:, t, :], in_=acc[t], func=ACT.Sin, bias=ph[:, b, t : t + 1])
             return sn
@@ -217,9 +216,9 @@ def tile_list_band_sine_field_kernel(
                     nc.sync.dma_start(out_rows[:, t - 1 : t + 1, j0 : j0 + w], y[:, t - 1 : t + 1, :])
             return y
 
-        def round_y(j0, w, y, copy):
+        def round_y(j0, w, y):
             y_bf = keep.tile([P, PACK * w], BF16, name="y_bf%d" % j0, align_bytes=64)
-            copy(woven(y_bf[:]), by_pairs(y[:]))
+            nc.vector.tensor_copy(woven(y_bf[:]), by_pairs(y[:]))
             return y_bf
 
         def store_codes(j0, w, y_bf):
@@ -247,27 +246,30 @@ def tile_list_band_sine_field_kernel(
         h2 = amplify(*first[2], sn[2])
         wm_bf.append(keep.tile([P, PACK * N], BF16, name="wm_bf0", tag="h_bf0_256", align_bytes=64))
         wm_bf.append(keep.tile([P, PACK * N], BF16, name="wm_bf1", tag="sn1_0", align_bytes=64))
-        round_wm(0, wm_raw0, 0, P, nc.scalar.copy)
-        round_wm(1, wm_raw1, 0, P // 2, nc.vector.tensor_copy)
+        round_wm(0, 0, P, nc.scalar.copy)
+        round_wm(1, 0, WM_SPLIT, nc.vector.tensor_copy)
         quantise_h(*first[2], h2)
-        wm_q = [quantise_wm(0, "wm_q0")]
+        wm_q = [quantise_wm(0)]
+
         rest = ((0, 512, 512), (1, 512, 256), (1, 768, 256))
         sn = [sines(*rest[0])]
-        round_wm(1, wm_raw1, P // 2, P, nc.scalar.copy)
+        round_wm(1, WM_SPLIT, P, nc.scalar.copy)
         sn.extend(sines(*piece) for piece in rest[1:])
         h3 = amplify(*rest[0], sn[0])
-        wm_q.append(quantise_wm(1, "wm_q1"))
+        wm_q.append(quantise_wm(1))
         quantise_h(*rest[0], h3)
         h4 = amplify(*rest[1], sn[1])
         h5 = amplify(*rest[2], sn[2])
         quantise_h(*rest[1], h4)
         quantise_h(*rest[2], h5)
-        chunks = ((0, 512), (512, 256), (768, 256))
-        y_bf = [round_y(*chunk, mix(*chunk), nc.vector.tensor_copy) for chunk in chunks]
+
+        chunks = [piece[1:] for piece in first[2:] + rest[1:]]
+        y_bf = [round_y(*chunk, mix(*chunk)) for chunk in chunks]
         for chunk, rounded in zip(chunks, y_bf):
             store_codes(*chunk, rounded)
-        for quad in range(4):
+        for quad in range(P // QUAD):
             queue = nc.scalar if quad % 2 else nc.sync
             queue.dma_start(
-                out_2[0, 4 * quad : 4 * quad + 4, :].bitcast(I32), y_sc[QUAD * quad : QUAD * quad + 4, :].bitcast(I32)
+                out_2[0, SCALE_ROWS * quad : SCALE_ROWS * (quad + 1), :].bitcast(I32),
+                y_sc[QUAD * quad : QUAD * quad + SCALE_ROWS, :].bitcast(I32),
             )

@@ -26,7 +26,6 @@ ROWS = 16
 LOW = P - ROWS
 RUN = 4
 SCALE_ROWS = ROWS * QUAD // P
-WM_SPLIT = P // 2
 COEF = P - 4
 
 
@@ -156,8 +155,8 @@ def tile_list_band_sine_field_kernel(
         def by_pairs(tile):
             return tile.rearrange("p t (c e) -> p c t e", e=2)
 
-        def sines(b, j0, w):
-            acc = psum_slices("a", w)
+        def sines(b, j0, w, sn, banks="a"):
+            acc = psum_slices(banks, w)
             for t in range(PACK):
                 nc.tensor.matmul_mx(
                     out=acc[t],
@@ -168,19 +167,22 @@ def tile_list_band_sine_field_kernel(
                     start=True,
                     stop=True,
                 )
-            sn = keep.tile([P, PACK, w], F32, name="sn", tag="sn%d_%d" % (b, j0), align_bytes=64)
             for t in range(PACK):
                 nc.scalar.activation(out=sn[:, t, :], in_=acc[t], func=ACT.Sin, bias=ph[:, b, t : t + 1])
             return sn
 
-        def amplify(b, j0, w, sn):
-            h_bf = keep.tile([P, PACK * w], BF16, name="h_bf", tag="h_bf%d_%d" % (b, j0), align_bytes=64)
-            spread = am[:, b : b + 1].to_broadcast([P, w // 2, PACK, 2])
-            nc.vector.tensor_tensor(woven(h_bf[:]), by_pairs(sn[:]), spread, ALU.mult)
-            return h_bf
+        def sine_tile(tag, w):
+            return keep.tile([P, PACK, w], F32, name=tag, tag=tag, align_bytes=64)[:]
+
+        def woven_tile(tag, w):
+            return keep.tile([P, PACK * w], BF16, name=tag, tag=tag, align_bytes=64)[:]
+
+        def amplify(b, sn, h_bf):
+            spread = am[:, b : b + 1].to_broadcast([P, sn.shape[2] // 2, PACK, 2])
+            nc.vector.tensor_tensor(woven(h_bf), by_pairs(sn), spread, ALU.mult)
 
         def quantise_h(b, j0, w, h_bf):
-            nc.vector.quantize_mx(out=cols(h_q[b], j0, w).bitcast(FP8X4), scales=cols(h_sc[b], j0, w), in_=h_bf[:])
+            nc.vector.quantize_mx(out=cols(h_q[b], j0, w).bitcast(FP8X4), scales=cols(h_sc[b], j0, w), in_=h_bf)
 
         def mix(j0, w):
             acc = psum_slices("y", w)
@@ -216,13 +218,11 @@ def tile_list_band_sine_field_kernel(
                     nc.sync.dma_start(out_rows[:, t - 1 : t + 1, j0 : j0 + w], y[:, t - 1 : t + 1, :])
             return y
 
-        def round_y(j0, w, y):
-            y_bf = keep.tile([P, PACK * w], BF16, name="y_bf%d" % j0, align_bytes=64)
-            nc.vector.tensor_copy(woven(y_bf[:]), by_pairs(y[:]))
-            return y_bf
+        def round_y(y, y_bf, c0, c1, copy):
+            copy(woven(y_bf[:, PACK * c0 : PACK * c1]), by_pairs(y[:, :, c0:c1]))
 
         def store_codes(j0, w, y_bf):
-            nc.vector.quantize_mx(out=y_q[:, j0 : j0 + w].bitcast(FP8X4), scales=y_sc[:, j0 : j0 + w], in_=y_bf[:])
+            nc.vector.quantize_mx(out=y_q[:, j0 : j0 + w].bitcast(FP8X4), scales=y_sc[:, j0 : j0 + w], in_=y_bf)
             nc.sync.dma_start(
                 out_1[0].rearrange("p j t -> p (j t)").bitcast(I32)[:, j0 : j0 + w], y_q[:, j0 : j0 + w].bitcast(I32)
             )
@@ -232,41 +232,52 @@ def tile_list_band_sine_field_kernel(
         gather_v2(1)
         v_q.append(gather_v(1, "v2_win"))
 
-        first = ((0, 0, 256), (0, 256, 256), (1, 0, 512))
-        sn = [sines(*piece) for piece in first]
-        h0 = amplify(*first[0], sn[0])
-        h1 = amplify(*first[1], sn[1])
-        quantise_h(*first[0], h0)
-        quantise_h(*first[1], h1)
-        w4_q = keep.tile([P, 2 * N], U8, name="w4_q", tag="h_bf0_0", align_bytes=64)
+        sn_a0a = sines(0, 0, 256, sine_tile("sn_a0a", 256))
+        sn_a0b = sines(0, 256, 256, sine_tile("sn_a0b", 256))
+        sn_a1 = sines(1, 0, 512, sine_tile("sn_a1", 512))
+        h_a0 = woven_tile("h_a0", 512)
+        amplify(0, sn_a0a, h_a0[:, 0:1024])
+        amplify(0, sn_a0b, h_a0[:, 1024:2048])
+        w4_q = keep.tile([P, 2 * N], U8, name="w4_q", tag="sn_a0b", align_bytes=64)
         nc.vector.tensor_copy(
             w4_q[:].bitcast(U16).rearrange("p (t m) -> p t m", t=PACK),
             w4_raw[:].bitcast(U16).rearrange("p (m t) -> p t m", t=PACK),
         )
-        h2 = amplify(*first[2], sn[2])
-        wm_bf.append(keep.tile([P, PACK * N], BF16, name="wm_bf0", tag="h_bf0_256", align_bytes=64))
-        wm_bf.append(keep.tile([P, PACK * N], BF16, name="wm_bf1", tag="sn1_0", align_bytes=64))
+        quantise_h(0, 0, 512, h_a0)
+        wm_bf.append(keep.tile([P, PACK * N], BF16, name="wm_bf0", tag="sn_a0a", align_bytes=64))
         round_wm(0, 0, P, nc.scalar.copy)
-        round_wm(1, 0, WM_SPLIT, nc.vector.tensor_copy)
-        quantise_h(*first[2], h2)
-        wm_q = [quantise_wm(0)]
+        h_a1 = woven_tile("h_a1", 512)
+        amplify(1, sn_a1, h_a1)
+        wm_bf.append(keep.tile([P, PACK * N], BF16, name="wm_bf1", tag="sn_a1", align_bytes=64))
+        round_wm(1, 0, P, nc.vector.tensor_copy)
+        quantise_h(1, 0, 512, h_a1)
+        wm_q = [quantise_wm(0), quantise_wm(1)]
 
-        rest = ((0, 512, 512), (1, 512, 256), (1, 768, 256))
-        sn = [sines(*rest[0])]
-        round_wm(1, WM_SPLIT, P, nc.scalar.copy)
-        sn.extend(sines(*piece) for piece in rest[1:])
-        h3 = amplify(*rest[0], sn[0])
-        wm_q.append(quantise_wm(1))
-        quantise_h(*rest[0], h3)
-        h4 = amplify(*rest[1], sn[1])
-        h5 = amplify(*rest[2], sn[2])
-        quantise_h(*rest[1], h4)
-        quantise_h(*rest[2], h5)
-
-        chunks = [piece[1:] for piece in first[2:] + rest[1:]]
-        y_bf = [round_y(*chunk, mix(*chunk)) for chunk in chunks]
-        for chunk, rounded in zip(chunks, y_bf):
-            store_codes(*chunk, rounded)
+        sn_bc0 = sines(0, 512, 512, wm_raw[:, 0])
+        sn_b1 = sines(1, 512, 256, sine_tile("sn_b1", 256))
+        y_a = mix(0, 512)
+        h_bc0 = woven_tile("h_bc0", 512)
+        amplify(0, sn_bc0, h_bc0)
+        h_b1 = woven_tile("h_b1", 256)
+        amplify(1, sn_b1, h_b1)
+        quantise_h(0, 512, 512, h_bc0)
+        quantise_h(1, 512, 256, h_b1)
+        sn_c1 = sines(1, 768, 256, sine_tile("sn_c1", 256), banks="y")
+        yb_a = woven_tile("yb_a", 512)
+        round_y(y_a, yb_a, 0, 256, nc.scalar.copy)
+        y_b = mix(512, 256)
+        h_c1 = woven_tile("h_c1", 256)
+        amplify(1, sn_c1, h_c1)
+        quantise_h(1, 768, 256, h_c1)
+        y_c = mix(768, 256)
+        round_y(y_a, yb_a, 256, 512, nc.vector.tensor_copy)
+        store_codes(0, 512, yb_a)
+        yb_b = woven_tile("yb_b", 256)
+        round_y(y_b, yb_b, 0, 256, nc.vector.tensor_copy)
+        yb_c = woven_tile("yb_c", 256)
+        round_y(y_c, yb_c, 0, 256, nc.vector.tensor_copy)
+        store_codes(512, 256, yb_b)
+        store_codes(768, 256, yb_c)
         for quad in range(P // QUAD):
             queue = nc.scalar if quad % 2 else nc.sync
             queue.dma_start(

@@ -26,7 +26,7 @@ ROWS = 16
 LOW = P - ROWS
 RUN = 4
 SCALE_ROWS = ROWS * QUAD // P
-COEF = P - 4
+COEF = 4
 
 
 def tile_list_band_sine_field_kernel(
@@ -49,8 +49,7 @@ def tile_list_band_sine_field_kernel(
 
         v_win = keep.tile([P, T], I32, name="v_win", align_bytes=64)
         v2_win = keep.tile([P, T2], I32, name="v2_win", tag="v2_win", align_bytes=64)
-        coef_rows = keep.tile([P, PASS], F32, name="coef_rows")
-        nc.vector.memset(coef_rows[0:COEF, :], 0.0)
+        coef_rows = keep.tile([COEF, PASS], F32, name="coef_rows")
         ident = keep.tile([P, P], F32, name="ident")
         make_identity(nc, ident[:])
         bi = keep.tile([P, PACK], F32, name="bi")
@@ -61,8 +60,8 @@ def tile_list_band_sine_field_kernel(
         nc.sync.dma_start(s2_win[LOW:P, :].bitcast(I32), tab2_scales[0].bitcast(I32))
         nc.sync.dma_start(s4_raw[LOW:P, :].bitcast(I32), w4_scales[0].bitcast(I32))
         nc.sync.dma_start(v_win[:], tab_words[0].rearrange("p c t -> p (c t)").bitcast(I32))
-        nc.sync.dma_start(coef_rows[COEF : COEF + 2, :], phase.rearrange("(b e) -> b e", b=2))
-        nc.sync.dma_start(coef_rows[COEF + 2 : P, :], amp.rearrange("(b e) -> b e", b=2))
+        nc.sync.dma_start(coef_rows[0:2, :], phase.rearrange("(b e) -> b e", b=2))
+        nc.sync.dma_start(coef_rows[2:COEF, :], amp.rearrange("(b e) -> b e", b=2))
         nc.sync.dma_start(v2_win[:], tab2_words[0].rearrange("p c t -> p (c t)").bitcast(I32))
         nc.sync.dma_start(w4_raw[:], w4_words[0].bitcast(I32))
         nc.sync.dma_start(bi[:], bias.rearrange("(p t) -> p t", t=PACK))
@@ -90,8 +89,9 @@ def tile_list_band_sine_field_kernel(
         w4_sc = planes[:, S2 + S :]
 
         sorted_rows = keep.tile([P, PASS], F32, name="sorted_rows")
+        nc.scalar.copy(sorted_rows[:].rearrange("p (t n) -> p t n", t=PACK), ident[:].unsqueeze(1).to_broadcast([P, PACK, P]))
         nc.scalar.copy(
-            sorted_rows[:].rearrange("p (t a r) -> p t a r", t=PACK, r=RUN),
+            sorted_rows[0:COEF, :].rearrange("p (t a r) -> p t a r", t=PACK, r=RUN),
             coef_rows[:].rearrange("p (a t r) -> p t a r", t=PACK, r=RUN),
         )
         turned = psum.tile([P, BANK], F32, name="turned", tag="a")
@@ -99,9 +99,9 @@ def tile_list_band_sine_field_kernel(
             nc.tensor.transpose(turned[:, P * t : P * (t + 1)], sorted_rows[:, P * t : P * (t + 1)], ident[:])
         by_row = turned[:].rearrange("p (t n) -> p n t", t=PACK)
         ph = keep.tile([P, 2, PACK], F32, name="ph")
-        nc.vector.tensor_copy(ph[:], by_row[:, COEF : COEF + 2, :])
+        nc.vector.tensor_copy(ph[:], by_row[:, 0:2, :])
         am = keep.tile([P, 2, PACK, 2], F32, name="am")
-        nc.scalar.copy(am[:], by_row[:, COEF + 2 : P, :].unsqueeze(3).to_broadcast([P, 2, PACK, 2]))
+        nc.scalar.copy(am[:], by_row[:, 2:COEF, :].unsqueeze(3).to_broadcast([P, 2, PACK, 2]))
 
         wm_rows = wm.rearrange("(b a u r) n -> b u a r n", b=2, u=PACK, r=RUN)
         wm_raw = keep.tile([P, 2, PACK, N], F32, name="wm_raw", tag="s2_picked", align_bytes=64)

@@ -47,7 +47,7 @@ def tile_list_band_sine_field_kernel(
         for win in (s_win, s2_win, s4_raw):
             nc.vector.memset(win[0:LOW, :].bitcast(I32), 0)
 
-        v_win = keep.tile([P, T], I32, name="v_win", align_bytes=64)
+        v_win = keep.tile([P, T], I32, name="v_win", tag="v_win", align_bytes=64)
         v2_win = keep.tile([P, T2], I32, name="v2_win", tag="v2_win", align_bytes=64)
         coef_rows = keep.tile([COEF, PASS], F32, name="coef_rows")
         ident = keep.tile([P, P], F32, name="ident")
@@ -59,10 +59,10 @@ def tile_list_band_sine_field_kernel(
         nc.sync.dma_start(idx2[:], offs2)
         nc.sync.dma_start(s2_win[LOW:P, :].bitcast(I32), tab2_scales[0].bitcast(I32))
         nc.sync.dma_start(s4_raw[LOW:P, :].bitcast(I32), w4_scales[0].bitcast(I32))
-        nc.sync.dma_start(v_win[:], tab_words[0].rearrange("p c t -> p (c t)").bitcast(I32))
         nc.sync.dma_start(coef_rows[0:2, :], phase.rearrange("(b e) -> b e", b=2))
         nc.sync.dma_start(coef_rows[2:COEF, :], amp.rearrange("(b e) -> b e", b=2))
         nc.sync.dma_start(v2_win[:], tab2_words[0].rearrange("p c t -> p (c t)").bitcast(I32))
+        nc.sync.dma_start(v_win[:], tab_words[0].rearrange("p c t -> p (c t)").bitcast(I32))
         nc.sync.dma_start(w4_raw[:], w4_words[0].bitcast(I32))
         nc.sync.dma_start(bi[:], bias.rearrange("(p t) -> p t", t=PACK))
 
@@ -109,7 +109,7 @@ def tile_list_band_sine_field_kernel(
             for u in range(PACK):
                 nc.sync.dma_start(wm_raw[:, b, u, :], wm_rows[b, u])
 
-        v2_q = [keep.tile([P, BANK], U32, name="v2_q%d" % c, align_bytes=64) for c in range(2)]
+        v2_q = keep.tile([P, S2], U32, name="v2_q", align_bytes=64)
         h_q = [[keep.tile([P, BANK], U32, name="h_q%d%d" % (b, c), align_bytes=64) for c in range(2)] for b in range(2)]
         h_sc = [[keep.tile([P, BANK], U8, name="h_sc%d%d" % (b, c), align_bytes=64) for c in range(2)] for b in range(2)]
         wm_sc = [keep.tile([P, N], U8, name="wm_sc%d" % b, align_bytes=64) for b in range(2)]
@@ -128,10 +128,6 @@ def tile_list_band_sine_field_kernel(
                 v_win[:].bitcast(U32).indirect(idx[:, span * b : span * (b + 1)]),
             )
             return dealt
-
-        def gather_v2(c):
-            span = BANK // 16
-            nc.vector.tensor_copy(v2_q[c][:], v2_win[:].bitcast(U32).indirect(idx2[:, span * c : span * (c + 1)]))
 
         def round_wm(b, m0, m1, copy):
             copy(
@@ -162,7 +158,7 @@ def tile_list_band_sine_field_kernel(
                     out=acc[t],
                     lhsT=v_q[b][:, P * t : P * (t + 1)].bitcast(FP8X4),
                     lhsT_scale=v_sc[:, PASS * b + P * t : PASS * b + P * (t + 1)],
-                    rhs=cols(v2_q, j0, w).bitcast(FP8X4),
+                    rhs=v2_q[:, j0 : j0 + w].bitcast(FP8X4),
                     rhs_scale=v2_sc[:, j0 : j0 + w],
                     start=True,
                     stop=True,
@@ -194,7 +190,7 @@ def tile_list_band_sine_field_kernel(
                         out=acc[t][:, c : c + step],
                         lhsT=w4_q[:, 2 * P * t : 2 * P * (t + 1)].bitcast(FP4X4),
                         lhsT_scale=w4_sc[:, P * t : P * (t + 1)],
-                        rhs=cols(v2_q, j0 + c, step).bitcast(FP8X4),
+                        rhs=v2_q[:, j0 + c : j0 + c + step].bitcast(FP8X4),
                         rhs_scale=v2_sc[:, j0 + c : j0 + c + step],
                         start=(t % per == 0 and c == 0),
                         stop=False,
@@ -227,31 +223,35 @@ def tile_list_band_sine_field_kernel(
                 out_1[0].rearrange("p j t -> p (j t)").bitcast(I32)[:, j0 : j0 + w], y_q[:, j0 : j0 + w].bitcast(I32)
             )
 
-        v_q = [gather_v(0, "v_q0")]
-        gather_v2(0)
-        gather_v2(1)
-        v_q.append(gather_v(1, "v2_win"))
-
-        sn_a0a = sines(0, 0, 256, sine_tile("sn_a0a", 256))
-        sn_a0b = sines(0, 256, 256, sine_tile("sn_a0b", 256))
-        sn_a1 = sines(1, 0, 512, sine_tile("sn_a1", 512))
-        h_a0 = woven_tile("h_a0", 512)
-        amplify(0, sn_a0a, h_a0[:, 0:1024])
-        amplify(0, sn_a0b, h_a0[:, 1024:2048])
-        w4_q = keep.tile([P, 2 * N], U8, name="w4_q", tag="sn_a0b", align_bytes=64)
+        nc.vector.tensor_copy(v2_q[:], v2_win[:].bitcast(U32).indirect(idx2[:]))
+        v_q = [gather_v(0, "v_q0"), gather_v(1, "v_q1")]
+        w4_q = keep.tile([P, 2 * N], U8, name="w4_q", tag="v_win", align_bytes=64)
         nc.vector.tensor_copy(
             w4_q[:].bitcast(U16).rearrange("p (t m) -> p t m", t=PACK),
             w4_raw[:].bitcast(U16).rearrange("p (m t) -> p t m", t=PACK),
         )
-        quantise_h(0, 0, 512, h_a0)
-        wm_bf.append(keep.tile([P, PACK * N], BF16, name="wm_bf0", tag="sn_a0a", align_bytes=64))
-        round_wm(0, 0, P, nc.scalar.copy)
+
+        sn_a00 = sines(0, 0, 128, sine_tile("sn_a00", 128))
+        sn_a01 = sines(0, 128, 128, sine_tile("sn_a01", 128))
+        sn_a0b = sines(0, 256, 256, sine_tile("sn_a0b", 256))
+        sn_a1 = sines(1, 0, 512, sine_tile("sn_a1", 512), banks="y")
+        h_a0a = woven_tile("h_a0a", 256)
+        h_a0b = woven_tile("h_a0b", 256)
+        amplify(0, sn_a00, h_a0a[:, 0:512])
+        amplify(0, sn_a01, h_a0a[:, 512:1024])
+        quantise_h(0, 0, 256, h_a0a)
+        amplify(0, sn_a0b, h_a0b)
+        wm_bf.append(keep.tile([P, PACK * N], BF16, name="wm_bf0", tag="h_a0a", align_bytes=64))
+        round_wm(0, 0, P // 2, nc.vector.tensor_copy)
+        quantise_h(0, 256, 256, h_a0b)
+        round_wm(0, P // 2, P, nc.scalar.copy)
         h_a1 = woven_tile("h_a1", 512)
         amplify(1, sn_a1, h_a1)
+        wm_q = [quantise_wm(0)]
         wm_bf.append(keep.tile([P, PACK * N], BF16, name="wm_bf1", tag="sn_a1", align_bytes=64))
         round_wm(1, 0, P, nc.vector.tensor_copy)
         quantise_h(1, 0, 512, h_a1)
-        wm_q = [quantise_wm(0), quantise_wm(1)]
+        wm_q.append(quantise_wm(1))
 
         sn_bc0 = sines(0, 512, 512, wm_raw[:, 0])
         sn_b1 = sines(1, 512, 256, sine_tile("sn_b1", 256))
@@ -262,15 +262,15 @@ def tile_list_band_sine_field_kernel(
         amplify(1, sn_b1, h_b1)
         quantise_h(0, 512, 512, h_bc0)
         quantise_h(1, 512, 256, h_b1)
-        sn_c1 = sines(1, 768, 256, sine_tile("sn_c1", 256), banks="y")
+        sn_c1 = sines(1, 768, 256, sine_tile("sn_c1", 256))
         yb_a = woven_tile("yb_a", 512)
-        round_y(y_a, yb_a, 0, 256, nc.scalar.copy)
+        round_y(y_a, yb_a, 0, 384, nc.scalar.copy)
         y_b = mix(512, 256)
         h_c1 = woven_tile("h_c1", 256)
         amplify(1, sn_c1, h_c1)
         quantise_h(1, 768, 256, h_c1)
         y_c = mix(768, 256)
-        round_y(y_a, yb_a, 256, 512, nc.vector.tensor_copy)
+        round_y(y_a, yb_a, 384, 512, nc.vector.tensor_copy)
         store_codes(0, 512, yb_a)
         yb_b = woven_tile("yb_b", 256)
         round_y(y_b, yb_b, 0, 256, nc.vector.tensor_copy)

@@ -59,9 +59,9 @@ def tile_list_band_sine_field_kernel(
         nc.sync.dma_start(idx2[:], offs2)
         nc.sync.dma_start(s2_win[LOW:P, :].bitcast(I32), tab2_scales[0].bitcast(I32))
         nc.sync.dma_start(s4_raw[LOW:P, :].bitcast(I32), w4_scales[0].bitcast(I32))
+        nc.sync.dma_start(v2_win[:], tab2_words[0].rearrange("p c t -> p (c t)").bitcast(I32))
         nc.sync.dma_start(coef_rows[0:2, :], phase.rearrange("(b e) -> b e", b=2))
         nc.sync.dma_start(coef_rows[2:COEF, :], amp.rearrange("(b e) -> b e", b=2))
-        nc.sync.dma_start(v2_win[:], tab2_words[0].rearrange("p c t -> p (c t)").bitcast(I32))
         nc.sync.dma_start(v_win[:], tab_words[0].rearrange("p c t -> p (c t)").bitcast(I32))
         nc.sync.dma_start(w4_raw[:], w4_words[0].bitcast(I32))
         nc.sync.dma_start(bi[:], bias.rearrange("(p t) -> p t", t=PACK))
@@ -89,7 +89,11 @@ def tile_list_band_sine_field_kernel(
         w4_sc = planes[:, S2 + S :]
 
         sorted_rows = keep.tile([P, PASS], F32, name="sorted_rows")
-        nc.scalar.copy(sorted_rows[:].rearrange("p (t n) -> p t n", t=PACK), ident[:].unsqueeze(1).to_broadcast([P, PACK, P]))
+        nc.scalar.activation(
+            out=sorted_rows[:].rearrange("p (t n) -> p t n", t=PACK),
+            in_=ident[:].unsqueeze(1).to_broadcast([P, PACK, P]),
+            func=ACT.Sin,
+        )
         nc.scalar.copy(
             sorted_rows[0:COEF, :].rearrange("p (t a r) -> p t a r", t=PACK, r=RUN),
             coef_rows[:].rearrange("p (a t r) -> p t a r", t=PACK, r=RUN),
@@ -98,10 +102,9 @@ def tile_list_band_sine_field_kernel(
         for t in range(PACK):
             nc.tensor.transpose(turned[:, P * t : P * (t + 1)], sorted_rows[:, P * t : P * (t + 1)], ident[:])
         by_row = turned[:].rearrange("p (t n) -> p n t", t=PACK)
-        ph = keep.tile([P, 2, PACK], F32, name="ph")
-        nc.vector.tensor_copy(ph[:], by_row[:, 0:2, :])
-        am = keep.tile([P, 2, PACK, 2], F32, name="am")
-        nc.scalar.copy(am[:], by_row[:, 2:COEF, :].unsqueeze(3).to_broadcast([P, 2, PACK, 2]))
+        coef = keep.tile([P, COEF, PACK, 2], F32, name="coef")
+        nc.scalar.copy(coef[:], by_row[:, 0:COEF, :].unsqueeze(3).to_broadcast([P, COEF, PACK, 2]))
+        am = coef[:, 2:COEF]
 
         wm_rows = wm.rearrange("(b a u r) n -> b u a r n", b=2, u=PACK, r=RUN)
         wm_raw = keep.tile([P, 2, PACK, N], F32, name="wm_raw", tag="s2_picked", align_bytes=64)
@@ -164,7 +167,7 @@ def tile_list_band_sine_field_kernel(
                     stop=True,
                 )
             for t in range(PACK):
-                nc.scalar.activation(out=sn[:, t, :], in_=acc[t], func=ACT.Sin, bias=ph[:, b, t : t + 1])
+                nc.scalar.activation(out=sn[:, t, :], in_=acc[t], func=ACT.Sin, bias=coef[:, b, t, 0:1])
             return sn
 
         def sine_tile(tag, w):
@@ -249,11 +252,12 @@ def tile_list_band_sine_field_kernel(
         amplify(1, sn_a1, h_a1)
         wm_q = [quantise_wm(0)]
         wm_bf.append(keep.tile([P, PACK * N], BF16, name="wm_bf1", tag="sn_a1", align_bytes=64))
-        round_wm(1, 0, P, nc.vector.tensor_copy)
+        round_wm(1, 0, 96, nc.vector.tensor_copy)
         quantise_h(1, 0, 512, h_a1)
+        sn_bc0 = sines(0, 512, 512, wm_raw[:, 0])
+        round_wm(1, 96, P, nc.scalar.copy)
         wm_q.append(quantise_wm(1))
 
-        sn_bc0 = sines(0, 512, 512, wm_raw[:, 0])
         sn_b1 = sines(1, 512, 256, sine_tile("sn_b1", 256))
         y_a = mix(0, 512)
         h_bc0 = woven_tile("h_bc0", 512)

@@ -59,10 +59,10 @@ def tile_list_band_sine_field_kernel(
         nc.sync.dma_start(idx2[:], offs2)
         nc.sync.dma_start(s2_win[LOW:P, :].bitcast(I32), tab2_scales[0].bitcast(I32))
         nc.sync.dma_start(s4_raw[LOW:P, :].bitcast(I32), w4_scales[0].bitcast(I32))
-        nc.sync.dma_start(v2_win[:], tab2_words[0].rearrange("p c t -> p (c t)").bitcast(I32))
+        nc.sync.dma_start(v_win[:], tab_words[0].rearrange("p c t -> p (c t)").bitcast(I32))
         nc.sync.dma_start(coef_rows[0:2, :], phase.rearrange("(b e) -> b e", b=2))
         nc.sync.dma_start(coef_rows[2:COEF, :], amp.rearrange("(b e) -> b e", b=2))
-        nc.sync.dma_start(v_win[:], tab_words[0].rearrange("p c t -> p (c t)").bitcast(I32))
+        nc.sync.dma_start(v2_win[:], tab2_words[0].rearrange("p c t -> p (c t)").bitcast(I32))
         nc.sync.dma_start(w4_raw[:], w4_words[0].bitcast(I32))
         nc.sync.dma_start(bi[:], bias.rearrange("(p t) -> p t", t=PACK))
 
@@ -112,7 +112,7 @@ def tile_list_band_sine_field_kernel(
             for u in range(PACK):
                 nc.sync.dma_start(wm_raw[:, b, u, :], wm_rows[b, u])
 
-        v2_q = keep.tile([P, S2], U32, name="v2_q", align_bytes=64)
+        v2_q = []
         h_q = [[keep.tile([P, BANK], U32, name="h_q%d%d" % (b, c), align_bytes=64) for c in range(2)] for b in range(2)]
         h_sc = [[keep.tile([P, BANK], U8, name="h_sc%d%d" % (b, c), align_bytes=64) for c in range(2)] for b in range(2)]
         wm_sc = [keep.tile([P, N], U8, name="wm_sc%d" % b, align_bytes=64) for b in range(2)]
@@ -131,6 +131,12 @@ def tile_list_band_sine_field_kernel(
                 v_win[:].bitcast(U32).indirect(idx[:, span * b : span * (b + 1)]),
             )
             return dealt
+
+        def gather_v2(c):
+            picked = keep.tile([P, BANK], U32, name="v2_q%d" % c, align_bytes=64)
+            span = BANK // 16
+            nc.vector.tensor_copy(picked[:], v2_win[:].bitcast(U32).indirect(idx2[:, span * c : span * (c + 1)]))
+            return picked
 
         def round_wm(b, m0, m1, copy):
             copy(
@@ -161,7 +167,7 @@ def tile_list_band_sine_field_kernel(
                     out=acc[t],
                     lhsT=v_q[b][:, P * t : P * (t + 1)].bitcast(FP8X4),
                     lhsT_scale=v_sc[:, PASS * b + P * t : PASS * b + P * (t + 1)],
-                    rhs=v2_q[:, j0 : j0 + w].bitcast(FP8X4),
+                    rhs=cols(v2_q, j0, w).bitcast(FP8X4),
                     rhs_scale=v2_sc[:, j0 : j0 + w],
                     start=True,
                     stop=True,
@@ -193,7 +199,7 @@ def tile_list_band_sine_field_kernel(
                         out=acc[t][:, c : c + step],
                         lhsT=w4_q[:, 2 * P * t : 2 * P * (t + 1)].bitcast(FP4X4),
                         lhsT_scale=w4_sc[:, P * t : P * (t + 1)],
-                        rhs=v2_q[:, j0 + c : j0 + c + step].bitcast(FP8X4),
+                        rhs=cols(v2_q, j0 + c, step).bitcast(FP8X4),
                         rhs_scale=v2_sc[:, j0 + c : j0 + c + step],
                         start=(t % per == 0 and c == 0),
                         stop=False,
@@ -226,24 +232,24 @@ def tile_list_band_sine_field_kernel(
                 out_1[0].rearrange("p j t -> p (j t)").bitcast(I32)[:, j0 : j0 + w], y_q[:, j0 : j0 + w].bitcast(I32)
             )
 
-        nc.vector.tensor_copy(v2_q[:], v2_win[:].bitcast(U32).indirect(idx2[:]))
-        v_q = [gather_v(0, "v_q0"), gather_v(1, "v_q1")]
+        v_q = [gather_v(0, "v_q0")]
+        v2_q.append(gather_v2(0))
+        v2_q.append(gather_v2(1))
+        v_q.append(gather_v(1, "v2_win"))
         w4_q = keep.tile([P, 2 * N], U8, name="w4_q", tag="v_win", align_bytes=64)
         nc.vector.tensor_copy(
             w4_q[:].bitcast(U16).rearrange("p (t m) -> p t m", t=PACK),
             w4_raw[:].bitcast(U16).rearrange("p (m t) -> p t m", t=PACK),
         )
 
-        sn_a00 = sines(0, 0, 128, sine_tile("sn_a00", 128))
-        sn_a01 = sines(0, 128, 128, sine_tile("sn_a01", 128))
+        sn_a0a = sines(0, 0, 256, sine_tile("sn_a0a", 256))
         sn_a0b = sines(0, 256, 256, sine_tile("sn_a0b", 256))
         sn_a1 = sines(1, 0, 512, sine_tile("sn_a1", 512), banks="y")
         h_a0a = woven_tile("h_a0a", 256)
         h_a0b = woven_tile("h_a0b", 256)
-        amplify(0, sn_a00, h_a0a[:, 0:512])
-        amplify(0, sn_a01, h_a0a[:, 512:1024])
-        quantise_h(0, 0, 256, h_a0a)
+        amplify(0, sn_a0a, h_a0a)
         amplify(0, sn_a0b, h_a0b)
+        quantise_h(0, 0, 256, h_a0a)
         wm_bf.append(keep.tile([P, PACK * N], BF16, name="wm_bf0", tag="h_a0a", align_bytes=64))
         round_wm(0, 0, P // 2, nc.vector.tensor_copy)
         quantise_h(0, 256, 256, h_a0b)

@@ -42,7 +42,7 @@ def tile_list_band_sine_field_kernel(
         idx = lists.tile([P, S // 16], U16, name="idx")
         idx2 = lists.tile([P, S2 // 16], U16, name="idx2")
         s_win = keep.tile([P, T], U8, name="s_win", align_bytes=64)
-        s2_win = keep.tile([P, T2], U8, name="s2_win", align_bytes=64)
+        s2_win = keep.tile([P, T2], U8, name="s2_win", tag="s2_win", align_bytes=64)
         s4_raw = keep.tile([P, N], U8, name="s4_raw", align_bytes=64)
         for win in (s_win, s2_win, s4_raw):
             nc.vector.memset(win[0:LOW, :].bitcast(I32), 0)
@@ -66,27 +66,24 @@ def tile_list_band_sine_field_kernel(
         nc.sync.dma_start(w4_raw[:], w4_words[0].bitcast(I32))
         nc.sync.dma_start(bi[:], bias.rearrange("(p t) -> p t", t=PACK))
 
-        s_picked = keep.tile([P, S], U8, name="s_picked", align_bytes=64)
-        s2_picked = keep.tile([P, S2], U8, name="s2_picked", tag="s2_picked", align_bytes=64)
-        planes = keep.tile([P, S2 + S + N], U8, name="planes", align_bytes=64)
-        nc.vector.tensor_copy(s_picked[:], s_win[:].indirect(idx[:]))
-        nc.vector.tensor_copy(s2_picked[:], s2_win[:].indirect(idx2[:]))
+        picked = keep.tile([P, S2 + S], U8, name="picked", align_bytes=64)
+        planes = keep.tile([P, S2 + S], U8, name="planes", align_bytes=64)
+        nc.gpsimd.memset(planes[:].bitcast(I32), 0)
         nc.vector.tensor_copy(
-            planes[:, S2 : S2 + S].bitcast(I32).rearrange("p (b t a) -> p b t a", b=2, t=PACK),
-            s_picked[:].bitcast(I32).rearrange("p (b a t) -> p b t a", b=2, t=PACK),
+            picked[:, S2:].rearrange("p (b t a r) -> p b a t r", b=2, t=PACK, r=RUN), s_win[:].indirect(idx[:])
         )
-        nc.vector.tensor_copy(
-            planes[:, S2 + S :].rearrange("p (t m) -> p t m", t=PACK), s4_raw[:].rearrange("p (m t) -> p t m", t=PACK)
-        )
-        nc.vector.tensor_copy(planes[:, 0:S2].bitcast(I32), s2_picked[:].bitcast(I32))
-        for quad in range(P // QUAD):
-            nc.sync.dma_start(
-                planes[QUAD * quad : QUAD * quad + SCALE_ROWS, :].bitcast(I32),
-                planes[LOW + SCALE_ROWS * quad : LOW + SCALE_ROWS * (quad + 1), :].bitcast(I32),
-            )
+        nc.vector.tensor_copy(picked[:, 0:S2], s2_win[:].indirect(idx2[:]))
+
+        def move_rows(dst, src):
+            for quad in range(P // QUAD):
+                nc.sync.dma_start(
+                    dst[QUAD * quad : QUAD * quad + SCALE_ROWS, :].bitcast(I32),
+                    src[LOW + SCALE_ROWS * quad : LOW + SCALE_ROWS * (quad + 1), :].bitcast(I32),
+                )
+
+        move_rows(planes, picked)
         v2_sc = planes[:, 0:S2]
         v_sc = planes[:, S2 : S2 + S]
-        w4_sc = planes[:, S2 + S :]
 
         sorted_rows = keep.tile([P, PASS], F32, name="sorted_rows")
         nc.scalar.activation(
@@ -107,12 +104,12 @@ def tile_list_band_sine_field_kernel(
         am = coef[:, 2:COEF]
 
         wm_rows = wm.rearrange("(b a u r) n -> b u a r n", b=2, u=PACK, r=RUN)
-        wm_raw = keep.tile([P, 2, PACK, N], F32, name="wm_raw", tag="s2_picked", align_bytes=64)
+        wm_raw = keep.tile([P, 2, PACK, N], F32, name="wm_raw", tag="s2_win", align_bytes=64)
         for b in range(2):
             for u in range(PACK):
                 nc.sync.dma_start(wm_raw[:, b, u, :], wm_rows[b, u])
 
-        v2_q = []
+        v2_q = [keep.tile([P, BANK], U32, name="v2_q%d" % c, align_bytes=64) for c in range(2)]
         h_q = [[keep.tile([P, BANK], U32, name="h_q%d%d" % (b, c), align_bytes=64) for c in range(2)] for b in range(2)]
         h_sc = [[keep.tile([P, BANK], U8, name="h_sc%d%d" % (b, c), align_bytes=64) for c in range(2)] for b in range(2)]
         wm_sc = [keep.tile([P, N], U8, name="wm_sc%d" % b, align_bytes=64) for b in range(2)]
@@ -132,11 +129,10 @@ def tile_list_band_sine_field_kernel(
             )
             return dealt
 
-        def gather_v2(c):
-            picked = keep.tile([P, BANK], U32, name="v2_q%d" % c, align_bytes=64)
-            span = BANK // 16
-            nc.vector.tensor_copy(picked[:], v2_win[:].bitcast(U32).indirect(idx2[:, span * c : span * (c + 1)]))
-            return picked
+        def gather_v2(j0, w):
+            nc.vector.tensor_copy(
+                cols(v2_q, j0, w), v2_win[:].bitcast(U32).indirect(idx2[:, j0 // 16 : (j0 + w) // 16])
+            )
 
         def round_wm(b, m0, m1, copy):
             copy(
@@ -189,8 +185,8 @@ def tile_list_band_sine_field_kernel(
         def quantise_h(b, j0, w, h_bf):
             nc.vector.quantize_mx(out=cols(h_q[b], j0, w).bitcast(FP8X4), scales=cols(h_sc[b], j0, w), in_=h_bf)
 
-        def mix(j0, w):
-            acc = psum_slices("y", w)
+        def mix(j0, w, banks="y"):
+            acc = psum_slices(banks, w)
             per = BANK // w
             step = w if w == BANK else P
             for t in range(PACK):
@@ -232,15 +228,20 @@ def tile_list_band_sine_field_kernel(
                 out_1[0].rearrange("p j t -> p (j t)").bitcast(I32)[:, j0 : j0 + w], y_q[:, j0 : j0 + w].bitcast(I32)
             )
 
-        v_q = [gather_v(0, "v_q0")]
-        v2_q.append(gather_v2(0))
-        v2_q.append(gather_v2(1))
-        v_q.append(gather_v(1, "v2_win"))
-        w4_q = keep.tile([P, 2 * N], U8, name="w4_q", tag="v_win", align_bytes=64)
-        nc.vector.tensor_copy(
+        v_q = [gather_v(0, "v_q0"), gather_v(1, "v_q1")]
+        gather_v2(0, 256)
+        gather_v2(256, 256)
+        gather_v2(512, 512)
+        w4_q = keep.tile([P, 2 * N], U8, name="w4_q", align_bytes=64)
+        nc.scalar.copy(
             w4_q[:].bitcast(U16).rearrange("p (t m) -> p t m", t=PACK),
             w4_raw[:].bitcast(U16).rearrange("p (m t) -> p t m", t=PACK),
         )
+        w4_sc = keep.tile([P, N], U8, name="w4_sc", tag="v2_win", align_bytes=64)
+        nc.vector.tensor_copy(
+            w4_sc[:].rearrange("p (t m) -> p t m", t=PACK), s4_raw[:].rearrange("p (m t) -> p t m", t=PACK)
+        )
+        move_rows(w4_sc, w4_sc)
 
         sn_a0a = sines(0, 0, 256, sine_tile("sn_a0a", 256))
         sn_a0b = sines(0, 256, 256, sine_tile("sn_a0b", 256))
@@ -264,15 +265,15 @@ def tile_list_band_sine_field_kernel(
         round_wm(1, 96, P, nc.scalar.copy)
         wm_q.append(quantise_wm(1))
 
-        sn_b1 = sines(1, 512, 256, sine_tile("sn_b1", 256))
-        y_a = mix(0, 512)
-        h_bc0 = woven_tile("h_bc0", 512)
+        sn_b1 = sines(1, 512, 256, sine_tile("sn_b1", 256), banks="y")
+        y_a = mix(0, 512, banks="a")
+        h_bc0 = woven_tile("sn_a1", 512)
         amplify(0, sn_bc0, h_bc0)
         h_b1 = woven_tile("h_b1", 256)
         amplify(1, sn_b1, h_b1)
         quantise_h(0, 512, 512, h_bc0)
         quantise_h(1, 512, 256, h_b1)
-        sn_c1 = sines(1, 768, 256, sine_tile("sn_c1", 256))
+        sn_c1 = sines(1, 768, 256, sine_tile("sn_c1", 256), banks="y")
         yb_a = woven_tile("yb_a", 512)
         round_y(y_a, yb_a, 0, 384, nc.scalar.copy)
         y_b = mix(512, 256)

@@ -26,6 +26,7 @@ ROWS = 16
 LOW = P - ROWS
 RUN = 4
 SCALE_ROWS = ROWS * QUAD // P
+W = 256
 COEF = 4
 
 
@@ -37,12 +38,13 @@ def tile_list_band_sine_field_kernel(
     with ExitStack() as ctx:
         lists = ctx.enter_context(tc.tile_pool(name="lists", bufs=1))
         keep = ctx.enter_context(tc.tile_pool(name="keep", bufs=1))
+        laid = ctx.enter_context(tc.tile_pool(name="laid", bufs=1))
         psum = ctx.enter_context(tc.psum_pool(name="psum", bufs=4))
 
         idx = lists.tile([P, S // 16], U16, name="idx")
         idx2 = lists.tile([P, S2 // 16], U16, name="idx2")
         s_win = keep.tile([P, T], U8, name="s_win", align_bytes=64)
-        s2_win = keep.tile([P, T2], U8, name="s2_win", tag="s2_win", align_bytes=64)
+        s2_win = keep.tile([P, T2], U8, name="s2_win", align_bytes=64)
         s4_raw = keep.tile([P, N], U8, name="s4_raw", align_bytes=64)
         for win in (s_win, s2_win, s4_raw):
             nc.vector.memset(win[0:LOW, :].bitcast(I32), 0)
@@ -53,7 +55,7 @@ def tile_list_band_sine_field_kernel(
         ident = keep.tile([P, P], F32, name="ident")
         make_identity(nc, ident[:])
         bi = keep.tile([P, PACK], F32, name="bi")
-        w4_raw = keep.tile([P, N // 2], I32, name="w4_raw", align_bytes=64)
+        w4_raw = laid.tile([P, N // 2], I32, name="w4_raw", offset=4 * PASS - N, align_bytes=64)
         nc.sync.dma_start(idx[:], offs)
         nc.sync.dma_start(s_win[LOW:P, :].bitcast(I32), tab_scales[0].bitcast(I32))
         nc.sync.dma_start(idx2[:], offs2)
@@ -66,13 +68,19 @@ def tile_list_band_sine_field_kernel(
         nc.sync.dma_start(w4_raw[:], w4_words[0].bitcast(I32))
         nc.sync.dma_start(bi[:], bias.rearrange("(p t) -> p t", t=PACK))
 
-        picked = keep.tile([P, S2 + S], U8, name="picked", align_bytes=64)
-        planes = keep.tile([P, S2 + S], U8, name="planes", align_bytes=64)
-        nc.gpsimd.memset(planes[:].bitcast(I32), 0)
+        s_picked = keep.tile([P, S], U8, name="s_picked", align_bytes=64)
+        s2_picked = keep.tile([P, S2], U8, name="s2_picked", tag="s2_picked", align_bytes=64)
+        planes = keep.tile([P, S2 + S + N], U8, name="planes", align_bytes=64)
+        nc.vector.tensor_copy(s_picked[:], s_win[:].indirect(idx[:]))
+        nc.vector.tensor_copy(s2_picked[:], s2_win[:].indirect(idx2[:]))
         nc.vector.tensor_copy(
-            picked[:, S2:].rearrange("p (b t a r) -> p b a t r", b=2, t=PACK, r=RUN), s_win[:].indirect(idx[:])
+            planes[:, S2 : S2 + S].bitcast(I32).rearrange("p (b t a) -> p b t a", b=2, t=PACK),
+            s_picked[:].bitcast(I32).rearrange("p (b a t) -> p b t a", b=2, t=PACK),
         )
-        nc.vector.tensor_copy(picked[:, 0:S2], s2_win[:].indirect(idx2[:]))
+        nc.vector.tensor_copy(
+            planes[:, S2 + S :].rearrange("p (t m) -> p t m", t=PACK), s4_raw[:].rearrange("p (m t) -> p t m", t=PACK)
+        )
+        nc.vector.tensor_copy(planes[:, 0:S2].bitcast(I32), s2_picked[:].bitcast(I32))
 
         def move_rows(dst, src):
             for quad in range(P // QUAD):
@@ -81,9 +89,10 @@ def tile_list_band_sine_field_kernel(
                     src[LOW + SCALE_ROWS * quad : LOW + SCALE_ROWS * (quad + 1), :].bitcast(I32),
                 )
 
-        move_rows(planes, picked)
+        move_rows(planes, planes)
         v2_sc = planes[:, 0:S2]
         v_sc = planes[:, S2 : S2 + S]
+        w4_sc = planes[:, S2 + S :]
 
         sorted_rows = keep.tile([P, PASS], F32, name="sorted_rows")
         nc.scalar.activation(
@@ -104,14 +113,18 @@ def tile_list_band_sine_field_kernel(
         am = coef[:, 2:COEF]
 
         wm_rows = wm.rearrange("(b a u r) n -> b u a r n", b=2, u=PACK, r=RUN)
-        wm_raw = keep.tile([P, 2, PACK, N], F32, name="wm_raw", tag="s2_win", align_bytes=64)
+        wm_raw = keep.tile([P, 2, PACK, N], F32, name="wm_raw", tag="s2_picked", align_bytes=64)
         for b in range(2):
             for u in range(PACK):
                 nc.sync.dma_start(wm_raw[:, b, u, :], wm_rows[b, u])
 
-        v2_q = [keep.tile([P, BANK], U32, name="v2_q%d" % c, align_bytes=64) for c in range(2)]
-        h_q = [[keep.tile([P, BANK], U32, name="h_q%d%d" % (b, c), align_bytes=64) for c in range(2)] for b in range(2)]
-        h_sc = [[keep.tile([P, BANK], U8, name="h_sc%d%d" % (b, c), align_bytes=64) for c in range(2)] for b in range(2)]
+        v2_q = [
+            keep.tile([P, BANK], U32, name="v2_q0", align_bytes=64),
+            laid.tile([P, BANK], U32, name="v2_q1", offset=4 * PASS, align_bytes=64),
+        ]
+        h_bf = [keep.tile([P, 2 * PACK * W], BF16, name="h_bf%d" % c, align_bytes=64) for c in range(S2 // W)]
+        h_q = [keep.tile([P, 2 * W], U32, name="h_q%d" % c, align_bytes=64) for c in range(S2 // W)]
+        h_sc = [keep.tile([P, 2 * W], U8, name="h_sc%d" % c, align_bytes=64) for c in range(S2 // W)]
         wm_sc = [keep.tile([P, N], U8, name="wm_sc%d" % b, align_bytes=64) for b in range(2)]
         wm_bf = []
         y_q = keep.tile([P, S2], U32, name="y_q", align_bytes=64)
@@ -120,8 +133,7 @@ def tile_list_band_sine_field_kernel(
         def cols(pair, j0, w):
             return pair[j0 // BANK][:, j0 % BANK : j0 % BANK + w]
 
-        def gather_v(b, tag):
-            dealt = keep.tile([P, PASS], U32, name="v_q%d" % b, tag=tag, align_bytes=64)
+        def gather_v(b, dealt):
             span = PASS // 16
             nc.vector.tensor_copy(
                 dealt[:].rearrange("p (t a r) -> p a t r", t=PACK, r=RUN),
@@ -145,8 +157,8 @@ def tile_list_band_sine_field_kernel(
             nc.vector.quantize_mx(out=codes[:].bitcast(FP8X4), scales=wm_sc[b][:], in_=wm_bf[b][:])
             return codes
 
-        def psum_slices(tag, w):
-            per = BANK // w
+        def psum_slices(tag, w, per=None):
+            per = per or BANK // w
             banks = [psum.tile([P, BANK], F32, name=tag, tag=tag) for bank in range(PACK // per)]
             return [banks[t // per][:, (t % per) * w : (t % per + 1) * w] for t in range(PACK)]
 
@@ -156,8 +168,8 @@ def tile_list_band_sine_field_kernel(
         def by_pairs(tile):
             return tile.rearrange("p t (c e) -> p c t e", e=2)
 
-        def sines(b, j0, w, sn, banks="a"):
-            acc = psum_slices(banks, w)
+        def sines(b, j0, w, sn, banks="a", per=None):
+            acc = psum_slices(banks, w, per)
             for t in range(PACK):
                 nc.tensor.matmul_mx(
                     out=acc[t],
@@ -178,36 +190,38 @@ def tile_list_band_sine_field_kernel(
         def woven_tile(tag, w):
             return keep.tile([P, PACK * w], BF16, name=tag, tag=tag, align_bytes=64)[:]
 
-        def amplify(b, sn, h_bf):
+        def amplify(b, c, sn):
             spread = am[:, b : b + 1].to_broadcast([P, sn.shape[2] // 2, PACK, 2])
-            nc.vector.tensor_tensor(woven(h_bf), by_pairs(sn), spread, ALU.mult)
+            nc.vector.tensor_tensor(woven(h_bf[c][:, PACK * W * b : PACK * W * (b + 1)]), by_pairs(sn), spread, ALU.mult)
 
-        def quantise_h(b, j0, w, h_bf):
-            nc.vector.quantize_mx(out=cols(h_q[b], j0, w).bitcast(FP8X4), scales=cols(h_sc[b], j0, w), in_=h_bf)
+        def quantise_h(c, b0, b1):
+            nc.vector.quantize_mx(
+                out=h_q[c][:, W * b0 : W * b1].bitcast(FP8X4),
+                scales=h_sc[c][:, W * b0 : W * b1],
+                in_=h_bf[c][:, PACK * W * b0 : PACK * W * b1],
+            )
 
         def mix(j0, w, banks="y"):
             acc = psum_slices(banks, w)
             per = BANK // w
-            step = w if w == BANK else P
             for t in range(PACK):
-                for c in range(0, w, step):
-                    nc.tensor.matmul_mx(
-                        out=acc[t][:, c : c + step],
-                        lhsT=w4_q[:, 2 * P * t : 2 * P * (t + 1)].bitcast(FP4X4),
-                        lhsT_scale=w4_sc[:, P * t : P * (t + 1)],
-                        rhs=cols(v2_q, j0 + c, step).bitcast(FP8X4),
-                        rhs_scale=v2_sc[:, j0 + c : j0 + c + step],
-                        start=(t % per == 0 and c == 0),
-                        stop=False,
-                    )
+                nc.tensor.matmul_mx(
+                    out=acc[t],
+                    lhsT=w4_q[:, 2 * P * t : 2 * P * (t + 1)].bitcast(FP4X4),
+                    lhsT_scale=w4_sc[:, P * t : P * (t + 1)],
+                    rhs=cols(v2_q, j0, w).bitcast(FP8X4),
+                    rhs_scale=v2_sc[:, j0 : j0 + w],
+                    start=(t % per == 0),
+                    stop=False,
+                )
             for b in range(2):
                 for t in range(PACK):
                     nc.tensor.matmul_mx(
                         out=acc[t],
                         lhsT=wm_q[b][:, P * t : P * (t + 1)].bitcast(FP8X4),
                         lhsT_scale=wm_sc[b][:, P * t : P * (t + 1)],
-                        rhs=cols(h_q[b], j0, w).bitcast(FP8X4),
-                        rhs_scale=cols(h_sc[b], j0, w),
+                        rhs=h_q[j0 // W][:, W * b : W * (b + 1)].bitcast(FP8X4),
+                        rhs_scale=h_sc[j0 // W][:, W * b : W * (b + 1)],
                         start=False,
                         stop=(b == 1 and t % per == per - 1),
                     )
@@ -222,73 +236,75 @@ def tile_list_band_sine_field_kernel(
         def round_y(y, y_bf, c0, c1, copy):
             copy(woven(y_bf[:, PACK * c0 : PACK * c1]), by_pairs(y[:, :, c0:c1]))
 
-        def store_codes(j0, w, y_bf):
-            nc.vector.quantize_mx(out=y_q[:, j0 : j0 + w].bitcast(FP8X4), scales=y_sc[:, j0 : j0 + w], in_=y_bf)
+        def quantise_y(j0, w):
+            nc.vector.quantize_mx(
+                out=y_q[:, j0 : j0 + w].bitcast(FP8X4),
+                scales=y_sc[:, j0 : j0 + w],
+                in_=y_bf[j0 // W][:, PACK * (j0 % W) : PACK * (j0 % W + w)],
+            )
+
+        def store_codes(j0, w):
             nc.sync.dma_start(
                 out_1[0].rearrange("p j t -> p (j t)").bitcast(I32)[:, j0 : j0 + w], y_q[:, j0 : j0 + w].bitcast(I32)
             )
 
-        v_q = [gather_v(0, "v_q0"), gather_v(1, "v_q1")]
+        v_q = [gather_v(0, keep.tile([P, PASS], U32, name="v_q0", align_bytes=64))]
         gather_v2(0, 256)
         gather_v2(256, 256)
-        gather_v2(512, 512)
         w4_q = keep.tile([P, 2 * N], U8, name="w4_q", align_bytes=64)
         nc.scalar.copy(
             w4_q[:].bitcast(U16).rearrange("p (t m) -> p t m", t=PACK),
             w4_raw[:].bitcast(U16).rearrange("p (m t) -> p t m", t=PACK),
         )
-        w4_sc = keep.tile([P, N], U8, name="w4_sc", tag="v2_win", align_bytes=64)
-        nc.vector.tensor_copy(
-            w4_sc[:].rearrange("p (t m) -> p t m", t=PACK), s4_raw[:].rearrange("p (m t) -> p t m", t=PACK)
-        )
-        move_rows(w4_sc, w4_sc)
+        v_q.append(gather_v(1, laid.tile([P, PASS], U32, name="v_q1", offset=0, align_bytes=64)))
+        gather_v2(512, 512)
 
-        sn_a0a = sines(0, 0, 256, sine_tile("sn_a0a", 256))
-        sn_a0b = sines(0, 256, 256, sine_tile("sn_a0b", 256))
-        sn_a1 = sines(1, 0, 512, sine_tile("sn_a1", 512), banks="y")
-        h_a0a = woven_tile("h_a0a", 256)
-        h_a0b = woven_tile("h_a0b", 256)
-        amplify(0, sn_a0a, h_a0a)
-        amplify(0, sn_a0b, h_a0b)
-        quantise_h(0, 0, 256, h_a0a)
-        wm_bf.append(keep.tile([P, PACK * N], BF16, name="wm_bf0", tag="h_a0a", align_bytes=64))
-        round_wm(0, 0, P // 2, nc.vector.tensor_copy)
-        quantise_h(0, 256, 256, h_a0b)
-        round_wm(0, P // 2, P, nc.scalar.copy)
-        h_a1 = woven_tile("h_a1", 512)
-        amplify(1, sn_a1, h_a1)
-        wm_q = [quantise_wm(0)]
-        wm_bf.append(keep.tile([P, PACK * N], BF16, name="wm_bf1", tag="sn_a1", align_bytes=64))
-        round_wm(1, 0, 96, nc.vector.tensor_copy)
-        quantise_h(1, 0, 512, h_a1)
-        sn_bc0 = sines(0, 512, 512, wm_raw[:, 0])
-        round_wm(1, 96, P, nc.scalar.copy)
-        wm_q.append(quantise_wm(1))
+        y_bf = [woven_tile("y_bf%d" % c, W) for c in range(S2 // W)]
+        sn = {}
+        y = {}
 
-        sn_b1 = sines(1, 512, 256, sine_tile("sn_b1", 256), banks="y")
-        y_a = mix(0, 512, banks="a")
-        h_bc0 = woven_tile("sn_a1", 512)
-        amplify(0, sn_bc0, h_bc0)
-        h_b1 = woven_tile("h_b1", 256)
-        amplify(1, sn_b1, h_b1)
-        quantise_h(0, 512, 512, h_bc0)
-        quantise_h(1, 512, 256, h_b1)
-        sn_c1 = sines(1, 768, 256, sine_tile("sn_c1", 256), banks="y")
-        yb_a = woven_tile("yb_a", 512)
-        round_y(y_a, yb_a, 0, 384, nc.scalar.copy)
-        y_b = mix(512, 256)
-        h_c1 = woven_tile("h_c1", 256)
-        amplify(1, sn_c1, h_c1)
-        quantise_h(1, 768, 256, h_c1)
-        y_c = mix(768, 256)
-        round_y(y_a, yb_a, 384, 512, nc.vector.tensor_copy)
-        store_codes(0, 512, yb_a)
-        yb_b = woven_tile("yb_b", 256)
-        round_y(y_b, yb_b, 0, 256, nc.vector.tensor_copy)
-        yb_c = woven_tile("yb_c", 256)
-        round_y(y_c, yb_c, 0, 256, nc.vector.tensor_copy)
-        store_codes(512, 256, yb_b)
-        store_codes(768, 256, yb_c)
+        def chunk_sines(c, b, banks="a", per=None):
+            sn[c, b] = sines(b, W * c, W, sine_tile("sn%d%d" % (c, b), W), banks, per)
+
+        chunk_sines(0, 0, banks="y", per=1)
+        chunk_sines(0, 1)
+        for b in range(2):
+            wm_bf.append(keep.tile([P, PACK * N], BF16, name="wm_bf%d" % b, align_bytes=64))
+        round_wm(0, 0, 32, nc.vector.tensor_copy)
+        round_wm(0, 32, P, nc.scalar.copy)
+        amplify(0, 0, sn[0, 0])
+        amplify(1, 0, sn[0, 1])
+        round_wm(1, 0, P, nc.vector.tensor_copy)
+        quantise_h(0, 0, 2)
+        wm_q = [quantise_wm(0), quantise_wm(1)]
+        for c in (1, 2):
+            chunk_sines(c, 0)
+            chunk_sines(c, 1)
+            y[c - 1] = mix(W * (c - 1), W)
+            amplify(0, c, sn[c, 0])
+            amplify(1, c, sn[c, 1])
+            quantise_h(c, 0, 2)
+        chunk_sines(3, 0)
+        chunk_sines(3, 1)
+        y[2] = mix(2 * W, W)
+        amplify(0, 3, sn[3, 0])
+        amplify(1, 3, sn[3, 1])
+        quantise_h(3, 0, 1)
+        quantise_h(3, 1, 2)
+        round_y(y[1], y_bf[1], 0, 256, nc.scalar.copy)
+        y[3] = mix(3 * W, W)
+        round_y(y[0], y_bf[0], 0, W, nc.vector.tensor_copy)
+        quantise_y(0, W)
+        round_y(y[2], y_bf[2], 0, W, nc.vector.tensor_copy)
+        quantise_y(W, W)
+        store_codes(0, 2 * W)
+        quantise_y(2 * W, W)
+        store_codes(2 * W, W)
+        round_y(y[3], y_bf[3], 0, W // 2, nc.vector.tensor_copy)
+        round_y(y[3], y_bf[3], W // 2, W, nc.vector.tensor_copy)
+        quantise_y(3 * W, W // 2)
+        quantise_y(3 * W + W // 2, W // 2)
+        store_codes(3 * W, W)
         for quad in range(P // QUAD):
             queue = nc.scalar if quad % 2 else nc.sync
             queue.dma_start(

@@ -270,8 +270,8 @@ def tile_list_band_sine_field_kernel(
         chunk_sines(0, 1)
         for b in range(2):
             wm_bf.append(keep.tile([P, PACK * N], BF16, name="wm_bf%d" % b, align_bytes=64))
-        round_wm(0, 0, 32, nc.vector.tensor_copy)
-        round_wm(0, 32, P, nc.scalar.copy)
+        round_wm(0, 0, 64, nc.vector.tensor_copy)
+        round_wm(0, 64, P, nc.scalar.copy)
         amplify(0, 0, sn[0, 0])
         amplify(1, 0, sn[0, 1])
         round_wm(1, 0, P, nc.vector.tensor_copy)
@@ -291,15 +291,16 @@ def tile_list_band_sine_field_kernel(
         amplify(1, 3, sn[3, 1])
         quantise_h(3, 0, 1)
         quantise_h(3, 1, 2)
-        round_y(y[1], y_bf[1], 0, 256, nc.scalar.copy)
+        round_y(y[1], y_bf[1], 0, 96, nc.scalar.copy)
         y[3] = mix(3 * W, W)
         round_y(y[0], y_bf[0], 0, W, nc.vector.tensor_copy)
         quantise_y(0, W)
+        store_codes(0, W)
+        round_y(y[1], y_bf[1], 96, W, nc.vector.tensor_copy)
         round_y(y[2], y_bf[2], 0, W, nc.vector.tensor_copy)
         quantise_y(W, W)
-        store_codes(0, 2 * W)
         quantise_y(2 * W, W)
-        store_codes(2 * W, W)
+        store_codes(W, 2 * W)
         round_y(y[3], y_bf[3], 0, W // 2, nc.vector.tensor_copy)
         round_y(y[3], y_bf[3], W // 2, W, nc.vector.tensor_copy)
         quantise_y(3 * W, W // 2)

@@ -69,30 +69,45 @@ def tile_list_band_sine_field_kernel(
         nc.sync.dma_start(bi[:], bias.rearrange("(p t) -> p t", t=PACK))
 
         s_picked = keep.tile([P, S], U8, name="s_picked", align_bytes=64)
-        s2_picked = keep.tile([P, S2], U8, name="s2_picked", tag="s2_picked", align_bytes=64)
-        planes = keep.tile([P, S2 + S + N], U8, name="planes", align_bytes=64)
+        s2_first = keep.tile([P, BANK], U8, name="s2_first", tag="s2_first", align_bytes=64)
+        s2_second = keep.tile([P, BANK], U8, name="s2_second", tag="s2_second", align_bytes=64)
+        early = keep.tile([P, S + BANK], U8, name="early", align_bytes=64)
+        late = keep.tile([P, BANK + N], U8, name="late", align_bytes=64)
+
+        def move_rows(queue, plane):
+            for quad in range(P // QUAD):
+                queue.dma_start(
+                    plane[QUAD * quad : QUAD * quad + SCALE_ROWS, :].bitcast(I32),
+                    plane[LOW + SCALE_ROWS * quad : LOW + SCALE_ROWS * (quad + 1), :].bitcast(I32),
+                )
+
+        wm_rows = wm.rearrange("(b a u r) n -> b u a r n", b=2, u=PACK, r=RUN)
+
+        def load_wm(b, tag):
+            raw = keep.tile([P, PACK, N], F32, name="wm_raw%d" % b, tag=tag, align_bytes=64)
+            for u in range(PACK):
+                nc.sync.dma_start(raw[:, u, :], wm_rows[b, u])
+            return raw
+
         nc.vector.tensor_copy(s_picked[:], s_win[:].indirect(idx[:]))
-        nc.vector.tensor_copy(s2_picked[:], s2_win[:].indirect(idx2[:]))
+        nc.vector.tensor_copy(s2_first[:], s2_win[:].indirect(idx2[:, 0 : BANK // 16]))
         nc.vector.tensor_copy(
-            planes[:, S2 : S2 + S].bitcast(I32).rearrange("p (b t a) -> p b t a", b=2, t=PACK),
+            early[:, 0:S].bitcast(I32).rearrange("p (b t a) -> p b t a", b=2, t=PACK),
             s_picked[:].bitcast(I32).rearrange("p (b a t) -> p b t a", b=2, t=PACK),
         )
         nc.vector.tensor_copy(
-            planes[:, S2 + S :].rearrange("p (t m) -> p t m", t=PACK), s4_raw[:].rearrange("p (m t) -> p t m", t=PACK)
+            late[:, BANK:].rearrange("p (t m) -> p t m", t=PACK), s4_raw[:].rearrange("p (m t) -> p t m", t=PACK)
         )
-        nc.vector.tensor_copy(planes[:, 0:S2].bitcast(I32), s2_picked[:].bitcast(I32))
-
-        def move_rows(dst, src):
-            for quad in range(P // QUAD):
-                nc.sync.dma_start(
-                    dst[QUAD * quad : QUAD * quad + SCALE_ROWS, :].bitcast(I32),
-                    src[LOW + SCALE_ROWS * quad : LOW + SCALE_ROWS * (quad + 1), :].bitcast(I32),
-                )
-
-        move_rows(planes, planes)
-        v2_sc = planes[:, 0:S2]
-        v_sc = planes[:, S2 : S2 + S]
-        w4_sc = planes[:, S2 + S :]
+        nc.vector.tensor_copy(early[:, S:].bitcast(I32), s2_first[:].bitcast(I32))
+        move_rows(nc.sync, early)
+        wm_raw = [load_wm(0, "s2_first")]
+        nc.vector.tensor_copy(s2_second[:], s2_win[:].indirect(idx2[:, BANK // 16 :]))
+        nc.vector.tensor_copy(late[:, 0:BANK].bitcast(I32), s2_second[:].bitcast(I32))
+        move_rows(nc.sync, late)
+        wm_raw.append(load_wm(1, "s2_second"))
+        v2_sc = [early[:, S:], late[:, 0:BANK]]
+        v_sc = early[:, 0:S]
+        w4_sc = late[:, BANK:]
 
         sorted_rows = keep.tile([P, PASS], F32, name="sorted_rows")
         nc.scalar.activation(
@@ -111,12 +126,6 @@ def tile_list_band_sine_field_kernel(
         coef = keep.tile([P, COEF, PACK, 2], F32, name="coef")
         nc.scalar.copy(coef[:], by_row[:, 0:COEF, :].unsqueeze(3).to_broadcast([P, COEF, PACK, 2]))
         am = coef[:, 2:COEF]
-
-        wm_rows = wm.rearrange("(b a u r) n -> b u a r n", b=2, u=PACK, r=RUN)
-        wm_raw = keep.tile([P, 2, PACK, N], F32, name="wm_raw", tag="s2_picked", align_bytes=64)
-        for b in range(2):
-            for u in range(PACK):
-                nc.sync.dma_start(wm_raw[:, b, u, :], wm_rows[b, u])
 
         v2_q = [
             keep.tile([P, BANK], U32, name="v2_q0", align_bytes=64),
@@ -149,7 +158,7 @@ def tile_list_band_sine_field_kernel(
         def round_wm(b, m0, m1, copy):
             copy(
                 wm_bf[b][:].rearrange("p (t m u) -> p m u t", t=PACK, u=PACK)[:, m0:m1],
-                wm_raw[:, b].rearrange("p u (m t) -> p m u t", t=PACK)[:, m0:m1],
+                wm_raw[b][:].rearrange("p u (m t) -> p m u t", t=PACK)[:, m0:m1],
             )
 
         def quantise_wm(b):
@@ -176,7 +185,7 @@ def tile_list_band_sine_field_kernel(
                     lhsT=v_q[b][:, P * t : P * (t + 1)].bitcast(FP8X4),
                     lhsT_scale=v_sc[:, PASS * b + P * t : PASS * b + P * (t + 1)],
                     rhs=cols(v2_q, j0, w).bitcast(FP8X4),
-                    rhs_scale=v2_sc[:, j0 : j0 + w],
+                    rhs_scale=cols(v2_sc, j0, w),
                     start=True,
                     stop=True,
                 )
@@ -210,7 +219,7 @@ def tile_list_band_sine_field_kernel(
                     lhsT=w4_q[:, 2 * P * t : 2 * P * (t + 1)].bitcast(FP4X4),
                     lhsT_scale=w4_sc[:, P * t : P * (t + 1)],
                     rhs=cols(v2_q, j0, w).bitcast(FP8X4),
-                    rhs_scale=v2_sc[:, j0 : j0 + w],
+                    rhs_scale=cols(v2_sc, j0, w),
                     start=(t % per == 0),
                     stop=False,
                 )
@@ -277,15 +286,14 @@ def tile_list_band_sine_field_kernel(
         round_wm(1, 0, P, nc.vector.tensor_copy)
         quantise_h(0, 0, 2)
         wm_q = [quantise_wm(0), quantise_wm(1)]
-        for c in (1, 2):
+        for c in (1, 2, 3):
             chunk_sines(c, 0)
             chunk_sines(c, 1)
+        for c in (1, 2):
             y[c - 1] = mix(W * (c - 1), W)
             amplify(0, c, sn[c, 0])
             amplify(1, c, sn[c, 1])
             quantise_h(c, 0, 2)
-        chunk_sines(3, 0)
-        chunk_sines(3, 1)
         y[2] = mix(2 * W, W)
         amplify(0, 3, sn[3, 0])
         amplify(1, 3, sn[3, 1])

@@ -28,6 +28,8 @@ RUN = 4
 SCALE_ROWS = ROWS * QUAD // P
 W = 256
 COEF = 4
+SHARE = 96
+WM_ON_VECTOR = 64
 
 
 def tile_list_band_sine_field_kernel(
@@ -39,7 +41,8 @@ def tile_list_band_sine_field_kernel(
         lists = ctx.enter_context(tc.tile_pool(name="lists", bufs=1))
         keep = ctx.enter_context(tc.tile_pool(name="keep", bufs=1))
         laid = ctx.enter_context(tc.tile_pool(name="laid", bufs=1))
-        psum = ctx.enter_context(tc.psum_pool(name="psum", bufs=4))
+        psum = ctx.enter_context(tc.psum_pool(name="psum", bufs=1))
+        bank_count = {"a": 4, "y": 3}
 
         idx = lists.tile([P, S // 16], U16, name="idx")
         idx2 = lists.tile([P, S2 // 16], U16, name="idx2")
@@ -119,7 +122,7 @@ def tile_list_band_sine_field_kernel(
             sorted_rows[0:COEF, :].rearrange("p (t a r) -> p t a r", t=PACK, r=RUN),
             coef_rows[:].rearrange("p (a t r) -> p t a r", t=PACK, r=RUN),
         )
-        turned = psum.tile([P, BANK], F32, name="turned", tag="a")
+        turned = psum.tile([P, BANK], F32, name="turned")
         for t in range(PACK):
             nc.tensor.transpose(turned[:, P * t : P * (t + 1)], sorted_rows[:, P * t : P * (t + 1)], ident[:])
         by_row = turned[:].rearrange("p (t n) -> p n t", t=PACK)
@@ -131,7 +134,6 @@ def tile_list_band_sine_field_kernel(
             keep.tile([P, BANK], U32, name="v2_q0", align_bytes=64),
             laid.tile([P, BANK], U32, name="v2_q1", offset=4 * PASS, align_bytes=64),
         ]
-        h_bf = [keep.tile([P, 2 * PACK * W], BF16, name="h_bf%d" % c, align_bytes=64) for c in range(S2 // W)]
         h_q = [keep.tile([P, 2 * W], U32, name="h_q%d" % c, align_bytes=64) for c in range(S2 // W)]
         h_sc = [keep.tile([P, 2 * W], U8, name="h_sc%d" % c, align_bytes=64) for c in range(S2 // W)]
         wm_sc = [keep.tile([P, N], U8, name="wm_sc%d" % b, align_bytes=64) for b in range(2)]
@@ -168,7 +170,7 @@ def tile_list_band_sine_field_kernel(
 
         def psum_slices(tag, w, per=None):
             per = per or BANK // w
-            banks = [psum.tile([P, BANK], F32, name=tag, tag=tag) for bank in range(PACK // per)]
+            banks = [psum.tile([P, BANK], F32, name=tag, tag=tag, bufs=bank_count[tag]) for bank in range(PACK // per)]
             return [banks[t // per][:, (t % per) * w : (t % per + 1) * w] for t in range(PACK)]
 
         def woven(tile):
@@ -199,38 +201,61 @@ def tile_list_band_sine_field_kernel(
         def woven_tile(tag, w):
             return keep.tile([P, PACK * w], BF16, name=tag, tag=tag, align_bytes=64)[:]
 
-        def amplify(b, c, sn):
-            spread = am[:, b : b + 1].to_broadcast([P, sn.shape[2] // 2, PACK, 2])
-            nc.vector.tensor_tensor(woven(h_bf[c][:, PACK * W * b : PACK * W * (b + 1)]), by_pairs(sn), spread, ALU.mult)
+        def h_start(c, b):
+            return PACK * (2 * W - SHARE + W * b if c % 2 else W * (1 - b))
 
-        def quantise_h(c, b0, b1):
+        def slot(c, b):
+            return b if c % 2 else 1 - b
+
+        def amplify(engine, c, b, c0, c1):
+            pairs = (c1 - c0) // 2
+            if engine is nc.vector:
+                amp_t = by_row[:, 2 + b, :].unsqueeze(1).unsqueeze(3).to_broadcast([P, pairs, PACK, 2])
+            else:
+                amp_t = am[:, b : b + 1].to_broadcast([P, pairs, PACK, 2])
+            first = h_start(c, b)
+            engine.tensor_tensor(
+                woven(h_bf[:, first + PACK * c0 : first + PACK * c1]), by_pairs(sn[c, b][:, :, c0:c1]), amp_t, ALU.mult
+            )
+
+        def products(c):
+            g0 = 0 if c % 2 else W - SHARE
+            v0 = SHARE if c % 2 else 0
+            amplify(nc.gpsimd, c, 0, g0, g0 + SHARE)
+            amplify(nc.vector, c, 0, v0, v0 + W - SHARE)
+            amplify(nc.vector, c, 1, 0, W)
+
+        def quantise_h(c, s0, s1):
+            first = min(h_start(c, 0), h_start(c, 1))
             nc.vector.quantize_mx(
-                out=h_q[c][:, W * b0 : W * b1].bitcast(FP8X4),
-                scales=h_sc[c][:, W * b0 : W * b1],
-                in_=h_bf[c][:, PACK * W * b0 : PACK * W * b1],
+                out=h_q[c][:, W * s0 : W * s1].bitcast(FP8X4),
+                scales=h_sc[c][:, W * s0 : W * s1],
+                in_=h_bf[:, first + PACK * W * s0 : first + PACK * W * s1],
             )
 
         def mix(j0, w, banks="y"):
             acc = psum_slices(banks, w)
             per = BANK // w
-            for t in range(PACK):
-                nc.tensor.matmul_mx(
-                    out=acc[t],
-                    lhsT=w4_q[:, 2 * P * t : 2 * P * (t + 1)].bitcast(FP4X4),
-                    lhsT_scale=w4_sc[:, P * t : P * (t + 1)],
-                    rhs=cols(v2_q, j0, w).bitcast(FP8X4),
-                    rhs_scale=cols(v2_sc, j0, w),
-                    start=(t % per == 0),
-                    stop=False,
-                )
+            c = j0 // W
+            for t0 in range(0, PACK, per):
+                for t in range(t0, t0 + per):
+                    nc.tensor.matmul_mx(
+                        out=acc[t],
+                        lhsT=w4_q[:, 2 * P * t : 2 * P * (t + 1)].bitcast(FP4X4),
+                        lhsT_scale=w4_sc[:, P * t : P * (t + 1)],
+                        rhs=cols(v2_q, j0, w).bitcast(FP8X4),
+                        rhs_scale=cols(v2_sc, j0, w),
+                        start=(t == t0),
+                        stop=False,
+                    )
             for b in range(2):
                 for t in range(PACK):
                     nc.tensor.matmul_mx(
                         out=acc[t],
                         lhsT=wm_q[b][:, P * t : P * (t + 1)].bitcast(FP8X4),
                         lhsT_scale=wm_sc[b][:, P * t : P * (t + 1)],
-                        rhs=h_q[j0 // W][:, W * b : W * (b + 1)].bitcast(FP8X4),
-                        rhs_scale=h_sc[j0 // W][:, W * b : W * (b + 1)],
+                        rhs=h_q[c][:, W * slot(c, b) : W * (slot(c, b) + 1)].bitcast(FP8X4),
+                        rhs_scale=h_sc[c][:, W * slot(c, b) : W * (slot(c, b) + 1)],
                         start=False,
                         stop=(b == 1 and t % per == per - 1),
                     )
@@ -275,36 +300,35 @@ def tile_list_band_sine_field_kernel(
         def chunk_sines(c, b, banks="a", per=None):
             sn[c, b] = sines(b, W * c, W, sine_tile("sn%d%d" % (c, b), W), banks, per)
 
-        chunk_sines(0, 0, banks="y", per=1)
+        h_bf = keep.tile([P, PACK * (4 * W - SHARE)], BF16, name="h_bf", tag="v2_win", align_bytes=64)
+        chunk_sines(0, 0, banks="y")
         chunk_sines(0, 1)
         for b in range(2):
             wm_bf.append(keep.tile([P, PACK * N], BF16, name="wm_bf%d" % b, align_bytes=64))
-        round_wm(0, 0, 64, nc.vector.tensor_copy)
-        round_wm(0, 64, P, nc.scalar.copy)
-        amplify(0, 0, sn[0, 0])
-        amplify(1, 0, sn[0, 1])
+        round_wm(0, 0, WM_ON_VECTOR, nc.vector.tensor_copy)
+        round_wm(0, WM_ON_VECTOR, P, nc.scalar.copy)
+        products(0)
         round_wm(1, 0, P, nc.vector.tensor_copy)
         quantise_h(0, 0, 2)
-        wm_q = [quantise_wm(0), quantise_wm(1)]
         for c in (1, 2, 3):
             chunk_sines(c, 0)
             chunk_sines(c, 1)
-        for c in (1, 2):
-            y[c - 1] = mix(W * (c - 1), W)
-            amplify(0, c, sn[c, 0])
-            amplify(1, c, sn[c, 1])
-            quantise_h(c, 0, 2)
-        y[2] = mix(2 * W, W)
-        amplify(0, 3, sn[3, 0])
-        amplify(1, 3, sn[3, 1])
+        products(1)
+        wm_q = [quantise_wm(0), quantise_wm(1)]
+        quantise_h(1, 0, 2)
+        y[0] = mix(0, W)
+        products(2)
+        quantise_h(2, 0, 2)
+        y[1] = mix(W, W)
+        products(3)
+        round_y(y[0], y_bf[0], 0, W, nc.vector.tensor_copy)
         quantise_h(3, 0, 1)
         quantise_h(3, 1, 2)
-        round_y(y[1], y_bf[1], 0, 96, nc.scalar.copy)
-        y[3] = mix(3 * W, W)
-        round_y(y[0], y_bf[0], 0, W, nc.vector.tensor_copy)
+        y[2] = mix(2 * W, W, banks="a")
+        y[3] = mix(3 * W, W, banks="a")
         quantise_y(0, W)
         store_codes(0, W)
-        round_y(y[1], y_bf[1], 96, W, nc.vector.tensor_copy)
+        round_y(y[1], y_bf[1], 0, W, nc.vector.tensor_copy)
         round_y(y[2], y_bf[2], 0, W, nc.vector.tensor_copy)
         quantise_y(W, W)
         quantise_y(2 * W, W)

@@ -27,8 +27,9 @@ LOW = P - ROWS
 RUN = 4
 SCALE_ROWS = ROWS * QUAD // P
 W = 256
+HALF = W // 2
 COEF = 4
-SHARE = 96
+SHARE = 128
 WM_ON_VECTOR = 64
 
 
@@ -225,12 +226,12 @@ def tile_list_band_sine_field_kernel(
             amplify(nc.vector, c, 0, v0, v0 + W - SHARE)
             amplify(nc.vector, c, 1, 0, W)
 
-        def quantise_h(c, s0, s1):
+        def quantise_h(c, w0, w1):
             first = min(h_start(c, 0), h_start(c, 1))
             nc.vector.quantize_mx(
-                out=h_q[c][:, W * s0 : W * s1].bitcast(FP8X4),
-                scales=h_sc[c][:, W * s0 : W * s1],
-                in_=h_bf[:, first + PACK * W * s0 : first + PACK * W * s1],
+                out=h_q[c][:, w0:w1].bitcast(FP8X4),
+                scales=h_sc[c][:, w0:w1],
+                in_=h_bf[:, first + PACK * w0 : first + PACK * w1],
             )
 
         def mix(j0, w, banks="y"):
@@ -254,8 +255,8 @@ def tile_list_band_sine_field_kernel(
                         out=acc[t],
                         lhsT=wm_q[b][:, P * t : P * (t + 1)].bitcast(FP8X4),
                         lhsT_scale=wm_sc[b][:, P * t : P * (t + 1)],
-                        rhs=h_q[c][:, W * slot(c, b) : W * (slot(c, b) + 1)].bitcast(FP8X4),
-                        rhs_scale=h_sc[c][:, W * slot(c, b) : W * (slot(c, b) + 1)],
+                        rhs=h_q[c][:, W * slot(c, b) + j0 % W : W * slot(c, b) + j0 % W + w].bitcast(FP8X4),
+                        rhs_scale=h_sc[c][:, W * slot(c, b) + j0 % W : W * slot(c, b) + j0 % W + w],
                         start=False,
                         stop=(b == 1 and t % per == per - 1),
                     )
@@ -263,8 +264,8 @@ def tile_list_band_sine_field_kernel(
             out_rows = out_0.rearrange("(p t) j -> p t j", t=PACK)
             for t in range(PACK):
                 nc.scalar.activation(out=y[:, t, :], in_=acc[t], func=ACT.Identity, bias=bi[:, t : t + 1])
-                if t % 2 == 1:
-                    nc.sync.dma_start(out_rows[:, t - 1 : t + 1, j0 : j0 + w], y[:, t - 1 : t + 1, :])
+                if t % per == per - 1:
+                    nc.sync.dma_start(out_rows[:, t + 1 - per : t + 1, j0 : j0 + w], y[:, t + 1 - per : t + 1, :])
             return y
 
         def round_y(y, y_bf, c0, c1, copy):
@@ -306,26 +307,31 @@ def tile_list_band_sine_field_kernel(
         for b in range(2):
             wm_bf.append(keep.tile([P, PACK * N], BF16, name="wm_bf%d" % b, align_bytes=64))
         round_wm(0, 0, WM_ON_VECTOR, nc.vector.tensor_copy)
-        round_wm(0, WM_ON_VECTOR, P, nc.scalar.copy)
         products(0)
+        round_wm(0, WM_ON_VECTOR, P, nc.vector.tensor_copy)
         round_wm(1, 0, P, nc.vector.tensor_copy)
-        quantise_h(0, 0, 2)
-        for c in (1, 2, 3):
-            chunk_sines(c, 0)
-            chunk_sines(c, 1)
+        wm_q = [quantise_wm(0)]
+        quantise_h(0, 0, 2 * W)
+        chunk_sines(1, 0)
+        chunk_sines(1, 1)
+        for b in range(2):
+            wide = sines(b, 2 * W, 2 * W, sine_tile("sn_wide%d" % b, 2 * W))
+            sn[2, b], sn[3, b] = wide[:, :, 0:W], wide[:, :, W:]
         products(1)
-        wm_q = [quantise_wm(0), quantise_wm(1)]
-        quantise_h(1, 0, 2)
+        wm_q.append(quantise_wm(1))
+        quantise_h(1, 0, 2 * W)
         y[0] = mix(0, W)
         products(2)
-        quantise_h(2, 0, 2)
+        quantise_h(2, W, 2 * W)
+        quantise_h(2, 0, W)
         y[1] = mix(W, W)
+        round_y(y[0], y_bf[0], 0, W, nc.scalar.copy)
         products(3)
-        round_y(y[0], y_bf[0], 0, W, nc.vector.tensor_copy)
-        quantise_h(3, 0, 1)
-        quantise_h(3, 1, 2)
+        quantise_h(3, 0, W)
+        quantise_h(3, W, W + HALF)
+        quantise_h(3, W + HALF, 2 * W)
         y[2] = mix(2 * W, W, banks="a")
-        y[3] = mix(3 * W, W, banks="a")
+        last = [mix(3 * W, HALF, banks="a"), mix(3 * W + HALF, HALF, banks="a")]
         quantise_y(0, W)
         store_codes(0, W)
         round_y(y[1], y_bf[1], 0, W, nc.vector.tensor_copy)
@@ -333,8 +339,8 @@ def tile_list_band_sine_field_kernel(
         quantise_y(W, W)
         quantise_y(2 * W, W)
         store_codes(W, 2 * W)
-        round_y(y[3], y_bf[3], 0, W // 2, nc.vector.tensor_copy)
-        round_y(y[3], y_bf[3], W // 2, W, nc.vector.tensor_copy)
+        round_y(last[0], y_bf[3][:, 0 : PACK * HALF], 0, HALF, nc.vector.tensor_copy)
+        round_y(last[1], y_bf[3][:, PACK * HALF :], 0, HALF, nc.vector.tensor_copy)
         quantise_y(3 * W, W // 2)
         quantise_y(3 * W + W // 2, W // 2)
         store_codes(3 * W, W)

@@ -27,10 +27,10 @@ LOW = P - ROWS
 RUN = 4
 SCALE_ROWS = ROWS * QUAD // P
 W = 256
+Y_ON_SCALAR = 96
 HALF = W // 2
 COEF = 4
-SHARE = 128
-WM_ON_VECTOR = 64
+SHARE = 104
 
 
 def tile_list_band_sine_field_kernel(
@@ -42,6 +42,7 @@ def tile_list_band_sine_field_kernel(
         lists = ctx.enter_context(tc.tile_pool(name="lists", bufs=1))
         keep = ctx.enter_context(tc.tile_pool(name="keep", bufs=1))
         laid = ctx.enter_context(tc.tile_pool(name="laid", bufs=1))
+        held = ctx.enter_context(tc.tile_pool(name="held", bufs=1))
         psum = ctx.enter_context(tc.psum_pool(name="psum", bufs=1))
         bank_count = {"a": 4, "y": 3}
 
@@ -127,15 +128,20 @@ def tile_list_band_sine_field_kernel(
         for t in range(PACK):
             nc.tensor.transpose(turned[:, P * t : P * (t + 1)], sorted_rows[:, P * t : P * (t + 1)], ident[:])
         by_row = turned[:].rearrange("p (t n) -> p n t", t=PACK)
-        coef = keep.tile([P, COEF, PACK, 2], F32, name="coef")
-        nc.scalar.copy(coef[:], by_row[:, 0:COEF, :].unsqueeze(3).to_broadcast([P, COEF, PACK, 2]))
-        am = coef[:, 2:COEF]
+        coef = keep.tile([P, COEF, PACK], F32, name="coef")
+        nc.scalar.copy(coef[:], by_row[:, 0:COEF, :])
 
         v2_q = [
             keep.tile([P, BANK], U32, name="v2_q0", align_bytes=64),
             laid.tile([P, BANK], U32, name="v2_q1", offset=4 * PASS, align_bytes=64),
         ]
-        h_q = [keep.tile([P, 2 * W], U32, name="h_q%d" % c, align_bytes=64) for c in range(S2 // W)]
+        room = 2 * PACK * N + 2 * PACK * W
+        last_phase = []
+        for c in range(S2 // W):
+            tile = held.tile([P, 32], F32, name="phase%d" % c, offset=room * c + 2 * PACK * N - 64, align_bytes=64)
+            nc.scalar.copy(tile[:, 0:PACK], by_row[:, 1, :])
+            last_phase.append(tile)
+        h_q = {}
         h_sc = [keep.tile([P, 2 * W], U8, name="h_sc%d" % c, align_bytes=64) for c in range(S2 // W)]
         wm_sc = [keep.tile([P, N], U8, name="wm_sc%d" % b, align_bytes=64) for b in range(2)]
         wm_bf = []
@@ -144,6 +150,9 @@ def tile_list_band_sine_field_kernel(
 
         def cols(pair, j0, w):
             return pair[j0 // BANK][:, j0 % BANK : j0 % BANK + w]
+
+        def words(j0, w):
+            return cols(v2_q, j0, w)
 
         def gather_v(b, dealt):
             span = PASS // 16
@@ -155,7 +164,7 @@ def tile_list_band_sine_field_kernel(
 
         def gather_v2(j0, w):
             nc.vector.tensor_copy(
-                cols(v2_q, j0, w), v2_win[:].bitcast(U32).indirect(idx2[:, j0 // 16 : (j0 + w) // 16])
+                words(j0, w), v2_win[:].bitcast(U32).indirect(idx2[:, j0 // 16 : (j0 + w) // 16])
             )
 
         def round_wm(b, m0, m1, copy):
@@ -164,8 +173,7 @@ def tile_list_band_sine_field_kernel(
                 wm_raw[b][:].rearrange("p u (m t) -> p m u t", t=PACK)[:, m0:m1],
             )
 
-        def quantise_wm(b):
-            codes = keep.tile([P, N], U32, name="wm_q%d" % b, align_bytes=64)
+        def quantise_wm(b, codes):
             nc.vector.quantize_mx(out=codes[:].bitcast(FP8X4), scales=wm_sc[b][:], in_=wm_bf[b][:])
             return codes
 
@@ -187,13 +195,13 @@ def tile_list_band_sine_field_kernel(
                     out=acc[t],
                     lhsT=v_q[b][:, P * t : P * (t + 1)].bitcast(FP8X4),
                     lhsT_scale=v_sc[:, PASS * b + P * t : PASS * b + P * (t + 1)],
-                    rhs=cols(v2_q, j0, w).bitcast(FP8X4),
+                    rhs=words(j0, w).bitcast(FP8X4),
                     rhs_scale=cols(v2_sc, j0, w),
                     start=True,
                     stop=True,
                 )
             for t in range(PACK):
-                nc.scalar.activation(out=sn[:, t, :], in_=acc[t], func=ACT.Sin, bias=coef[:, b, t, 0:1])
+                nc.scalar.activation(out=sn[:, t, :], in_=acc[t], func=ACT.Sin, bias=(last_phase[j0 // W] if b else coef[:, 0])[:, t : t + 1])
             return sn
 
         def sine_tile(tag, w):
@@ -203,28 +211,31 @@ def tile_list_band_sine_field_kernel(
             return keep.tile([P, PACK * w], BF16, name=tag, tag=tag, align_bytes=64)[:]
 
         def h_start(c, b):
-            return PACK * (2 * W - SHARE + W * b if c % 2 else W * (1 - b))
+            return PACK * (W * b + (2 * W - SHARE) * c)
 
         def slot(c, b):
-            return b if c % 2 else 1 - b
+            return b
 
         def amplify(engine, c, b, c0, c1):
             pairs = (c1 - c0) // 2
+            first = h_start(c, b)
+            out = h_bf[:, first + PACK * c0 : first + PACK * c1]
             if engine is nc.vector:
                 amp_t = by_row[:, 2 + b, :].unsqueeze(1).unsqueeze(3).to_broadcast([P, pairs, PACK, 2])
+                engine.tensor_tensor(woven(out), by_pairs(sn[c, b][:, :, c0:c1]), amp_t, ALU.mult)
             else:
-                amp_t = am[:, b : b + 1].to_broadcast([P, pairs, PACK, 2])
-            first = h_start(c, b)
-            engine.tensor_tensor(
-                woven(h_bf[:, first + PACK * c0 : first + PACK * c1]), by_pairs(sn[c, b][:, :, c0:c1]), amp_t, ALU.mult
-            )
+                engine.tensor_tensor(
+                    out.rearrange("p (j t) -> p j t", t=PACK),
+                    sn[c, b][:, :, c0:c1].rearrange("p t j -> p j t"),
+                    coef[:, 2 + b : 3 + b, :].to_broadcast([P, c1 - c0, PACK]),
+                    ALU.mult,
+                )
 
         def products(c):
-            g0 = 0 if c % 2 else W - SHARE
-            v0 = SHARE if c % 2 else 0
-            amplify(nc.gpsimd, c, 0, g0, g0 + SHARE)
-            amplify(nc.vector, c, 0, v0, v0 + W - SHARE)
+            amplify(nc.gpsimd, c, 0, 0, SHARE)
+            amplify(nc.vector, c, 0, SHARE, W)
             amplify(nc.vector, c, 1, 0, W)
+            h_q[c] = held.tile([P, 2 * W], U32, name="h_q%d" % c, offset=room * c + 2 * PACK * N, align_bytes=64)
 
         def quantise_h(c, w0, w1):
             first = min(h_start(c, 0), h_start(c, 1))
@@ -244,7 +255,7 @@ def tile_list_band_sine_field_kernel(
                         out=acc[t],
                         lhsT=w4_q[:, 2 * P * t : 2 * P * (t + 1)].bitcast(FP4X4),
                         lhsT_scale=w4_sc[:, P * t : P * (t + 1)],
-                        rhs=cols(v2_q, j0, w).bitcast(FP8X4),
+                        rhs=words(j0, w).bitcast(FP8X4),
                         rhs_scale=cols(v2_sc, j0, w),
                         start=(t == t0),
                         stop=False,
@@ -301,31 +312,31 @@ def tile_list_band_sine_field_kernel(
         def chunk_sines(c, b, banks="a", per=None):
             sn[c, b] = sines(b, W * c, W, sine_tile("sn%d%d" % (c, b), W), banks, per)
 
-        h_bf = keep.tile([P, PACK * (4 * W - SHARE)], BF16, name="h_bf", tag="v2_win", align_bytes=64)
-        chunk_sines(0, 0, banks="y")
-        chunk_sines(0, 1)
-        for b in range(2):
-            wm_bf.append(keep.tile([P, PACK * N], BF16, name="wm_bf%d" % b, align_bytes=64))
-        round_wm(0, 0, WM_ON_VECTOR, nc.vector.tensor_copy)
+        chunk_sines(0, 0, per=1)
+        wm_bf.append(keep.tile([P, PACK * N], BF16, name="wm_bf0", align_bytes=64))
+        round_wm(0, 0, P, nc.vector.tensor_copy)
+        chunk_sines(0, 1, banks="y")
+        h_bf = keep.tile([P, PACK * (8 * W - 3 * SHARE)], BF16, name="h_bf", tag="s2_first", align_bytes=64)
+        for c in (1, 2, 3):
+            chunk_sines(c, 0)
+            chunk_sines(c, 1)
+        wm_q = []
         products(0)
-        round_wm(0, WM_ON_VECTOR, P, nc.vector.tensor_copy)
-        round_wm(1, 0, P, nc.vector.tensor_copy)
-        wm_q = [quantise_wm(0)]
+        wm_q.append(quantise_wm(0, held.tile([P, N], U32, name="wm_q0", offset=PACK * N, align_bytes=64)))
         quantise_h(0, 0, 2 * W)
-        chunk_sines(1, 0)
-        chunk_sines(1, 1)
-        for b in range(2):
-            wide = sines(b, 2 * W, 2 * W, sine_tile("sn_wide%d" % b, 2 * W))
-            sn[2, b], sn[3, b] = wide[:, :, 0:W], wide[:, :, W:]
         products(1)
-        wm_q.append(quantise_wm(1))
-        quantise_h(1, 0, 2 * W)
+        wm_bf.append(held.tile([P, PACK * N], BF16, name="wm_bf1", offset=room, align_bytes=64))
+        round_wm(1, 0, P, nc.vector.tensor_copy)
+        quantise_h(1, 0, W)
+        wm_q.append(quantise_wm(1, keep.tile([P, N], U32, name="wm_q1", align_bytes=64)))
+        quantise_h(1, W, 2 * W)
         y[0] = mix(0, W)
         products(2)
-        quantise_h(2, W, 2 * W)
         quantise_h(2, 0, W)
+        quantise_h(2, W, 2 * W)
         y[1] = mix(W, W)
         round_y(y[0], y_bf[0], 0, W, nc.scalar.copy)
+        round_y(y[1], y_bf[1], 0, Y_ON_SCALAR, nc.scalar.copy)
         products(3)
         quantise_h(3, 0, W)
         quantise_h(3, W, W + HALF)
@@ -334,7 +345,7 @@ def tile_list_band_sine_field_kernel(
         last = [mix(3 * W, HALF, banks="a"), mix(3 * W + HALF, HALF, banks="a")]
         quantise_y(0, W)
         store_codes(0, W)
-        round_y(y[1], y_bf[1], 0, W, nc.vector.tensor_copy)
+        round_y(y[1], y_bf[1], Y_ON_SCALAR, W, nc.vector.tensor_copy)
         round_y(y[2], y_bf[2], 0, W, nc.vector.tensor_copy)
         quantise_y(W, W)
         quantise_y(2 * W, W)

@@ -28,9 +28,10 @@ RUN = 4
 SCALE_ROWS = ROWS * QUAD // P
 W = 256
 Y_ON_SCALAR = 96
+WM_ON_SCALAR = 64
 HALF = W // 2
 COEF = 4
-SHARE = 104
+SHARE = 128
 
 
 def tile_list_band_sine_field_kernel(
@@ -317,7 +318,11 @@ def tile_list_band_sine_field_kernel(
         round_wm(0, 0, P, nc.vector.tensor_copy)
         chunk_sines(0, 1, banks="y")
         h_bf = keep.tile([P, PACK * (8 * W - 3 * SHARE)], BF16, name="h_bf", tag="s2_first", align_bytes=64)
-        for c in (1, 2, 3):
+        chunk_sines(1, 0)
+        chunk_sines(1, 1)
+        wm_bf.append(held.tile([P, PACK * N], BF16, name="wm_bf1", offset=room, align_bytes=64))
+        round_wm(1, 0, WM_ON_SCALAR, nc.scalar.copy)
+        for c in (2, 3):
             chunk_sines(c, 0)
             chunk_sines(c, 1)
         wm_q = []
@@ -325,8 +330,7 @@ def tile_list_band_sine_field_kernel(
         wm_q.append(quantise_wm(0, held.tile([P, N], U32, name="wm_q0", offset=PACK * N, align_bytes=64)))
         quantise_h(0, 0, 2 * W)
         products(1)
-        wm_bf.append(held.tile([P, PACK * N], BF16, name="wm_bf1", offset=room, align_bytes=64))
-        round_wm(1, 0, P, nc.vector.tensor_copy)
+        round_wm(1, WM_ON_SCALAR, P, nc.vector.tensor_copy)
         quantise_h(1, 0, W)
         wm_q.append(quantise_wm(1, keep.tile([P, N], U32, name="wm_q1", align_bytes=64)))
         quantise_h(1, W, 2 * W)

@@ -31,7 +31,7 @@ Y_ON_SCALAR = 96
 WM_ON_SCALAR = 64
 HALF = W // 2
 COEF = 4
-SHARE = 128
+SHARE = 104
 
 
 def tile_list_band_sine_field_kernel(

@@ -27,11 +27,12 @@ LOW = P - ROWS
 RUN = 4
 SCALE_ROWS = ROWS * QUAD // P
 W = 256
-Y_ON_SCALAR = 96
-WM_ON_SCALAR = 64
+CHUNKS = S2 // W
 HALF = W // 2
 COEF = 4
 SHARE = 104
+WM_ON_SCALAR = 64
+Y_ON_SCALAR = 96
 
 
 def tile_list_band_sine_field_kernel(
@@ -61,7 +62,8 @@ def tile_list_band_sine_field_kernel(
         ident = keep.tile([P, P], F32, name="ident")
         make_identity(nc, ident[:])
         bi = keep.tile([P, PACK], F32, name="bi")
-        w4_raw = laid.tile([P, N // 2], I32, name="w4_raw", offset=4 * PASS - N, align_bytes=64)
+        border = 4 * PASS
+        w4_raw = laid.tile([P, N // 2], I32, name="w4_raw", offset=border - N, align_bytes=64)
         nc.sync.dma_start(idx[:], offs)
         nc.sync.dma_start(s_win[LOW:P, :].bitcast(I32), tab_scales[0].bitcast(I32))
         nc.sync.dma_start(idx2[:], offs2)
@@ -80,9 +82,9 @@ def tile_list_band_sine_field_kernel(
         early = keep.tile([P, S + BANK], U8, name="early", align_bytes=64)
         late = keep.tile([P, BANK + N], U8, name="late", align_bytes=64)
 
-        def move_rows(queue, plane):
+        def move_rows(plane):
             for quad in range(P // QUAD):
-                queue.dma_start(
+                nc.sync.dma_start(
                     plane[QUAD * quad : QUAD * quad + SCALE_ROWS, :].bitcast(I32),
                     plane[LOW + SCALE_ROWS * quad : LOW + SCALE_ROWS * (quad + 1), :].bitcast(I32),
                 )
@@ -105,11 +107,11 @@ def tile_list_band_sine_field_kernel(
             late[:, BANK:].rearrange("p (t m) -> p t m", t=PACK), s4_raw[:].rearrange("p (m t) -> p t m", t=PACK)
         )
         nc.vector.tensor_copy(early[:, S:].bitcast(I32), s2_first[:].bitcast(I32))
-        move_rows(nc.sync, early)
+        move_rows(early)
         wm_raw = [load_wm(0, "s2_first")]
         nc.vector.tensor_copy(s2_second[:], s2_win[:].indirect(idx2[:, BANK // 16 :]))
         nc.vector.tensor_copy(late[:, 0:BANK].bitcast(I32), s2_second[:].bitcast(I32))
-        move_rows(nc.sync, late)
+        move_rows(late)
         wm_raw.append(load_wm(1, "s2_second"))
         v2_sc = [early[:, S:], late[:, 0:BANK]]
         v_sc = early[:, 0:S]
@@ -129,21 +131,22 @@ def tile_list_band_sine_field_kernel(
         for t in range(PACK):
             nc.tensor.transpose(turned[:, P * t : P * (t + 1)], sorted_rows[:, P * t : P * (t + 1)], ident[:])
         by_row = turned[:].rearrange("p (t n) -> p n t", t=PACK)
-        coef = keep.tile([P, COEF, PACK], F32, name="coef")
-        nc.scalar.copy(coef[:], by_row[:, 0:COEF, :])
+        coef = keep.tile([P, 2, PACK], F32, name="coef")
+        nc.scalar.copy(coef[:], by_row[:, 0:COEF:2, :])
 
         v2_q = [
             keep.tile([P, BANK], U32, name="v2_q0", align_bytes=64),
-            laid.tile([P, BANK], U32, name="v2_q1", offset=4 * PASS, align_bytes=64),
+            laid.tile([P, BANK], U32, name="v2_q1", offset=border, align_bytes=64),
         ]
-        room = 2 * PACK * N + 2 * PACK * W
+        below = 2 * PACK * N
+        room = below + 4 * 2 * W
         last_phase = []
-        for c in range(S2 // W):
-            tile = held.tile([P, 32], F32, name="phase%d" % c, offset=room * c + 2 * PACK * N - 64, align_bytes=64)
+        for c in range(CHUNKS):
+            tile = held.tile([P, 32], F32, name="phase%d" % c, offset=room * c + below - 64, align_bytes=64)
             nc.scalar.copy(tile[:, 0:PACK], by_row[:, 1, :])
             last_phase.append(tile)
         h_q = {}
-        h_sc = [keep.tile([P, 2 * W], U8, name="h_sc%d" % c, align_bytes=64) for c in range(S2 // W)]
+        h_sc = [keep.tile([P, 2 * W], U8, name="h_sc%d" % c, align_bytes=64) for c in range(CHUNKS)]
         wm_sc = [keep.tile([P, N], U8, name="wm_sc%d" % b, align_bytes=64) for b in range(2)]
         wm_bf = []
         y_q = keep.tile([P, S2], U32, name="y_q", align_bytes=64)
@@ -151,9 +154,6 @@ def tile_list_band_sine_field_kernel(
 
         def cols(pair, j0, w):
             return pair[j0 // BANK][:, j0 % BANK : j0 % BANK + w]
-
-        def words(j0, w):
-            return cols(v2_q, j0, w)
 
         def gather_v(b, dealt):
             span = PASS // 16
@@ -165,7 +165,7 @@ def tile_list_band_sine_field_kernel(
 
         def gather_v2(j0, w):
             nc.vector.tensor_copy(
-                words(j0, w), v2_win[:].bitcast(U32).indirect(idx2[:, j0 // 16 : (j0 + w) // 16])
+                cols(v2_q, j0, w), v2_win[:].bitcast(U32).indirect(idx2[:, j0 // 16 : (j0 + w) // 16])
             )
 
         def round_wm(b, m0, m1, copy):
@@ -189,99 +189,82 @@ def tile_list_band_sine_field_kernel(
         def by_pairs(tile):
             return tile.rearrange("p t (c e) -> p c t e", e=2)
 
-        def sines(b, j0, w, sn, banks="a", per=None):
-            acc = psum_slices(banks, w, per)
+        def sines(c, b, banks="a", per=None):
+            sn[c, b] = keep.tile([P, PACK, W], F32, name="sn%d%d" % (c, b), align_bytes=64)[:]
+            acc = psum_slices(banks, W, per)
             for t in range(PACK):
                 nc.tensor.matmul_mx(
                     out=acc[t],
                     lhsT=v_q[b][:, P * t : P * (t + 1)].bitcast(FP8X4),
                     lhsT_scale=v_sc[:, PASS * b + P * t : PASS * b + P * (t + 1)],
-                    rhs=words(j0, w).bitcast(FP8X4),
-                    rhs_scale=cols(v2_sc, j0, w),
+                    rhs=cols(v2_q, W * c, W).bitcast(FP8X4),
+                    rhs_scale=cols(v2_sc, W * c, W),
                     start=True,
                     stop=True,
                 )
+            phase_t = last_phase[c] if b else coef[:, 0]
             for t in range(PACK):
-                nc.scalar.activation(out=sn[:, t, :], in_=acc[t], func=ACT.Sin, bias=(last_phase[j0 // W] if b else coef[:, 0])[:, t : t + 1])
-            return sn
+                nc.scalar.activation(out=sn[c, b][:, t, :], in_=acc[t], func=ACT.Sin, bias=phase_t[:, t : t + 1])
 
-        def sine_tile(tag, w):
-            return keep.tile([P, PACK, w], F32, name=tag, tag=tag, align_bytes=64)[:]
+        def h_cols(c, w0, w1):
+            first = (2 * W - SHARE) * c
+            return h_bf[:, PACK * (first + w0) : PACK * (first + w1)]
 
-        def woven_tile(tag, w):
-            return keep.tile([P, PACK * w], BF16, name=tag, tag=tag, align_bytes=64)[:]
-
-        def h_start(c, b):
-            return PACK * (W * b + (2 * W - SHARE) * c)
-
-        def slot(c, b):
-            return b
-
-        def amplify(engine, c, b, c0, c1):
-            pairs = (c1 - c0) // 2
-            first = h_start(c, b)
-            out = h_bf[:, first + PACK * c0 : first + PACK * c1]
-            if engine is nc.vector:
-                amp_t = by_row[:, 2 + b, :].unsqueeze(1).unsqueeze(3).to_broadcast([P, pairs, PACK, 2])
-                engine.tensor_tensor(woven(out), by_pairs(sn[c, b][:, :, c0:c1]), amp_t, ALU.mult)
-            else:
-                engine.tensor_tensor(
-                    out.rearrange("p (j t) -> p j t", t=PACK),
-                    sn[c, b][:, :, c0:c1].rearrange("p t j -> p j t"),
-                    coef[:, 2 + b : 3 + b, :].to_broadcast([P, c1 - c0, PACK]),
-                    ALU.mult,
-                )
+        def vector_product(c, b, c0):
+            amp_t = by_row[:, 2 + b, :].unsqueeze(1).unsqueeze(3).to_broadcast([P, (W - c0) // 2, PACK, 2])
+            out = woven(h_cols(c, W * b + c0, W * (b + 1)))
+            nc.vector.tensor_tensor(out, by_pairs(sn[c, b][:, :, c0:W]), amp_t, ALU.mult)
 
         def products(c):
-            amplify(nc.gpsimd, c, 0, 0, SHARE)
-            amplify(nc.vector, c, 0, SHARE, W)
-            amplify(nc.vector, c, 1, 0, W)
-            h_q[c] = held.tile([P, 2 * W], U32, name="h_q%d" % c, offset=room * c + 2 * PACK * N, align_bytes=64)
+            nc.gpsimd.tensor_tensor(
+                h_cols(c, 0, SHARE).rearrange("p (j t) -> p j t", t=PACK),
+                sn[c, 0][:, :, 0:SHARE].rearrange("p t j -> p j t"),
+                coef[:, 1:2, :].to_broadcast([P, SHARE, PACK]),
+                ALU.mult,
+            )
+            vector_product(c, 0, SHARE)
+            vector_product(c, 1, 0)
+            h_q[c] = held.tile([P, 2 * W], U32, name="h_q%d" % c, offset=room * c + below, align_bytes=64)
 
         def quantise_h(c, w0, w1):
-            first = min(h_start(c, 0), h_start(c, 1))
-            nc.vector.quantize_mx(
-                out=h_q[c][:, w0:w1].bitcast(FP8X4),
-                scales=h_sc[c][:, w0:w1],
-                in_=h_bf[:, first + PACK * w0 : first + PACK * w1],
-            )
+            nc.vector.quantize_mx(out=h_q[c][:, w0:w1].bitcast(FP8X4), scales=h_sc[c][:, w0:w1], in_=h_cols(c, w0, w1))
 
         def mix(j0, w, banks="y"):
             acc = psum_slices(banks, w)
             per = BANK // w
             c = j0 // W
-            for t0 in range(0, PACK, per):
-                for t in range(t0, t0 + per):
-                    nc.tensor.matmul_mx(
-                        out=acc[t],
-                        lhsT=w4_q[:, 2 * P * t : 2 * P * (t + 1)].bitcast(FP4X4),
-                        lhsT_scale=w4_sc[:, P * t : P * (t + 1)],
-                        rhs=words(j0, w).bitcast(FP8X4),
-                        rhs_scale=cols(v2_sc, j0, w),
-                        start=(t == t0),
-                        stop=False,
-                    )
+            for t in range(PACK):
+                nc.tensor.matmul_mx(
+                    out=acc[t],
+                    lhsT=w4_q[:, 2 * P * t : 2 * P * (t + 1)].bitcast(FP4X4),
+                    lhsT_scale=w4_sc[:, P * t : P * (t + 1)],
+                    rhs=cols(v2_q, j0, w).bitcast(FP8X4),
+                    rhs_scale=cols(v2_sc, j0, w),
+                    start=(t % per == 0),
+                    stop=False,
+                )
             for b in range(2):
+                w0 = W * b + j0 % W
                 for t in range(PACK):
                     nc.tensor.matmul_mx(
                         out=acc[t],
                         lhsT=wm_q[b][:, P * t : P * (t + 1)].bitcast(FP8X4),
                         lhsT_scale=wm_sc[b][:, P * t : P * (t + 1)],
-                        rhs=h_q[c][:, W * slot(c, b) + j0 % W : W * slot(c, b) + j0 % W + w].bitcast(FP8X4),
-                        rhs_scale=h_sc[c][:, W * slot(c, b) + j0 % W : W * slot(c, b) + j0 % W + w],
+                        rhs=h_q[c][:, w0 : w0 + w].bitcast(FP8X4),
+                        rhs_scale=h_sc[c][:, w0 : w0 + w],
                         start=False,
                         stop=(b == 1 and t % per == per - 1),
                     )
-            y = keep.tile([P, PACK, w], F32, name="y%d" % j0, align_bytes=64)
+            rows = keep.tile([P, PACK, w], F32, name="y%d" % j0, align_bytes=64)
             out_rows = out_0.rearrange("(p t) j -> p t j", t=PACK)
             for t in range(PACK):
-                nc.scalar.activation(out=y[:, t, :], in_=acc[t], func=ACT.Identity, bias=bi[:, t : t + 1])
+                nc.scalar.activation(out=rows[:, t, :], in_=acc[t], func=ACT.Identity, bias=bi[:, t : t + 1])
                 if t % per == per - 1:
-                    nc.sync.dma_start(out_rows[:, t + 1 - per : t + 1, j0 : j0 + w], y[:, t + 1 - per : t + 1, :])
-            return y
+                    nc.sync.dma_start(out_rows[:, t + 1 - per : t + 1, j0 : j0 + w], rows[:, t + 1 - per : t + 1, :])
+            return rows
 
-        def round_y(y, y_bf, c0, c1, copy):
-            copy(woven(y_bf[:, PACK * c0 : PACK * c1]), by_pairs(y[:, :, c0:c1]))
+        def round_y(rows, out, c0, c1, copy):
+            copy(woven(out[:, PACK * c0 : PACK * c1]), by_pairs(rows[:, :, c0:c1]))
 
         def quantise_y(j0, w):
             nc.vector.quantize_mx(
@@ -296,38 +279,37 @@ def tile_list_band_sine_field_kernel(
             )
 
         v_q = [gather_v(0, keep.tile([P, PASS], U32, name="v_q0", align_bytes=64))]
-        gather_v2(0, 256)
-        gather_v2(256, 256)
+        gather_v2(0, W)
+        gather_v2(W, W)
         w4_q = keep.tile([P, 2 * N], U8, name="w4_q", align_bytes=64)
         nc.scalar.copy(
             w4_q[:].bitcast(U16).rearrange("p (t m) -> p t m", t=PACK),
             w4_raw[:].bitcast(U16).rearrange("p (m t) -> p t m", t=PACK),
         )
         v_q.append(gather_v(1, laid.tile([P, PASS], U32, name="v_q1", offset=0, align_bytes=64)))
-        gather_v2(512, 512)
+        gather_v2(BANK, BANK)
 
-        y_bf = [woven_tile("y_bf%d" % c, W) for c in range(S2 // W)]
+        y_bf = [keep.tile([P, PACK * W], BF16, name="y_bf%d" % c, align_bytes=64)[:] for c in range(CHUNKS)]
         sn = {}
         y = {}
 
-        def chunk_sines(c, b, banks="a", per=None):
-            sn[c, b] = sines(b, W * c, W, sine_tile("sn%d%d" % (c, b), W), banks, per)
-
-        chunk_sines(0, 0, per=1)
+        sines(0, 0, per=1)
         wm_bf.append(keep.tile([P, PACK * N], BF16, name="wm_bf0", align_bytes=64))
         round_wm(0, 0, P, nc.vector.tensor_copy)
-        chunk_sines(0, 1, banks="y")
-        h_bf = keep.tile([P, PACK * (8 * W - 3 * SHARE)], BF16, name="h_bf", tag="s2_first", align_bytes=64)
-        chunk_sines(1, 0)
-        chunk_sines(1, 1)
+        sines(0, 1, banks="y")
+        h_width = 2 * W * CHUNKS - SHARE * (CHUNKS - 1)
+        h_bf = keep.tile([P, PACK * h_width], BF16, name="h_bf", tag="s2_first", align_bytes=64)
+        sines(1, 0)
+        sines(1, 1)
         wm_bf.append(held.tile([P, PACK * N], BF16, name="wm_bf1", offset=room, align_bytes=64))
         round_wm(1, 0, WM_ON_SCALAR, nc.scalar.copy)
-        for c in (2, 3):
-            chunk_sines(c, 0)
-            chunk_sines(c, 1)
+        for c in range(2, CHUNKS):
+            sines(c, 0)
+            sines(c, 1)
+
         wm_q = []
         products(0)
-        wm_q.append(quantise_wm(0, held.tile([P, N], U32, name="wm_q0", offset=PACK * N, align_bytes=64)))
+        wm_q.append(quantise_wm(0, held.tile([P, N], U32, name="wm_q0", offset=below - 4 * N, align_bytes=64)))
         quantise_h(0, 0, 2 * W)
         products(1)
         round_wm(1, WM_ON_SCALAR, P, nc.vector.tensor_copy)
@@ -345,6 +327,7 @@ def tile_list_band_sine_field_kernel(
         quantise_h(3, 0, W)
         quantise_h(3, W, W + HALF)
         quantise_h(3, W + HALF, 2 * W)
+
         y[2] = mix(2 * W, W, banks="a")
         last = [mix(3 * W, HALF, banks="a"), mix(3 * W + HALF, HALF, banks="a")]
         quantise_y(0, W)
@@ -356,8 +339,8 @@ def tile_list_band_sine_field_kernel(
         store_codes(W, 2 * W)
         round_y(last[0], y_bf[3][:, 0 : PACK * HALF], 0, HALF, nc.vector.tensor_copy)
         round_y(last[1], y_bf[3][:, PACK * HALF :], 0, HALF, nc.vector.tensor_copy)
-        quantise_y(3 * W, W // 2)
-        quantise_y(3 * W + W // 2, W // 2)
+        quantise_y(3 * W, HALF)
+        quantise_y(3 * W + HALF, HALF)
         store_codes(3 * W, W)
         for quad in range(P // QUAD):
             queue = nc.scalar if quad % 2 else nc.sync

@@ -131,8 +131,8 @@ def tile_list_band_sine_field_kernel(
         for t in range(PACK):
             nc.tensor.transpose(turned[:, P * t : P * (t + 1)], sorted_rows[:, P * t : P * (t + 1)], ident[:])
         by_row = turned[:].rearrange("p (t n) -> p n t", t=PACK)
-        coef = keep.tile([P, 2, PACK], F32, name="coef")
-        nc.scalar.copy(coef[:], by_row[:, 0:COEF:2, :])
+        coef = keep.tile([P, COEF, PACK], F32, name="coef")
+        nc.scalar.copy(coef[:, 0:COEF:2, :], by_row[:, 0:COEF:2, :])
 
         v2_q = [
             keep.tile([P, BANK], U32, name="v2_q0", align_bytes=64),
@@ -219,7 +219,7 @@ def tile_list_band_sine_field_kernel(
             nc.gpsimd.tensor_tensor(
                 h_cols(c, 0, SHARE).rearrange("p (j t) -> p j t", t=PACK),
                 sn[c, 0][:, :, 0:SHARE].rearrange("p t j -> p j t"),
-                coef[:, 1:2, :].to_broadcast([P, SHARE, PACK]),
+                coef[:, 2:3, :].to_broadcast([P, SHARE, PACK]),
                 ALU.mult,
             )
             vector_product(c, 0, SHARE)

@@ -31,8 +31,8 @@ CHUNKS = S2 // W
 HALF = W // 2
 COEF = 4
 SHARE = 104
-WM_ON_SCALAR = 64
-Y_ON_SCALAR = 96
+LAP = 64
+Y_ON_SCALAR = 192
 
 
 def tile_list_band_sine_field_kernel(
@@ -44,20 +44,21 @@ def tile_list_band_sine_field_kernel(
         lists = ctx.enter_context(tc.tile_pool(name="lists", bufs=1))
         keep = ctx.enter_context(tc.tile_pool(name="keep", bufs=1))
         laid = ctx.enter_context(tc.tile_pool(name="laid", bufs=1))
+        reused = ctx.enter_context(tc.tile_pool(name="reused", bufs=1))
         held = ctx.enter_context(tc.tile_pool(name="held", bufs=1))
         psum = ctx.enter_context(tc.psum_pool(name="psum", bufs=1))
-        bank_count = {"a": 4, "y": 3}
 
         idx = lists.tile([P, S // 16], U16, name="idx")
         idx2 = lists.tile([P, S2 // 16], U16, name="idx2")
         s_win = keep.tile([P, T], U8, name="s_win", align_bytes=64)
         s2_win = keep.tile([P, T2], U8, name="s2_win", align_bytes=64)
         s4_raw = keep.tile([P, N], U8, name="s4_raw", align_bytes=64)
-        for win in (s_win, s2_win, s4_raw):
+        for win in (s_win, s2_win):
             nc.vector.memset(win[0:LOW, :].bitcast(I32), 0)
+        nc.gpsimd.memset(s4_raw[0:LOW, :].bitcast(I32), 0)
 
-        v_win = keep.tile([P, T], I32, name="v_win", tag="v_win", align_bytes=64)
-        v2_win = keep.tile([P, T2], I32, name="v2_win", tag="v2_win", align_bytes=64)
+        v_win = keep.tile([P, T], I32, name="v_win", align_bytes=64)
+        v2_win = keep.tile([P, T2], I32, name="v2_win", align_bytes=64)
         coef_rows = keep.tile([COEF, PASS], F32, name="coef_rows")
         ident = keep.tile([P, P], F32, name="ident")
         make_identity(nc, ident[:])
@@ -72,13 +73,13 @@ def tile_list_band_sine_field_kernel(
         nc.sync.dma_start(v_win[:], tab_words[0].rearrange("p c t -> p (c t)").bitcast(I32))
         nc.sync.dma_start(coef_rows[0:2, :], phase.rearrange("(b e) -> b e", b=2))
         nc.sync.dma_start(coef_rows[2:COEF, :], amp.rearrange("(b e) -> b e", b=2))
+        nc.sync.dma_start(bi[:], bias.rearrange("(p t) -> p t", t=PACK))
         nc.sync.dma_start(v2_win[:], tab2_words[0].rearrange("p c t -> p (c t)").bitcast(I32))
         nc.sync.dma_start(w4_raw[:], w4_words[0].bitcast(I32))
-        nc.sync.dma_start(bi[:], bias.rearrange("(p t) -> p t", t=PACK))
 
         s_picked = keep.tile([P, S], U8, name="s_picked", align_bytes=64)
         s2_first = keep.tile([P, BANK], U8, name="s2_first", tag="s2_first", align_bytes=64)
-        s2_second = keep.tile([P, BANK], U8, name="s2_second", tag="s2_second", align_bytes=64)
+        s2_second = reused.tile([P, BANK], U8, name="s2_second", offset=0, align_bytes=64)
         early = keep.tile([P, S + BANK], U8, name="early", align_bytes=64)
         late = keep.tile([P, BANK + N], U8, name="late", align_bytes=64)
 
@@ -91,28 +92,27 @@ def tile_list_band_sine_field_kernel(
 
         wm_rows = wm.rearrange("(b a u r) n -> b u a r n", b=2, u=PACK, r=RUN)
 
-        def load_wm(b, tag):
-            raw = keep.tile([P, PACK, N], F32, name="wm_raw%d" % b, tag=tag, align_bytes=64)
+        def load_wm(b, raw):
             for u in range(PACK):
                 nc.sync.dma_start(raw[:, u, :], wm_rows[b, u])
             return raw
 
+        nc.gpsimd.tensor_copy(
+            late[:, BANK:].rearrange("p (t m) -> p t m", t=PACK), s4_raw[:].rearrange("p (m t) -> p t m", t=PACK)
+        )
         nc.vector.tensor_copy(s_picked[:], s_win[:].indirect(idx[:]))
         nc.vector.tensor_copy(s2_first[:], s2_win[:].indirect(idx2[:, 0 : BANK // 16]))
         nc.vector.tensor_copy(
             early[:, 0:S].bitcast(I32).rearrange("p (b t a) -> p b t a", b=2, t=PACK),
             s_picked[:].bitcast(I32).rearrange("p (b a t) -> p b t a", b=2, t=PACK),
         )
-        nc.vector.tensor_copy(
-            late[:, BANK:].rearrange("p (t m) -> p t m", t=PACK), s4_raw[:].rearrange("p (m t) -> p t m", t=PACK)
-        )
+        nc.vector.tensor_copy(s2_second[:], s2_win[:].indirect(idx2[:, BANK // 16 :]))
         nc.vector.tensor_copy(early[:, S:].bitcast(I32), s2_first[:].bitcast(I32))
         move_rows(early)
-        wm_raw = [load_wm(0, "s2_first")]
-        nc.vector.tensor_copy(s2_second[:], s2_win[:].indirect(idx2[:, BANK // 16 :]))
+        wm_raw = [load_wm(0, keep.tile([P, PACK, N], F32, name="wm_raw0", tag="s2_first", align_bytes=64))]
         nc.vector.tensor_copy(late[:, 0:BANK].bitcast(I32), s2_second[:].bitcast(I32))
+        wm_raw.append(load_wm(1, reused.tile([P, PACK, N], F32, name="wm_raw1", offset=0, align_bytes=64)))
         move_rows(late)
-        wm_raw.append(load_wm(1, "s2_second"))
         v2_sc = [early[:, S:], late[:, 0:BANK]]
         v_sc = early[:, 0:S]
         w4_sc = late[:, BANK:]
@@ -132,34 +132,44 @@ def tile_list_band_sine_field_kernel(
             nc.tensor.transpose(turned[:, P * t : P * (t + 1)], sorted_rows[:, P * t : P * (t + 1)], ident[:])
         by_row = turned[:].rearrange("p (t n) -> p n t", t=PACK)
         coef = keep.tile([P, COEF, PACK], F32, name="coef")
-        nc.scalar.copy(coef[:, 0:COEF:2, :], by_row[:, 0:COEF:2, :])
+        nc.scalar.copy(coef[:, 0:3, :], by_row[:, 0:3, :])
 
         v2_q = [
             keep.tile([P, BANK], U32, name="v2_q0", align_bytes=64),
             laid.tile([P, BANK], U32, name="v2_q1", offset=border, align_bytes=64),
         ]
-        below = 2 * PACK * N
-        room = below + 4 * 2 * W
-        last_phase = []
-        for c in range(CHUNKS):
-            tile = held.tile([P, 32], F32, name="phase%d" % c, offset=room * c + below - 64, align_bytes=64)
-            nc.scalar.copy(tile[:, 0:PACK], by_row[:, 1, :])
-            last_phase.append(tile)
+        codes = 4 * 2 * W
+        meet = {1: codes, 2: 2 * codes + 64, 3: 5 * codes}
+        own_phase = {}
+        for n, (c, b) in enumerate(((1, 1), (2, 1), (3, 1))):
+            tile = held.tile([P, 32], F32, name="phase%d%d" % (c, b), offset=meet[n + 1] - 64, align_bytes=64)
+            nc.scalar.copy(tile[:, 0:PACK], by_row[:, b, :])
+            own_phase[c, b] = tile
         h_q = {}
         h_sc = [keep.tile([P, 2 * W], U8, name="h_sc%d" % c, align_bytes=64) for c in range(CHUNKS)]
         wm_sc = [keep.tile([P, N], U8, name="wm_sc%d" % b, align_bytes=64) for b in range(2)]
-        wm_bf = []
-        y_q = keep.tile([P, S2], U32, name="y_q", align_bytes=64)
         y_sc = keep.tile([P, S2], U8, name="y_sc", align_bytes=64)
+
+        span = PACK * 2 * W
+        part = PACK * W
+        first = keep.tile([P, span], BF16, name="h_bf0", align_bytes=64)
+        shared = keep.tile([P, 3 * part], BF16, name="shared", align_bytes=64)
+        h_bf = {0: first[:], (0, 0): first[:, 0:part], (0, 1): first[:, part:], (1, 0): shared[:, 0:part]}
+        h_bf[1, 1] = keep.tile([P, part], BF16, name="h_bf11", align_bytes=64)[:]
+        h_bf[2, 0] = shared[:, part - LAP : 2 * part - LAP]
+        h_bf[2, 1] = shared[:, 2 * part - LAP : 3 * part - LAP]
+        wm_bf = [keep.tile([P, PACK * N], BF16, name="wm_bf0", align_bytes=64)[:], shared[:, part:]]
+        y_bf = {c: keep.tile([P, PACK * W], BF16, name="y_bf%d" % c, align_bytes=64)[:] for c in range(1, CHUNKS)}
+        y_bf[0] = h_bf[2, 1]
 
         def cols(pair, j0, w):
             return pair[j0 // BANK][:, j0 % BANK : j0 % BANK + w]
 
         def gather_v(b, dealt):
-            span = PASS // 16
+            run = PASS // 16
             nc.vector.tensor_copy(
                 dealt[:].rearrange("p (t a r) -> p a t r", t=PACK, r=RUN),
-                v_win[:].bitcast(U32).indirect(idx[:, span * b : span * (b + 1)]),
+                v_win[:].bitcast(U32).indirect(idx[:, run * b : run * (b + 1)]),
             )
             return dealt
 
@@ -168,20 +178,23 @@ def tile_list_band_sine_field_kernel(
                 cols(v2_q, j0, w), v2_win[:].bitcast(U32).indirect(idx2[:, j0 // 16 : (j0 + w) // 16])
             )
 
-        def round_wm(b, m0, m1, copy):
+        def gpsimd_round(out, in_):
+            nc.gpsimd.tensor_scalar(out, in_, 1.0, 0.0, ALU.mult, ALU.add)
+
+        def round_wm(b, t0, t1, walk, copy):
             copy(
-                wm_bf[b][:].rearrange("p (t m u) -> p m u t", t=PACK, u=PACK)[:, m0:m1],
-                wm_raw[b][:].rearrange("p u (m t) -> p m u t", t=PACK)[:, m0:m1],
+                wm_bf[b][:, PASS * t0 : PASS * t1].rearrange("p (t m u) -> " + walk, t=t1 - t0, u=PACK),
+                wm_raw[b][:].rearrange("p u (m t) -> p u m t", t=PACK)[:, :, :, t0:t1].rearrange("p u m t -> " + walk),
             )
 
-        def quantise_wm(b, codes):
-            nc.vector.quantize_mx(out=codes[:].bitcast(FP8X4), scales=wm_sc[b][:], in_=wm_bf[b][:])
-            return codes
+        def quantise_wm(b, tile):
+            nc.vector.quantize_mx(out=tile[:].bitcast(FP8X4), scales=wm_sc[b][:], in_=wm_bf[b])
+            return tile
 
-        def psum_slices(tag, w, per=None):
-            per = per or BANK // w
-            banks = [psum.tile([P, BANK], F32, name=tag, tag=tag, bufs=bank_count[tag]) for bank in range(PACK // per)]
-            return [banks[t // per][:, (t % per) * w : (t % per + 1) * w] for t in range(PACK)]
+        def psum_slices(banks, w):
+            per = PACK // len(banks)
+            tiles = [psum.tile([P, BANK], F32, name="bank%d" % k, tag="bank%d" % k) for k in banks]
+            return [tiles[t // per][:, (t % per) * w : (t % per + 1) * w] for t in range(PACK)]
 
         def woven(tile):
             return tile.rearrange("p (c e t) -> p c t e", e=2, t=PACK)
@@ -189,9 +202,9 @@ def tile_list_band_sine_field_kernel(
         def by_pairs(tile):
             return tile.rearrange("p t (c e) -> p c t e", e=2)
 
-        def sines(c, b, banks="a", per=None):
+        def sines(c, b, banks):
             sn[c, b] = keep.tile([P, PACK, W], F32, name="sn%d%d" % (c, b), align_bytes=64)[:]
-            acc = psum_slices(banks, W, per)
+            acc = psum_slices(banks, W)
             for t in range(PACK):
                 nc.tensor.matmul_mx(
                     out=acc[t],
@@ -202,59 +215,56 @@ def tile_list_band_sine_field_kernel(
                     start=True,
                     stop=True,
                 )
-            phase_t = last_phase[c] if b else coef[:, 0]
+            phase_t = own_phase.get((c, b), coef[:, b])
             for t in range(PACK):
                 nc.scalar.activation(out=sn[c, b][:, t, :], in_=acc[t], func=ACT.Sin, bias=phase_t[:, t : t + 1])
 
         def h_cols(c, w0, w1):
-            first = (2 * W - SHARE) * c
-            return h_bf[:, PACK * (first + w0) : PACK * (first + w1)]
+            if w1 - w0 == 2 * W:
+                return h_bf[c]
+            return h_bf[c, w0 // W][:, PACK * (w0 % W) : PACK * (w0 % W + w1 - w0)]
 
-        def vector_product(c, b, c0):
-            amp_t = by_row[:, 2 + b, :].unsqueeze(1).unsqueeze(3).to_broadcast([P, (W - c0) // 2, PACK, 2])
-            out = woven(h_cols(c, W * b + c0, W * (b + 1)))
-            nc.vector.tensor_tensor(out, by_pairs(sn[c, b][:, :, c0:W]), amp_t, ALU.mult)
+        def vector_product(c, b, c0, c1=W):
+            amp_t = by_row[:, 2 + b, :].unsqueeze(1).unsqueeze(3).to_broadcast([P, (c1 - c0) // 2, PACK, 2])
+            out = woven(h_cols(c, W * b + c0, W * b + c1))
+            nc.vector.tensor_tensor(out, by_pairs(sn[c, b][:, :, c0:c1]), amp_t, ALU.mult)
 
-        def products(c):
+        def gpsimd_product(c):
             nc.gpsimd.tensor_tensor(
                 h_cols(c, 0, SHARE).rearrange("p (j t) -> p j t", t=PACK),
                 sn[c, 0][:, :, 0:SHARE].rearrange("p t j -> p j t"),
                 coef[:, 2:3, :].to_broadcast([P, SHARE, PACK]),
                 ALU.mult,
             )
-            vector_product(c, 0, SHARE)
-            vector_product(c, 1, 0)
-            h_q[c] = held.tile([P, 2 * W], U32, name="h_q%d" % c, offset=room * c + below, align_bytes=64)
 
         def quantise_h(c, w0, w1):
             nc.vector.quantize_mx(out=h_q[c][:, w0:w1].bitcast(FP8X4), scales=h_sc[c][:, w0:w1], in_=h_cols(c, w0, w1))
 
-        def mix(j0, w, banks="y"):
+        def mix(j0, w, banks, skip_first):
             acc = psum_slices(banks, w)
             per = BANK // w
             c = j0 // W
-            for t in range(PACK):
-                nc.tensor.matmul_mx(
-                    out=acc[t],
-                    lhsT=w4_q[:, 2 * P * t : 2 * P * (t + 1)].bitcast(FP4X4),
-                    lhsT_scale=w4_sc[:, P * t : P * (t + 1)],
-                    rhs=cols(v2_q, j0, w).bitcast(FP8X4),
-                    rhs_scale=cols(v2_sc, j0, w),
-                    start=(t % per == 0),
-                    stop=False,
-                )
+            skip = (w4_q[:].bitcast(U16), FP4X4, w4_sc, cols(v2_q, j0, w), cols(v2_sc, j0, w))
+            terms = []
             for b in range(2):
                 w0 = W * b + j0 % W
+                terms.append((wm_q[b][:], FP8X4, wm_sc[b][:], h_q[c][:, w0 : w0 + w], h_sc[c][:, w0 : w0 + w]))
+            terms.insert(0 if skip_first else 1, skip)
+            for n, (words, fmt, scales, moving, moving_scales) in enumerate(terms):
                 for t in range(PACK):
                     nc.tensor.matmul_mx(
                         out=acc[t],
-                        lhsT=wm_q[b][:, P * t : P * (t + 1)].bitcast(FP8X4),
-                        lhsT_scale=wm_sc[b][:, P * t : P * (t + 1)],
-                        rhs=h_q[c][:, w0 : w0 + w].bitcast(FP8X4),
-                        rhs_scale=h_sc[c][:, w0 : w0 + w],
-                        start=False,
-                        stop=(b == 1 and t % per == per - 1),
+                        lhsT=words[:, P * t : P * (t + 1)].bitcast(fmt),
+                        lhsT_scale=scales[:, P * t : P * (t + 1)],
+                        rhs=moving.bitcast(FP8X4),
+                        rhs_scale=moving_scales,
+                        start=(n == 0 and t % per == 0),
+                        stop=(n == len(terms) - 1 and t % per == per - 1),
                     )
+            return acc
+
+        def add_bias(acc, j0, w):
+            per = BANK // w
             rows = keep.tile([P, PACK, w], F32, name="y%d" % j0, align_bytes=64)
             out_rows = out_0.rearrange("(p t) j -> p t j", t=PACK)
             for t in range(PACK):
@@ -280,58 +290,65 @@ def tile_list_band_sine_field_kernel(
 
         v_q = [gather_v(0, keep.tile([P, PASS], U32, name="v_q0", align_bytes=64))]
         gather_v2(0, W)
-        gather_v2(W, W)
         w4_q = keep.tile([P, 2 * N], U8, name="w4_q", align_bytes=64)
         nc.scalar.copy(
             w4_q[:].bitcast(U16).rearrange("p (t m) -> p t m", t=PACK),
             w4_raw[:].bitcast(U16).rearrange("p (m t) -> p t m", t=PACK),
         )
         v_q.append(gather_v(1, laid.tile([P, PASS], U32, name="v_q1", offset=0, align_bytes=64)))
+        gather_v2(W, W)
         gather_v2(BANK, BANK)
 
-        y_bf = [keep.tile([P, PACK * W], BF16, name="y_bf%d" % c, align_bytes=64)[:] for c in range(CHUNKS)]
         sn = {}
-        y = {}
+        sines(0, 0, [0, 1, 2, 3])
+        sines(0, 1, [4, 5])
+        sines(1, 0, [0, 1])
+        sines(1, 1, [2, 3])
+        round_wm(0, 0, 2, "p m t u", gpsimd_round)
+        round_wm(0, 2, PACK, "p m u t", nc.scalar.copy)
+        round_wm(1, 0, PACK, "p m t u", gpsimd_round)
+        sines(2, 0, [0, 1])
+        sines(2, 1, [2, 3])
+        sines(3, 0, [0, 1])
 
-        sines(0, 0, per=1)
-        wm_bf.append(keep.tile([P, PACK * N], BF16, name="wm_bf0", align_bytes=64))
-        round_wm(0, 0, P, nc.vector.tensor_copy)
-        sines(0, 1, banks="y")
-        h_width = 2 * W * CHUNKS - SHARE * (CHUNKS - 1)
-        h_bf = keep.tile([P, PACK * h_width], BF16, name="h_bf", tag="s2_first", align_bytes=64)
-        sines(1, 0)
-        sines(1, 1)
-        wm_bf.append(held.tile([P, PACK * N], BF16, name="wm_bf1", offset=room, align_bytes=64))
-        round_wm(1, 0, WM_ON_SCALAR, nc.scalar.copy)
-        for c in range(2, CHUNKS):
-            sines(c, 0)
-            sines(c, 1)
-
-        wm_q = []
-        products(0)
-        wm_q.append(quantise_wm(0, held.tile([P, N], U32, name="wm_q0", offset=below - 4 * N, align_bytes=64)))
+        for c in range(2):
+            vector_product(c, 0, 0)
+            vector_product(c, 1, 0)
+        h_q[0] = held.tile([P, 2 * W], U32, name="h_q0", offset=meet[1], align_bytes=64)
+        h_q[1] = reused.tile([P, 2 * W], U32, name="h_q1", offset=0, align_bytes=64)
         quantise_h(0, 0, 2 * W)
-        products(1)
-        round_wm(1, WM_ON_SCALAR, P, nc.vector.tensor_copy)
-        quantise_h(1, 0, W)
+        wm_q = [quantise_wm(0, held.tile([P, N], U32, name="wm_q0", offset=meet[1] - codes, align_bytes=64))]
         wm_q.append(quantise_wm(1, keep.tile([P, N], U32, name="wm_q1", align_bytes=64)))
+        quantise_h(1, 0, W)
+        y = [add_bias(mix(0, W, [6, 4], True), 0, W)]
+        sines(3, 1, [5, 6])
+        for b in range(2):
+            h_bf[3, b] = reused.tile([P, part], BF16, name="h_bf3%d" % b, offset=codes * (b + 1), align_bytes=64)[:]
+        gpsimd_product(2)
+        vector_product(2, 0, SHARE)
+        vector_product(2, 1, 0)
         quantise_h(1, W, 2 * W)
-        y[0] = mix(0, W)
-        products(2)
+        acc1 = mix(W, W, [2, 3], False)
+        h_q[2] = held.tile([P, 2 * W], U32, name="h_q2", offset=2 * codes, align_bytes=64)
         quantise_h(2, 0, W)
         quantise_h(2, W, 2 * W)
-        y[1] = mix(W, W)
-        round_y(y[0], y_bf[0], 0, W, nc.scalar.copy)
+        y.append(add_bias(acc1, W, W))
         round_y(y[1], y_bf[1], 0, Y_ON_SCALAR, nc.scalar.copy)
-        products(3)
+
+        gpsimd_round(y_bf[0].rearrange("p (j t) -> p j t", t=PACK), y[0][:].rearrange("p t j -> p j t"))
+        vector_product(3, 0, 0)
+        vector_product(3, 1, 0, HALF)
+        h_q[3] = held.tile([P, 2 * W], U32, name="h_q3", offset=meet[3], align_bytes=64)
+        y_q = held.tile([P, S2], U32, name="y_q", offset=meet[3] - 4 * S2, align_bytes=64)
         quantise_h(3, 0, W)
         quantise_h(3, W, W + HALF)
-        quantise_h(3, W + HALF, 2 * W)
-
-        y[2] = mix(2 * W, W, banks="a")
-        last = [mix(3 * W, HALF, banks="a"), mix(3 * W + HALF, HALF, banks="a")]
+        vector_product(3, 1, HALF)
         quantise_y(0, W)
         store_codes(0, W)
+        quantise_h(3, W + HALF, 2 * W)
+
+        y.append(add_bias(mix(2 * W, W, [0, 1], False), 2 * W, W))
+        last = [add_bias(mix(3 * W, HALF, [4], True), 3 * W, HALF), add_bias(mix(3 * W + HALF, HALF, [5], True), 3 * W + HALF, HALF)]
         round_y(y[1], y_bf[1], Y_ON_SCALAR, W, nc.vector.tensor_copy)
         round_y(y[2], y_bf[2], 0, W, nc.vector.tensor_copy)
         quantise_y(W, W)

@@ -31,8 +31,9 @@ CHUNKS = S2 // W
 HALF = W // 2
 COEF = 4
 SHARE = 104
-LAP = 64
-Y_ON_SCALAR = 192
+SKIP = 2
+Y_ON_GPSIMD = 192
+Y_ON_SCALAR = 128
 
 
 def tile_list_band_sine_field_kernel(
@@ -44,7 +45,6 @@ def tile_list_band_sine_field_kernel(
         lists = ctx.enter_context(tc.tile_pool(name="lists", bufs=1))
         keep = ctx.enter_context(tc.tile_pool(name="keep", bufs=1))
         laid = ctx.enter_context(tc.tile_pool(name="laid", bufs=1))
-        reused = ctx.enter_context(tc.tile_pool(name="reused", bufs=1))
         held = ctx.enter_context(tc.tile_pool(name="held", bufs=1))
         psum = ctx.enter_context(tc.psum_pool(name="psum", bufs=1))
 
@@ -53,9 +53,8 @@ def tile_list_band_sine_field_kernel(
         s_win = keep.tile([P, T], U8, name="s_win", align_bytes=64)
         s2_win = keep.tile([P, T2], U8, name="s2_win", align_bytes=64)
         s4_raw = keep.tile([P, N], U8, name="s4_raw", align_bytes=64)
-        for win in (s_win, s2_win):
+        for win in (s_win, s2_win, s4_raw):
             nc.vector.memset(win[0:LOW, :].bitcast(I32), 0)
-        nc.gpsimd.memset(s4_raw[0:LOW, :].bitcast(I32), 0)
 
         v_win = keep.tile([P, T], I32, name="v_win", align_bytes=64)
         v2_win = keep.tile([P, T2], I32, name="v2_win", align_bytes=64)
@@ -79,7 +78,7 @@ def tile_list_band_sine_field_kernel(
 
         s_picked = keep.tile([P, S], U8, name="s_picked", align_bytes=64)
         s2_first = keep.tile([P, BANK], U8, name="s2_first", tag="s2_first", align_bytes=64)
-        s2_second = reused.tile([P, BANK], U8, name="s2_second", offset=0, align_bytes=64)
+        s2_second = keep.tile([P, BANK], U8, name="s2_second", tag="s2_second", align_bytes=64)
         early = keep.tile([P, S + BANK], U8, name="early", align_bytes=64)
         late = keep.tile([P, BANK + N], U8, name="late", align_bytes=64)
 
@@ -97,9 +96,6 @@ def tile_list_band_sine_field_kernel(
                 nc.sync.dma_start(raw[:, u, :], wm_rows[b, u])
             return raw
 
-        nc.gpsimd.tensor_copy(
-            late[:, BANK:].rearrange("p (t m) -> p t m", t=PACK), s4_raw[:].rearrange("p (m t) -> p t m", t=PACK)
-        )
         nc.vector.tensor_copy(s_picked[:], s_win[:].indirect(idx[:]))
         nc.vector.tensor_copy(s2_first[:], s2_win[:].indirect(idx2[:, 0 : BANK // 16]))
         nc.vector.tensor_copy(
@@ -109,9 +105,12 @@ def tile_list_band_sine_field_kernel(
         nc.vector.tensor_copy(s2_second[:], s2_win[:].indirect(idx2[:, BANK // 16 :]))
         nc.vector.tensor_copy(early[:, S:].bitcast(I32), s2_first[:].bitcast(I32))
         move_rows(early)
+        nc.vector.tensor_copy(
+            late[:, BANK:].rearrange("p (t m) -> p t m", t=PACK), s4_raw[:].rearrange("p (m t) -> p t m", t=PACK)
+        )
         wm_raw = [load_wm(0, keep.tile([P, PACK, N], F32, name="wm_raw0", tag="s2_first", align_bytes=64))]
         nc.vector.tensor_copy(late[:, 0:BANK].bitcast(I32), s2_second[:].bitcast(I32))
-        wm_raw.append(load_wm(1, reused.tile([P, PACK, N], F32, name="wm_raw1", offset=0, align_bytes=64)))
+        wm_raw.append(load_wm(1, keep.tile([P, PACK, N], F32, name="wm_raw1", tag="s2_second", align_bytes=64)))
         move_rows(late)
         v2_sc = [early[:, S:], late[:, 0:BANK]]
         v_sc = early[:, 0:S]
@@ -139,7 +138,7 @@ def tile_list_band_sine_field_kernel(
             laid.tile([P, BANK], U32, name="v2_q1", offset=border, align_bytes=64),
         ]
         codes = 4 * 2 * W
-        meet = {1: codes, 2: 2 * codes + 64, 3: 5 * codes}
+        meet = {1: codes, 2: 3 * codes + 64, 3: 6 * codes}
         own_phase = {}
         for n, (c, b) in enumerate(((1, 1), (2, 1), (3, 1))):
             tile = held.tile([P, 32], F32, name="phase%d%d" % (c, b), offset=meet[n + 1] - 64, align_bytes=64)
@@ -153,12 +152,12 @@ def tile_list_band_sine_field_kernel(
         span = PACK * 2 * W
         part = PACK * W
         first = keep.tile([P, span], BF16, name="h_bf0", align_bytes=64)
-        shared = keep.tile([P, 3 * part], BF16, name="shared", align_bytes=64)
-        h_bf = {0: first[:], (0, 0): first[:, 0:part], (0, 1): first[:, part:], (1, 0): shared[:, 0:part]}
-        h_bf[1, 1] = keep.tile([P, part], BF16, name="h_bf11", align_bytes=64)[:]
-        h_bf[2, 0] = shared[:, part - LAP : 2 * part - LAP]
-        h_bf[2, 1] = shared[:, 2 * part - LAP : 3 * part - LAP]
-        wm_bf = [keep.tile([P, PACK * N], BF16, name="wm_bf0", align_bytes=64)[:], shared[:, part:]]
+        shared = keep.tile([P, span], BF16, name="shared", align_bytes=64)
+        h_bf = {0: first[:], (0, 0): first[:, 0:part], (0, 1): first[:, part:]}
+        for b in range(2):
+            h_bf[1, b] = keep.tile([P, part], BF16, name="h_bf1%d" % b, align_bytes=64)[:]
+            h_bf[2, b] = shared[:, part * b : part * (b + 1)]
+        wm_bf = [keep.tile([P, PACK * N], BF16, name="wm_bf0", align_bytes=64)[:], shared[:]]
         y_bf = {c: keep.tile([P, PACK * W], BF16, name="y_bf%d" % c, align_bytes=64)[:] for c in range(1, CHUNKS)}
         y_bf[0] = h_bf[2, 1]
 
@@ -202,8 +201,10 @@ def tile_list_band_sine_field_kernel(
         def by_pairs(tile):
             return tile.rearrange("p t (c e) -> p c t e", e=2)
 
-        def sines(c, b, banks):
-            sn[c, b] = keep.tile([P, PACK, W], F32, name="sn%d%d" % (c, b), align_bytes=64)[:]
+        def sines(c, b, banks, room=None):
+            if room is None:
+                room = keep.tile([P, PACK, W], F32, name="sn%d%d" % (c, b), align_bytes=64)[:]
+            sn[c, b] = room
             acc = psum_slices(banks, W)
             for t in range(PACK):
                 nc.tensor.matmul_mx(
@@ -240,7 +241,7 @@ def tile_list_band_sine_field_kernel(
         def quantise_h(c, w0, w1):
             nc.vector.quantize_mx(out=h_q[c][:, w0:w1].bitcast(FP8X4), scales=h_sc[c][:, w0:w1], in_=h_cols(c, w0, w1))
 
-        def mix(j0, w, banks, skip_first):
+        def mix(j0, w, banks, order):
             acc = psum_slices(banks, w)
             per = BANK // w
             c = j0 // W
@@ -249,8 +250,9 @@ def tile_list_band_sine_field_kernel(
             for b in range(2):
                 w0 = W * b + j0 % W
                 terms.append((wm_q[b][:], FP8X4, wm_sc[b][:], h_q[c][:, w0 : w0 + w], h_sc[c][:, w0 : w0 + w]))
-            terms.insert(0 if skip_first else 1, skip)
-            for n, (words, fmt, scales, moving, moving_scales) in enumerate(terms):
+            terms.append(skip)
+            for n, term in enumerate(order):
+                words, fmt, scales, moving, moving_scales = terms[term]
                 for t in range(PACK):
                     nc.tensor.matmul_mx(
                         out=acc[t],
@@ -304,38 +306,43 @@ def tile_list_band_sine_field_kernel(
         sines(0, 1, [4, 5])
         sines(1, 0, [0, 1])
         sines(1, 1, [2, 3])
-        round_wm(0, 0, 2, "p m t u", gpsimd_round)
-        round_wm(0, 2, PACK, "p m u t", nc.scalar.copy)
-        round_wm(1, 0, PACK, "p m t u", gpsimd_round)
+        round_wm(0, 0, PACK, "p m t u", gpsimd_round)
+        round_wm(1, 0, 2, "p m t u", gpsimd_round)
         sines(2, 0, [0, 1])
         sines(2, 1, [2, 3])
-        sines(3, 0, [0, 1])
+        round_wm(1, 2, PACK, "p m u t", nc.scalar.copy)
+        sines(3, 0, [0, 1], keep.tile([P, PACK, W], F32, name="sn30", tag="s2_second", align_bytes=64)[:])
 
         for c in range(2):
             vector_product(c, 0, 0)
             vector_product(c, 1, 0)
-        h_q[0] = held.tile([P, 2 * W], U32, name="h_q0", offset=meet[1], align_bytes=64)
-        h_q[1] = reused.tile([P, 2 * W], U32, name="h_q1", offset=0, align_bytes=64)
+        pair = held.tile([P, 4 * W], U32, name="h_q01", offset=meet[1], align_bytes=64)
+        h_q[0] = pair[:, 0 : 2 * W]
+        h_q[1] = pair[:, 2 * W :]
         quantise_h(0, 0, 2 * W)
         wm_q = [quantise_wm(0, held.tile([P, N], U32, name="wm_q0", offset=meet[1] - codes, align_bytes=64))]
+        quantise_h(1, W, 2 * W)
         wm_q.append(quantise_wm(1, keep.tile([P, N], U32, name="wm_q1", align_bytes=64)))
-        quantise_h(1, 0, W)
-        y = [add_bias(mix(0, W, [6, 4], True), 0, W)]
+        y = [add_bias(mix(0, W, [6, 4], (SKIP, 0, 1)), 0, W)]
         sines(3, 1, [5, 6])
         for b in range(2):
-            h_bf[3, b] = reused.tile([P, part], BF16, name="h_bf3%d" % b, offset=codes * (b + 1), align_bytes=64)[:]
+            h_bf[3, b] = keep.tile([P, part], BF16, name="h_bf3%d" % b, align_bytes=64)[:]
         gpsimd_product(2)
         vector_product(2, 0, SHARE)
         vector_product(2, 1, 0)
-        quantise_h(1, W, 2 * W)
-        acc1 = mix(W, W, [2, 3], False)
-        h_q[2] = held.tile([P, 2 * W], U32, name="h_q2", offset=2 * codes, align_bytes=64)
+        quantise_h(1, 0, W)
+        acc1 = mix(W, W, [2, 3], (1, SKIP, 0))
+        h_q[2] = held.tile([P, 2 * W], U32, name="h_q2", offset=3 * codes, align_bytes=64)
         quantise_h(2, 0, W)
         quantise_h(2, W, 2 * W)
         y.append(add_bias(acc1, W, W))
+        round_y(y[0], y_bf[0], Y_ON_GPSIMD, W, nc.scalar.copy)
         round_y(y[1], y_bf[1], 0, Y_ON_SCALAR, nc.scalar.copy)
 
-        gpsimd_round(y_bf[0].rearrange("p (j t) -> p j t", t=PACK), y[0][:].rearrange("p t j -> p j t"))
+        gpsimd_round(
+            y_bf[0][:, 0 : PACK * Y_ON_GPSIMD].rearrange("p (j t) -> p j t", t=PACK),
+            y[0][:, :, 0:Y_ON_GPSIMD].rearrange("p t j -> p j t"),
+        )
         vector_product(3, 0, 0)
         vector_product(3, 1, 0, HALF)
         h_q[3] = held.tile([P, 2 * W], U32, name="h_q3", offset=meet[3], align_bytes=64)
@@ -347,8 +354,8 @@ def tile_list_band_sine_field_kernel(
         store_codes(0, W)
         quantise_h(3, W + HALF, 2 * W)
 
-        y.append(add_bias(mix(2 * W, W, [0, 1], False), 2 * W, W))
-        last = [add_bias(mix(3 * W, HALF, [4], True), 3 * W, HALF), add_bias(mix(3 * W + HALF, HALF, [5], True), 3 * W + HALF, HALF)]
+        y.append(add_bias(mix(2 * W, W, [0, 1], (0, SKIP, 1)), 2 * W, W))
+        last = [add_bias(mix(3 * W, HALF, [4], (SKIP, 0, 1)), 3 * W, HALF), add_bias(mix(3 * W + HALF, HALF, [5], (SKIP, 0, 1)), 3 * W + HALF, HALF)]
         round_y(y[1], y_bf[1], Y_ON_SCALAR, W, nc.vector.tensor_copy)
         round_y(y[2], y_bf[2], 0, W, nc.vector.tensor_copy)
         quantise_y(W, W)

@@ -32,6 +32,7 @@ HALF = W // 2
 COEF = 4
 SHARE = 104
 SKIP = 2
+WARM = 6
 Y_ON_GPSIMD = 192
 Y_ON_SCALAR = 128
 
@@ -111,7 +112,6 @@ def tile_list_band_sine_field_kernel(
         wm_raw = [load_wm(0, keep.tile([P, PACK, N], F32, name="wm_raw0", tag="s2_first", align_bytes=64))]
         nc.vector.tensor_copy(late[:, 0:BANK].bitcast(I32), s2_second[:].bitcast(I32))
         wm_raw.append(load_wm(1, keep.tile([P, PACK, N], F32, name="wm_raw1", tag="s2_second", align_bytes=64)))
-        move_rows(late)
         v2_sc = [early[:, S:], late[:, 0:BANK]]
         v_sc = early[:, 0:S]
         w4_sc = late[:, BANK:]
@@ -128,8 +128,8 @@ def tile_list_band_sine_field_kernel(
         )
         turned = psum.tile([P, BANK], F32, name="turned")
         for t in range(PACK):
-            nc.tensor.transpose(turned[:, P * t : P * (t + 1)], sorted_rows[:, P * t : P * (t + 1)], ident[:])
-        by_row = turned[:].rearrange("p (t n) -> p n t", t=PACK)
+            nc.tensor.transpose(turned[:, COEF * t : COEF * t + P], sorted_rows[:, P * t : P * (t + 1)], ident[:])
+        by_row = turned[:, 0 : COEF * PACK].rearrange("p (t n) -> p n t", t=PACK)
         coef = keep.tile([P, COEF, PACK], F32, name="coef")
         nc.scalar.copy(coef[:, 0:3, :], by_row[:, 0:3, :])
 
@@ -144,6 +144,17 @@ def tile_list_band_sine_field_kernel(
             tile = held.tile([P, 32], F32, name="phase%d%d" % (c, b), offset=meet[n + 1] - 64, align_bytes=64)
             nc.scalar.copy(tile[:, 0:PACK], by_row[:, b, :])
             own_phase[c, b] = tile
+        for turn in range(WARM):
+            nc.tensor.matmul_mx(
+                out=turned[:, W:],
+                lhsT=v_win[:, 0:P].bitcast(FP8X4),
+                lhsT_scale=late[:, 0:P],
+                rhs=v_win[:, 0:W].bitcast(FP8X4),
+                rhs_scale=late[:, 0:W],
+                start=True,
+                stop=True,
+            )
+        move_rows(late)
         h_q = {}
         h_sc = [keep.tile([P, 2 * W], U8, name="h_sc%d" % c, align_bytes=64) for c in range(CHUNKS)]
         wm_sc = [keep.tile([P, N], U8, name="wm_sc%d" % b, align_bytes=64) for b in range(2)]

@@ -303,19 +303,19 @@ def tile_list_band_sine_field_kernel(
 
         v_q = [gather_v(0, keep.tile([P, PASS], U32, name="v_q0", align_bytes=64))]
         gather_v2(0, W)
+        gather_v2(W, W)
         w4_q = keep.tile([P, 2 * N], U8, name="w4_q", align_bytes=64)
         nc.scalar.copy(
             w4_q[:].bitcast(U16).rearrange("p (t m) -> p t m", t=PACK),
             w4_raw[:].bitcast(U16).rearrange("p (m t) -> p t m", t=PACK),
         )
         v_q.append(gather_v(1, laid.tile([P, PASS], U32, name="v_q1", offset=0, align_bytes=64)))
-        gather_v2(W, W)
         gather_v2(BANK, BANK)
 
         sn = {}
         sines(0, 0, [0, 1, 2, 3])
-        sines(0, 1, [4, 5])
-        sines(1, 0, [0, 1])
+        sines(1, 0, [4, 5])
+        sines(0, 1, [0, 1])
         sines(1, 1, [2, 3])
         round_wm(0, 0, PACK, "p m t u", gpsimd_round)
         round_wm(1, 0, 2, "p m t u", gpsimd_round)
@@ -324,9 +324,9 @@ def tile_list_band_sine_field_kernel(
         round_wm(1, 2, PACK, "p m u t", nc.scalar.copy)
         sines(3, 0, [0, 1], keep.tile([P, PACK, W], F32, name="sn30", tag="s2_second", align_bytes=64)[:])
 
-        for c in range(2):
-            vector_product(c, 0, 0)
-            vector_product(c, 1, 0)
+        for b in range(2):
+            vector_product(0, b, 0)
+            vector_product(1, b, 0)
         pair = held.tile([P, 4 * W], U32, name="h_q01", offset=meet[1], align_bytes=64)
         h_q[0] = pair[:, 0 : 2 * W]
         h_q[1] = pair[:, 2 * W :]

@@ -34,7 +34,7 @@ SHARE = 104
 SKIP = 2
 WARM = 6
 Y_ON_GPSIMD = 192
-Y_ON_SCALAR = 128
+Y_ON_SCALAR = 192
 
 
 def tile_list_band_sine_field_kernel(
@@ -323,6 +323,7 @@ def tile_list_band_sine_field_kernel(
         sines(2, 1, [2, 3])
         round_wm(1, 2, PACK, "p m u t", nc.scalar.copy)
         sines(3, 0, [0, 1], keep.tile([P, PACK, W], F32, name="sn30", tag="s2_second", align_bytes=64)[:])
+        sines(3, 1, [5, 2])
 
         for b in range(2):
             vector_product(0, b, 0)
@@ -335,19 +336,19 @@ def tile_list_band_sine_field_kernel(
         quantise_h(1, W, 2 * W)
         wm_q.append(quantise_wm(1, keep.tile([P, N], U32, name="wm_q1", align_bytes=64)))
         y = [add_bias(mix(0, W, [6, 4], (SKIP, 0, 1)), 0, W)]
-        sines(3, 1, [5, 6])
         for b in range(2):
             h_bf[3, b] = keep.tile([P, part], BF16, name="h_bf3%d" % b, align_bytes=64)[:]
         gpsimd_product(2)
         vector_product(2, 0, SHARE)
         vector_product(2, 1, 0)
         quantise_h(1, 0, W)
-        acc1 = mix(W, W, [2, 3], (1, SKIP, 0))
+        acc1 = mix(W, W, [0, 1], (1, SKIP, 0))
         h_q[2] = held.tile([P, 2 * W], U32, name="h_q2", offset=3 * codes, align_bytes=64)
         quantise_h(2, 0, W)
         quantise_h(2, W, 2 * W)
         y.append(add_bias(acc1, W, W))
         round_y(y[0], y_bf[0], Y_ON_GPSIMD, W, nc.scalar.copy)
+        y.append(add_bias(mix(2 * W, W, [3, 5], (SKIP, 0, 1)), 2 * W, W))
         round_y(y[1], y_bf[1], 0, Y_ON_SCALAR, nc.scalar.copy)
 
         gpsimd_round(
@@ -365,14 +366,13 @@ def tile_list_band_sine_field_kernel(
         store_codes(0, W)
         quantise_h(3, W + HALF, 2 * W)
 
-        y.append(add_bias(mix(2 * W, W, [0, 1], (0, SKIP, 1)), 2 * W, W))
-        last = [add_bias(mix(3 * W, HALF, [4], (SKIP, 0, 1)), 3 * W, HALF), add_bias(mix(3 * W + HALF, HALF, [5], (SKIP, 0, 1)), 3 * W + HALF, HALF)]
+        last = [add_bias(mix(3 * W, HALF, [4], (SKIP, 0, 1)), 3 * W, HALF), add_bias(mix(3 * W + HALF, HALF, [6], (SKIP, 0, 1)), 3 * W + HALF, HALF)]
         round_y(y[1], y_bf[1], Y_ON_SCALAR, W, nc.vector.tensor_copy)
         round_y(y[2], y_bf[2], 0, W, nc.vector.tensor_copy)
         quantise_y(W, W)
+        round_y(last[0], y_bf[3][:, 0 : PACK * HALF], 0, HALF, nc.vector.tensor_copy)
         quantise_y(2 * W, W)
         store_codes(W, 2 * W)
-        round_y(last[0], y_bf[3][:, 0 : PACK * HALF], 0, HALF, nc.vector.tensor_copy)
         round_y(last[1], y_bf[3][:, PACK * HALF :], 0, HALF, nc.vector.tensor_copy)
         quantise_y(3 * W, HALF)
         quantise_y(3 * W + HALF, HALF)

@@ -254,7 +254,7 @@ def tile_list_band_sine_field_kernel(
 
         def mix(j0, w, banks, order):
             acc = psum_slices(banks, w)
-            per = BANK // w
+            per = PACK // len(banks)
             c = j0 // W
             skip = (w4_q[:].bitcast(U16), FP4X4, w4_sc, cols(v2_q, j0, w), cols(v2_sc, j0, w))
             terms = []
@@ -363,16 +363,15 @@ def tile_list_band_sine_field_kernel(
         quantise_h(3, W, W + HALF)
         vector_product(3, 1, HALF)
         quantise_y(0, W)
-        store_codes(0, W)
         quantise_h(3, W + HALF, 2 * W)
 
-        last = [add_bias(mix(3 * W, HALF, [4], (SKIP, 0, 1)), 3 * W, HALF), add_bias(mix(3 * W + HALF, HALF, [6], (SKIP, 0, 1)), 3 * W + HALF, HALF)]
+        last = [add_bias(mix(3 * W, HALF, [4], (SKIP, 0, 1)), 3 * W, HALF), add_bias(mix(3 * W + HALF, HALF, [6, 0, 1, 2], (SKIP, 0, 1)), 3 * W + HALF, HALF)]
         round_y(y[1], y_bf[1], Y_ON_SCALAR, W, nc.vector.tensor_copy)
         round_y(y[2], y_bf[2], 0, W, nc.vector.tensor_copy)
         quantise_y(W, W)
-        round_y(last[0], y_bf[3][:, 0 : PACK * HALF], 0, HALF, nc.vector.tensor_copy)
         quantise_y(2 * W, W)
-        store_codes(W, 2 * W)
+        store_codes(0, 3 * W)
+        round_y(last[0], y_bf[3][:, 0 : PACK * HALF], 0, HALF, nc.vector.tensor_copy)
         round_y(last[1], y_bf[3][:, PACK * HALF :], 0, HALF, nc.vector.tensor_copy)
         quantise_y(3 * W, HALF)
         quantise_y(3 * W + HALF, HALF)

@@ -33,7 +33,8 @@ COEF = 4
 SHARE = 104
 SKIP = 2
 WARM = 6
-Y_ON_GPSIMD = 192
+LAST_SHARE = 72
+LAP = 64
 Y_ON_SCALAR = 192
 
 
@@ -163,14 +164,14 @@ def tile_list_band_sine_field_kernel(
         span = PACK * 2 * W
         part = PACK * W
         first = keep.tile([P, span], BF16, name="h_bf0", align_bytes=64)
-        shared = keep.tile([P, span], BF16, name="shared", align_bytes=64)
+        shared = keep.tile([P, span + part], BF16, name="shared", align_bytes=64)
         h_bf = {0: first[:], (0, 0): first[:, 0:part], (0, 1): first[:, part:]}
         for b in range(2):
             h_bf[1, b] = keep.tile([P, part], BF16, name="h_bf1%d" % b, align_bytes=64)[:]
             h_bf[2, b] = shared[:, part * b : part * (b + 1)]
-        wm_bf = [keep.tile([P, PACK * N], BF16, name="wm_bf0", align_bytes=64)[:], shared[:]]
-        y_bf = {c: keep.tile([P, PACK * W], BF16, name="y_bf%d" % c, align_bytes=64)[:] for c in range(1, CHUNKS)}
-        y_bf[0] = h_bf[2, 1]
+        wm_bf = [keep.tile([P, PACK * N], BF16, name="wm_bf0", align_bytes=64)[:], shared[:, 0:span]]
+        y_bf = {c: keep.tile([P, PACK * W], BF16, name="y_bf%d" % c, align_bytes=64)[:] for c in range(CHUNKS)}
+        h_bf[3, 0] = shared[:, span - LAP : span + part - LAP]
 
         def cols(pair, j0, w):
             return pair[j0 // BANK][:, j0 % BANK : j0 % BANK + w]
@@ -241,11 +242,11 @@ def tile_list_band_sine_field_kernel(
             out = woven(h_cols(c, W * b + c0, W * b + c1))
             nc.vector.tensor_tensor(out, by_pairs(sn[c, b][:, :, c0:c1]), amp_t, ALU.mult)
 
-        def gpsimd_product(c):
+        def gpsimd_product(c, share):
             nc.gpsimd.tensor_tensor(
-                h_cols(c, 0, SHARE).rearrange("p (j t) -> p j t", t=PACK),
-                sn[c, 0][:, :, 0:SHARE].rearrange("p t j -> p j t"),
-                coef[:, 2:3, :].to_broadcast([P, SHARE, PACK]),
+                h_cols(c, 0, share).rearrange("p (j t) -> p j t", t=PACK),
+                sn[c, 0][:, :, 0:share].rearrange("p t j -> p j t"),
+                coef[:, 2:3, :].to_broadcast([P, share, PACK]),
                 ALU.mult,
             )
 
@@ -336,9 +337,8 @@ def tile_list_band_sine_field_kernel(
         quantise_h(1, W, 2 * W)
         wm_q.append(quantise_wm(1, keep.tile([P, N], U32, name="wm_q1", align_bytes=64)))
         y = [add_bias(mix(0, W, [6, 4], (SKIP, 0, 1)), 0, W)]
-        for b in range(2):
-            h_bf[3, b] = keep.tile([P, part], BF16, name="h_bf3%d" % b, align_bytes=64)[:]
-        gpsimd_product(2)
+        h_bf[3, 1] = keep.tile([P, part], BF16, name="h_bf31", align_bytes=64)[:]
+        gpsimd_product(2, SHARE)
         vector_product(2, 0, SHARE)
         vector_product(2, 1, 0)
         quantise_h(1, 0, W)
@@ -347,35 +347,32 @@ def tile_list_band_sine_field_kernel(
         quantise_h(2, 0, W)
         quantise_h(2, W, 2 * W)
         y.append(add_bias(acc1, W, W))
-        round_y(y[0], y_bf[0], Y_ON_GPSIMD, W, nc.scalar.copy)
+        round_y(y[0], y_bf[0], 0, Y_ON_SCALAR, nc.scalar.copy)
         y.append(add_bias(mix(2 * W, W, [3, 5], (SKIP, 0, 1)), 2 * W, W))
-        round_y(y[1], y_bf[1], 0, Y_ON_SCALAR, nc.scalar.copy)
 
-        gpsimd_round(
-            y_bf[0][:, 0 : PACK * Y_ON_GPSIMD].rearrange("p (j t) -> p j t", t=PACK),
-            y[0][:, :, 0:Y_ON_GPSIMD].rearrange("p t j -> p j t"),
-        )
-        vector_product(3, 0, 0)
+        gpsimd_product(3, LAST_SHARE)
+        vector_product(3, 0, LAST_SHARE)
         vector_product(3, 1, 0, HALF)
         h_q[3] = held.tile([P, 2 * W], U32, name="h_q3", offset=meet[3], align_bytes=64)
         y_q = held.tile([P, S2], U32, name="y_q", offset=meet[3] - 4 * S2, align_bytes=64)
         quantise_h(3, 0, W)
         quantise_h(3, W, W + HALF)
         vector_product(3, 1, HALF)
-        quantise_y(0, W)
+        round_y(y[0], y_bf[0], Y_ON_SCALAR, W, nc.vector.tensor_copy)
         quantise_h(3, W + HALF, 2 * W)
 
         last = [add_bias(mix(3 * W, HALF, [4], (SKIP, 0, 1)), 3 * W, HALF), add_bias(mix(3 * W + HALF, HALF, [6, 0, 1, 2], (SKIP, 0, 1)), 3 * W + HALF, HALF)]
-        round_y(y[1], y_bf[1], Y_ON_SCALAR, W, nc.vector.tensor_copy)
+        round_y(y[1], y_bf[1], 0, W, nc.vector.tensor_copy)
+        quantise_y(0, W)
         round_y(y[2], y_bf[2], 0, W, nc.vector.tensor_copy)
         quantise_y(W, W)
-        quantise_y(2 * W, W)
-        store_codes(0, 3 * W)
+        store_codes(0, 2 * W)
         round_y(last[0], y_bf[3][:, 0 : PACK * HALF], 0, HALF, nc.vector.tensor_copy)
-        round_y(last[1], y_bf[3][:, PACK * HALF :], 0, HALF, nc.vector.tensor_copy)
+        quantise_y(2 * W, W)
+        round_y(last[1], y_bf[3][:, PACK * HALF :], 0, HALF, nc.scalar.copy)
         quantise_y(3 * W, HALF)
         quantise_y(3 * W + HALF, HALF)
-        store_codes(3 * W, W)
+        store_codes(2 * W, 2 * W)
         for quad in range(P // QUAD):
             queue = nc.scalar if quad % 2 else nc.sync
             queue.dma_start(

@@ -32,7 +32,6 @@ HALF = W // 2
 COEF = 4
 SHARE = 104
 SKIP = 2
-WARM = 6
 LAST_SHARE = 72
 LAP = 64
 Y_ON_SCALAR = 192
@@ -145,16 +144,6 @@ def tile_list_band_sine_field_kernel(
             tile = held.tile([P, 32], F32, name="phase%d%d" % (c, b), offset=meet[n + 1] - 64, align_bytes=64)
             nc.scalar.copy(tile[:, 0:PACK], by_row[:, b, :])
             own_phase[c, b] = tile
-        for turn in range(WARM):
-            nc.tensor.matmul_mx(
-                out=turned[:, W:],
-                lhsT=v_win[:, 0:P].bitcast(FP8X4),
-                lhsT_scale=late[:, 0:P],
-                rhs=v_win[:, 0:W].bitcast(FP8X4),
-                rhs_scale=late[:, 0:W],
-                start=True,
-                stop=True,
-            )
         move_rows(late)
         h_q = {}
         h_sc = [keep.tile([P, 2 * W], U8, name="h_sc%d" % c, align_bytes=64) for c in range(CHUNKS)]

from contextlib import ExitStack

import concourse.mybir as mybir
from concourse.masks import make_identity

K, T, S, T2, S2, N = 512, 2048, 1024, 4096, 1024, 512
FLOPS = 2 * (K * S * S2 + S * N * S2 + K * N * S2)

F32 = mybir.dt.float32
BF16 = mybir.dt.bfloat16
I32 = mybir.dt.int32
U32 = mybir.dt.uint32
U16 = mybir.dt.uint16
U8 = mybir.dt.uint8
FP8X4 = mybir.dt.float8_e4m3fn_x4
FP4X4 = mybir.dt.float4_e2m1fn_x4
ACT = mybir.ActivationFunctionType
ALU = mybir.AluOpType

P = 128
PACK = 4
PASS = P * PACK
BANK = 512
QUAD = 32
ROWS = 16
LOW = P - ROWS
RUN = 4
SCALE_ROWS = ROWS * QUAD // P
W = 256
CHUNKS = S2 // W
HALF = W // 2
COEF = 4
SHARE = 104
SKIP = 2
LAST_SHARE = 72
LAP = 64
Y_ON_SCALAR = 192


def tile_list_band_sine_field_kernel(
    tc, tab_words, tab_scales, tab2_words, tab2_scales, offs, offs2, phase, amp, wm, w4_words, w4_scales, bias,
    out_0, out_1, out_2,
):
    nc = tc.nc
    with ExitStack() as ctx:
        lists = ctx.enter_context(tc.tile_pool(name="lists", bufs=1))
        keep = ctx.enter_context(tc.tile_pool(name="keep", bufs=1))
        laid = ctx.enter_context(tc.tile_pool(name="laid", bufs=1))
        held = ctx.enter_context(tc.tile_pool(name="held", bufs=1))
        psum = ctx.enter_context(tc.psum_pool(name="psum", bufs=1))

        idx = lists.tile([P, S // 16], U16, name="idx")
        idx2 = lists.tile([P, S2 // 16], U16, name="idx2")
        s_win = keep.tile([P, T], U8, name="s_win", align_bytes=64)
        s2_win = keep.tile([P, T2], U8, name="s2_win", align_bytes=64)
        s4_raw = keep.tile([P, N], U8, name="s4_raw", align_bytes=64)
        for win in (s_win, s2_win, s4_raw):
            nc.vector.memset(win[0:LOW, :].bitcast(I32), 0)

        v_win = keep.tile([P, T], I32, name="v_win", align_bytes=64)
        v2_win = keep.tile([P, T2], I32, name="v2_win", align_bytes=64)
        coef_rows = keep.tile([COEF, PASS], F32, name="coef_rows")
        ident = keep.tile([P, P], F32, name="ident")
        make_identity(nc, ident[:])
        bi = keep.tile([P, PACK], F32, name="bi")
        border = 4 * PASS
        w4_raw = laid.tile([P, N // 2], I32, name="w4_raw", offset=border - N, align_bytes=64)
        nc.sync.dma_start(idx[:], offs)
        nc.sync.dma_start(s_win[LOW:P, :].bitcast(I32), tab_scales[0].bitcast(I32))
        nc.sync.dma_start(idx2[:], offs2)
        nc.sync.dma_start(s2_win[LOW:P, :].bitcast(I32), tab2_scales[0].bitcast(I32))
        nc.sync.dma_start(s4_raw[LOW:P, :].bitcast(I32), w4_scales[0].bitcast(I32))
        nc.sync.dma_start(v_win[:], tab_words[0].rearrange("p c t -> p (c t)").bitcast(I32))
        nc.sync.dma_start(coef_rows[0:2, :], phase.rearrange("(b e) -> b e", b=2))
        nc.sync.dma_start(coef_rows[2:COEF, :], amp.rearrange("(b e) -> b e", b=2))
        nc.sync.dma_start(bi[:], bias.rearrange("(p t) -> p t", t=PACK))
        nc.sync.dma_start(v2_win[:], tab2_words[0].rearrange("p c t -> p (c t)").bitcast(I32))
        nc.sync.dma_start(w4_raw[:], w4_words[0].bitcast(I32))

        s_picked = keep.tile([P, S], U8, name="s_picked", align_bytes=64)
        s2_first = keep.tile([P, BANK], U8, name="s2_first", tag="s2_first", align_bytes=64)
        s2_second = keep.tile([P, BANK], U8, name="s2_second", tag="s2_second", align_bytes=64)
        early = keep.tile([P, S + BANK], U8, name="early", align_bytes=64)
        late = keep.tile([P, BANK + N], U8, name="late", align_bytes=64)

        def move_rows(plane):
            for quad in range(P // QUAD):
                nc.sync.dma_start(
                    plane[QUAD * quad : QUAD * quad + SCALE_ROWS, :].bitcast(I32),
                    plane[LOW + SCALE_ROWS * quad : LOW + SCALE_ROWS * (quad + 1), :].bitcast(I32),
                )

        wm_rows = wm.rearrange("(b a u r) n -> b u a r n", b=2, u=PACK, r=RUN)

        def load_wm(b, raw):
            for u in range(PACK):
                nc.sync.dma_start(raw[:, u, :], wm_rows[b, u])
            return raw

        nc.vector.tensor_copy(s_picked[:], s_win[:].indirect(idx[:]))
        nc.vector.tensor_copy(s2_first[:], s2_win[:].indirect(idx2[:, 0 : BANK // 16]))
        nc.vector.tensor_copy(
            early[:, 0:S].bitcast(I32).rearrange("p (b t a) -> p b t a", b=2, t=PACK),
            s_picked[:].bitcast(I32).rearrange("p (b a t) -> p b t a", b=2, t=PACK),
        )
        nc.vector.tensor_copy(s2_second[:], s2_win[:].indirect(idx2[:, BANK // 16 :]))
        nc.vector.tensor_copy(early[:, S:].bitcast(I32), s2_first[:].bitcast(I32))
        move_rows(early)
        nc.vector.tensor_copy(
            late[:, BANK:].rearrange("p (t m) -> p t m", t=PACK), s4_raw[:].rearrange("p (m t) -> p t m", t=PACK)
        )
        wm_raw = [load_wm(0, keep.tile([P, PACK, N], F32, name="wm_raw0", tag="s2_first", align_bytes=64))]
        nc.vector.tensor_copy(late[:, 0:BANK].bitcast(I32), s2_second[:].bitcast(I32))
        wm_raw.append(load_wm(1, keep.tile([P, PACK, N], F32, name="wm_raw1", tag="s2_second", align_bytes=64)))
        v2_sc = [early[:, S:], late[:, 0:BANK]]
        v_sc = early[:, 0:S]
        w4_sc = late[:, BANK:]

        sorted_rows = keep.tile([P, PASS], F32, name="sorted_rows")
        nc.scalar.activation(
            out=sorted_rows[:].rearrange("p (t n) -> p t n", t=PACK),
            in_=ident[:].unsqueeze(1).to_broadcast([P, PACK, P]),
            func=ACT.Sin,
        )
        nc.scalar.copy(
            sorted_rows[0:COEF, :].rearrange("p (t a r) -> p t a r", t=PACK, r=RUN),
            coef_rows[:].rearrange("p (a t r) -> p t a r", t=PACK, r=RUN),
        )
        turned = psum.tile([P, BANK], F32, name="turned")
        for t in range(PACK):
            nc.tensor.transpose(turned[:, COEF * t : COEF * t + P], sorted_rows[:, P * t : P * (t + 1)], ident[:])
        by_row = turned[:, 0 : COEF * PACK].rearrange("p (t n) -> p n t", t=PACK)
        coef = keep.tile([P, COEF, PACK], F32, name="coef")
        nc.scalar.copy(coef[:, 0:3, :], by_row[:, 0:3, :])

        v2_q = [
            keep.tile([P, BANK], U32, name="v2_q0", align_bytes=64),
            laid.tile([P, BANK], U32, name="v2_q1", offset=border, align_bytes=64),
        ]
        codes = 4 * 2 * W
        meet = {1: codes, 2: 3 * codes + 64, 3: 6 * codes}
        own_phase = {}
        for n, (c, b) in enumerate(((1, 1), (2, 1), (3, 1))):
            tile = held.tile([P, 32], F32, name="phase%d%d" % (c, b), offset=meet[n + 1] - 64, align_bytes=64)
            nc.scalar.copy(tile[:, 0:PACK], by_row[:, b, :])
            own_phase[c, b] = tile
        move_rows(late)
        h_q = {}
        h_sc = [keep.tile([P, 2 * W], U8, name="h_sc%d" % c, align_bytes=64) for c in range(CHUNKS)]
        wm_sc = [keep.tile([P, N], U8, name="wm_sc%d" % b, align_bytes=64) for b in range(2)]
        y_sc = keep.tile([P, S2], U8, name="y_sc", align_bytes=64)

        span = PACK * 2 * W
        part = PACK * W
        first = keep.tile([P, span], BF16, name="h_bf0", align_bytes=64)
        shared = keep.tile([P, span + part], BF16, name="shared", align_bytes=64)
        h_bf = {0: first[:], (0, 0): first[:, 0:part], (0, 1): first[:, part:]}
        for b in range(2):
            h_bf[1, b] = keep.tile([P, part], BF16, name="h_bf1%d" % b, align_bytes=64)[:]
            h_bf[2, b] = shared[:, part * b : part * (b + 1)]
        wm_bf = [keep.tile([P, PACK * N], BF16, name="wm_bf0", align_bytes=64)[:], shared[:, 0:span]]
        y_bf = {c: keep.tile([P, PACK * W], BF16, name="y_bf%d" % c, align_bytes=64)[:] for c in range(CHUNKS)}
        h_bf[3, 0] = shared[:, span - LAP : span + part - LAP]

        def cols(pair, j0, w):
            return pair[j0 // BANK][:, j0 % BANK : j0 % BANK + w]

        def gather_v(b, dealt):
            run = PASS // 16
            nc.vector.tensor_copy(
                dealt[:].rearrange("p (t a r) -> p a t r", t=PACK, r=RUN),
                v_win[:].bitcast(U32).indirect(idx[:, run * b : run * (b + 1)]),
            )
            return dealt

        def gather_v2(j0, w):
            nc.vector.tensor_copy(
                cols(v2_q, j0, w), v2_win[:].bitcast(U32).indirect(idx2[:, j0 // 16 : (j0 + w) // 16])
            )

        def gpsimd_round(out, in_):
            nc.gpsimd.tensor_scalar(out, in_, 1.0, 0.0, ALU.mult, ALU.add)

        def round_wm(b, t0, t1, walk, copy):
            copy(
                wm_bf[b][:, PASS * t0 : PASS * t1].rearrange("p (t m u) -> " + walk, t=t1 - t0, u=PACK),
                wm_raw[b][:].rearrange("p u (m t) -> p u m t", t=PACK)[:, :, :, t0:t1].rearrange("p u m t -> " + walk),
            )

        def quantise_wm(b, tile):
            nc.vector.quantize_mx(out=tile[:].bitcast(FP8X4), scales=wm_sc[b][:], in_=wm_bf[b])
            return tile

        def psum_slices(banks, w):
            per = PACK // len(banks)
            tiles = [psum.tile([P, BANK], F32, name="bank%d" % k, tag="bank%d" % k) for k in banks]
            return [tiles[t // per][:, (t % per) * w : (t % per + 1) * w] for t in range(PACK)]

        def woven(tile):
            return tile.rearrange("p (c e t) -> p c t e", e=2, t=PACK)

        def by_pairs(tile):
            return tile.rearrange("p t (c e) -> p c t e", e=2)

        def sines(c, b, banks, room=None):
            if room is None:
                room = keep.tile([P, PACK, W], F32, name="sn%d%d" % (c, b), align_bytes=64)[:]
            sn[c, b] = room
            acc = psum_slices(banks, W)
            for t in range(PACK):
                nc.tensor.matmul_mx(
                    out=acc[t],
                    lhsT=v_q[b][:, P * t : P * (t + 1)].bitcast(FP8X4),
                    lhsT_scale=v_sc[:, PASS * b + P * t : PASS * b + P * (t + 1)],
                    rhs=cols(v2_q, W * c, W).bitcast(FP8X4),
                    rhs_scale=cols(v2_sc, W * c, W),
                    start=True,
                    stop=True,
                )
            phase_t = own_phase.get((c, b), coef[:, b])
            for t in range(PACK):
                nc.scalar.activation(out=sn[c, b][:, t, :], in_=acc[t], func=ACT.Sin, bias=phase_t[:, t : t + 1])

        def h_cols(c, w0, w1):
            if w1 - w0 == 2 * W:
                return h_bf[c]
            return h_bf[c, w0 // W][:, PACK * (w0 % W) : PACK * (w0 % W + w1 - w0)]

        def vector_product(c, b, c0, c1=W):
            amp_t = by_row[:, 2 + b, :].unsqueeze(1).unsqueeze(3).to_broadcast([P, (c1 - c0) // 2, PACK, 2])
            out = woven(h_cols(c, W * b + c0, W * b + c1))
            nc.vector.tensor_tensor(out, by_pairs(sn[c, b][:, :, c0:c1]), amp_t, ALU.mult)

        def gpsimd_product(c, share):
            nc.gpsimd.tensor_tensor(
                h_cols(c, 0, share).rearrange("p (j t) -> p j t", t=PACK),
                sn[c, 0][:, :, 0:share].rearrange("p t j -> p j t"),
                coef[:, 2:3, :].to_broadcast([P, share, PACK]),
                ALU.mult,
            )

        def quantise_h(c, w0, w1):
            nc.vector.quantize_mx(out=h_q[c][:, w0:w1].bitcast(FP8X4), scales=h_sc[c][:, w0:w1], in_=h_cols(c, w0, w1))

        def mix(j0, w, banks, order):
            acc = psum_slices(banks, w)
            per = PACK // len(banks)
            c = j0 // W
            skip = (w4_q[:].bitcast(U16), FP4X4, w4_sc, cols(v2_q, j0, w), cols(v2_sc, j0, w))
            terms = []
            for b in range(2):
                w0 = W * b + j0 % W
                terms.append((wm_q[b][:], FP8X4, wm_sc[b][:], h_q[c][:, w0 : w0 + w], h_sc[c][:, w0 : w0 + w]))
            terms.append(skip)
            for n, term in enumerate(order):
                words, fmt, scales, moving, moving_scales = terms[term]
                for t in range(PACK):
                    nc.tensor.matmul_mx(
                        out=acc[t],
                        lhsT=words[:, P * t : P * (t + 1)].bitcast(fmt),
                        lhsT_scale=scales[:, P * t : P * (t + 1)],
                        rhs=moving.bitcast(FP8X4),
                        rhs_scale=moving_scales,
                        start=(n == 0 and t % per == 0),
                        stop=(n == len(terms) - 1 and t % per == per - 1),
                    )
            return acc

        def add_bias(acc, j0, w):
            per = BANK // w
            rows = keep.tile([P, PACK, w], F32, name="y%d" % j0, align_bytes=64)
            out_rows = out_0.rearrange("(p t) j -> p t j", t=PACK)
            for t in range(PACK):
                nc.scalar.activation(out=rows[:, t, :], in_=acc[t], func=ACT.Identity, bias=bi[:, t : t + 1])
                if t % per == per - 1:
                    nc.sync.dma_start(out_rows[:, t + 1 - per : t + 1, j0 : j0 + w], rows[:, t + 1 - per : t + 1, :])
            return rows

        def round_y(rows, out, c0, c1, copy):
            copy(woven(out[:, PACK * c0 : PACK * c1]), by_pairs(rows[:, :, c0:c1]))

        def quantise_y(j0, w):
            nc.vector.quantize_mx(
                out=y_q[:, j0 : j0 + w].bitcast(FP8X4),
                scales=y_sc[:, j0 : j0 + w],
                in_=y_bf[j0 // W][:, PACK * (j0 % W) : PACK * (j0 % W + w)],
            )

        def store_codes(j0, w):
            nc.sync.dma_start(
                out_1[0].rearrange("p j t -> p (j t)").bitcast(I32)[:, j0 : j0 + w], y_q[:, j0 : j0 + w].bitcast(I32)
            )

        v_q = [gather_v(0, keep.tile([P, PASS], U32, name="v_q0", align_bytes=64))]
        gather_v2(0, W)
        gather_v2(W, W)
        w4_q = keep.tile([P, 2 * N], U8, name="w4_q", align_bytes=64)
        nc.scalar.copy(
            w4_q[:].bitcast(U16).rearrange("p (t m) -> p t m", t=PACK),
            w4_raw[:].bitcast(U16).rearrange("p (m t) -> p t m", t=PACK),
        )
        v_q.append(gather_v(1, laid.tile([P, PASS], U32, name="v_q1", offset=0, align_bytes=64)))
        gather_v2(BANK, BANK)

        sn = {}
        sines(0, 0, [0, 1, 2, 3])
        sines(1, 0, [4, 5])
        sines(0, 1, [0, 1])
        sines(1, 1, [2, 3])
        round_wm(0, 0, PACK, "p m t u", gpsimd_round)
        round_wm(1, 0, 2, "p m t u", gpsimd_round)
        sines(2, 0, [0, 1])
        sines(2, 1, [2, 3])
        round_wm(1, 2, PACK, "p m u t", nc.scalar.copy)
        sines(3, 0, [0, 1], keep.tile([P, PACK, W], F32, name="sn30", tag="s2_second", align_bytes=64)[:])
        sines(3, 1, [5, 2])

        for b in range(2):
            vector_product(0, b, 0)
            vector_product(1, b, 0)
        pair = held.tile([P, 4 * W], U32, name="h_q01", offset=meet[1], align_bytes=64)
        h_q[0] = pair[:, 0 : 2 * W]
        h_q[1] = pair[:, 2 * W :]
        quantise_h(0, 0, 2 * W)
        wm_q = [quantise_wm(0, held.tile([P, N], U32, name="wm_q0", offset=meet[1] - codes, align_bytes=64))]
        quantise_h(1, W, 2 * W)
        wm_q.append(quantise_wm(1, keep.tile([P, N], U32, name="wm_q1", align_bytes=64)))
        y = [add_bias(mix(0, W, [6, 4], (SKIP, 0, 1)), 0, W)]
        h_bf[3, 1] = keep.tile([P, part], BF16, name="h_bf31", align_bytes=64)[:]
        gpsimd_product(2, SHARE)
        vector_product(2, 0, SHARE)
        vector_product(2, 1, 0)
        quantise_h(1, 0, W)
        acc1 = mix(W, W, [0, 1], (1, SKIP, 0))
        h_q[2] = held.tile([P, 2 * W], U32, name="h_q2", offset=3 * codes, align_bytes=64)
        quantise_h(2, 0, W)
        quantise_h(2, W, 2 * W)
        y.append(add_bias(acc1, W, W))
        round_y(y[0], y_bf[0], 0, Y_ON_SCALAR, nc.scalar.copy)
        y.append(add_bias(mix(2 * W, W, [3, 5], (SKIP, 0, 1)), 2 * W, W))

        gpsimd_product(3, LAST_SHARE)
        vector_product(3, 0, LAST_SHARE)
        vector_product(3, 1, 0, HALF)
        h_q[3] = held.tile([P, 2 * W], U32, name="h_q3", offset=meet[3], align_bytes=64)
        y_q = held.tile([P, S2], U32, name="y_q", offset=meet[3] - 4 * S2, align_bytes=64)
        quantise_h(3, 0, W)
        quantise_h(3, W, W + HALF)
        vector_product(3, 1, HALF)
        round_y(y[0], y_bf[0], Y_ON_SCALAR, W, nc.vector.tensor_copy)
        quantise_h(3, W + HALF, 2 * W)

        last = [add_bias(mix(3 * W, HALF, [4], (SKIP, 0, 1)), 3 * W, HALF), add_bias(mix(3 * W + HALF, HALF, [6, 0, 1, 2], (SKIP, 0, 1)), 3 * W + HALF, HALF)]
        round_y(y[1], y_bf[1], 0, W, nc.vector.tensor_copy)
        quantise_y(0, W)
        round_y(y[2], y_bf[2], 0, W, nc.vector.tensor_copy)
        quantise_y(W, W)
        store_codes(0, 2 * W)
        round_y(last[0], y_bf[3][:, 0 : PACK * HALF], 0, HALF, nc.vector.tensor_copy)
        quantise_y(2 * W, W)
        round_y(last[1], y_bf[3][:, PACK * HALF :], 0, HALF, nc.scalar.copy)
        quantise_y(3 * W, HALF)
        quantise_y(3 * W + HALF, HALF)
        store_codes(2 * W, 2 * W)
        for quad in range(P // QUAD):
            queue = nc.scalar if quad % 2 else nc.sync
            queue.dma_start(
                out_2[0, SCALE_ROWS * quad : SCALE_ROWS * (quad + 1), :].bitcast(I32),
                y_sc[QUAD * quad : QUAD * quad + SCALE_ROWS, :].bitcast(I32),
            )
